import numpy as np, ml_dtypes
CORES = [25,29,65,69,153,157,193,197]
N = 8
import mx_ref
BF = ml_dtypes.bfloat16
def cols(t, e):
    v = np.concatenate([t.reshape(128, -1, 4), np.zeros((128, 1, 4), BF)], axis=1)
    return np.ascontiguousarray(v[:, e]).reshape(128, -1)
def cut(t, i, w=512):
    return t[:, w * i:w * i + w]
def pick(q, e):
    c = np.concatenate([q[0].reshape(128, -1, 4), np.zeros((128, 1, 4), np.uint8)], axis=1); s = np.concatenate([q[1], np.ones((16, 1), np.uint8)], axis=1)
    return (np.ascontiguousarray(c[:, e].reshape(128, -1)), np.ascontiguousarray(s[:, e]))
def join(*qs):
    return (np.concatenate([q[0] for q in qs], axis=1), np.concatenate([q[1] for q in qs], axis=1))
def put(q, e, v):
    c, s = q[0].reshape(128, -1, 4).copy(), q[1].copy(); c[:, e] = v[0].reshape(128, -1, 4); s[:, e] = v[1]
    return (c.reshape(128, -1), s)
def pk(c, s):
    return (np.ascontiguousarray(c), mx_ref.live(s))
def emit(q):
    return q[0], q[1]
def decode(q):
    o = []
    for b in range(4):
        e = np.zeros((128, 128, 4), np.float32); e[np.arange(128), np.arange(128), b] = 1
        o.append(mx_ref.matmul(mx_ref.quantize(e.reshape(128, 512).astype(BF)), q))
    return np.stack(o, axis=2).reshape(128, -1)
def f(rng, *shape):
    return mx_ref.flush((rng.standard_normal(shape, dtype=np.float32) * np.exp2(rng.integers(-2, 3, shape[:-1] + (1,)))).astype(BF))
def wide(rng, *shape, cols=0):
    v = rng.standard_normal(shape, dtype=np.float32) * np.exp2(rng.integers(-12, 13, shape)).astype(np.float32)
    if cols: v *= np.repeat(np.exp2(rng.integers(-cols, cols + 1, shape[:-2] + (1, shape[-1] // 4))) * (rng.random(shape[:-2] + (1, shape[-1] // 4)) > 0.0625), 4, axis=-1).astype(np.float32)
    return mx_ref.flush(v.astype(BF))
M, A, E, R, O = 128, 16, 32, 2, 1
def big(v):
    v = v.astype(np.float32)
    v[np.abs(v) < np.float32(2.0 ** -14)] = 0
    return v.astype(BF)
def plain(rng):
    return {"me": big(f(rng, N, 128, 4 * M)), "x": big(f(rng, N, 128, 4 * A)), "w": f(rng, N, 128, 512 * O)}
def signs(rng, n):
    h = np.ones((1, 1))
    while len(h) < n: h = np.block([[h, h], [h, -h]])
    return h[rng.permutation(n)[:128]][:, rng.permutation(n)] * rng.choice([-1.0, 1.0], n)
def tiles(v):
    return v.reshape(-1, 128, 4).transpose(1, 0, 2).reshape(128, -1)
def store(rng, m, q):
    return {"me": big(np.stack([tiles(v) for v in m.reshape(N, M, 512)])), "x": big(np.stack([tiles(v) for v in q.reshape(N, A, 512)])), "w": f(rng, N, 128, 512 * O)}
def low(rng):
    return rng.standard_normal((N * M, 512), dtype=np.float32) * np.float32(2.0 ** -6)
def rough(rng, v):
    return v * (1 + 0.0625 * rng.uniform(-1, 1, v.shape)) * np.exp2(rng.integers(0, 2, (len(v), 1)))
def places(rng, s):
    at = np.zeros(len(s), int)
    for r in range(N):
        j = np.flatnonzero(s == r)
        at[j] = r * M + rng.permutation(M)[:len(j)]
    return at
def spare(rng, r, at):
    return rng.permutation(np.setdiff1d(np.arange(r * M, r * M + M), at))
def planted(rng, at, o):
    k, i = np.unique(at, return_inverse=True)
    v, m = signs(rng, 512), low(rng)
    m[k] = rough(rng, v[:len(k)])
    m[at[o[0]]] *= 8
    q = rough(rng, v[i])
    q[o[0]] = 4 * v[i[o[0]]] + 8 * v[i[o[-1]]]
    q[o[2]] = q[o[1]]
    return store(rng, m, q)
def setup_inputs(rng):
    return plain(rng)
def setup_inputs_hot(rng):
    h = int(rng.integers(0, N))
    g = (h + int(rng.integers(1, N))) % N
    at = (h + rng.integers(1, N, 128)) % N * M + rng.integers(0, M, 128)
    o = np.flatnonzero(np.arange(128) // A != h)
    p, u = h * M + rng.permutation(M)[:7], g * M + rng.permutation(M)[:6]
    at[o] = u[rng.integers(0, 6, len(o))]
    k = np.concatenate([o[:A], rng.permutation(o[A:-1])[:len(o) // 2 - A - 1]])
    at[k] = p[rng.integers(0, 6, len(k))]
    at[o[2]] = at[o[1]]
    at[o[-1]] = p[6]
    return planted(rng, at, o)
def setup_inputs_ties(rng):
    d, b = plain(rng), int(rng.integers(2, N))
    g = np.full((N, 4), 4.0)
    g[b] = 1
    g[(b + int(rng.integers(1, N))) % N] = 16
    p = big(np.abs(f(rng, 128, 16 * N).astype(np.float32)) * np.repeat(g.reshape(-1), 4))
    k = f(rng, 128, 120).astype(np.float32)
    k[:, :96] = np.abs(k[:, :96])
    k[:, :48] = -k[:, :48]
    k[:, :16] = k[:, :16] * np.float32(2.0 ** 24)
    k = big(k)
    e = rng.permutation(np.concatenate([np.arange(30), rng.integers(12, 24, 58), rng.integers(0, 30, 40)]))
    m = []
    for r in range(N):
        own = np.concatenate([4 * r + np.arange(4), 4 * ((r + 1) % N) + np.arange(4)])
        m.append(cols(p, rng.permutation(np.concatenate([own, own, own[rng.integers(0, 8, M - 16)]]))))
    d["me"] = np.stack(m)
    d["x"] = np.stack([cols(k, e[r * A:r * A + A]) for r in range(N)])
    return d
def setup_inputs_second(rng):
    a, b = signs(rng, 256), signs(rng, 256)
    s = rng.permutation(np.arange(128) % N)
    p = places(rng, np.concatenate([s, (s + rng.integers(1, N, 128)) % N]))
    e = rng.permutation(512)
    e, g = e[:256], e[256:]
    m, q = low(rng), rng.uniform(-1, 1, (128, 512)) * 2.0 ** -6
    q[:, e] = a
    m[p[:128, None], e] = a
    m[p[:128, None], g] = 4 * b
    m[p[128:, None], g] = 16 * b
    return store(rng, m, q)
def setup_inputs_idle(rng):
    o = rng.permutation(N)
    s = o[rng.integers(2, N, 128)]
    s[rng.permutation(128)[:E]] = o[1]
    at = places(rng, s)
    j = int(np.argmin(s))
    z = np.sort(spare(rng, int(s[j]), at)[:2])
    at[j] = z[0]
    far = spare(rng, int(s.max()), at)[0]
    v, m = signs(rng, 512), low(rng)
    v = v * v[j]
    m[at] = rough(rng, v)
    m = m - np.float32(0.25)
    m[[z[0], z[1], far]] = 0
    q = rough(rng, v)
    q[j] = 2 * q[j]
    d = store(rng, m * np.float32(2.0 ** 27), q * 2.0 ** 27)
    c = 4 * int(z[0] % M)
    d["me"][int(s[j]), :, c:c + 4] = BF(-0.0)
    return d
def setup_inputs_spread(rng):
    return {**plain(rng), "me": big(wide(rng, N, 128, 4 * M, cols=3)), "x": big(wide(rng, N, 128, 4 * A, cols=3))}
def check_inputs(d):
    b = []
    for k, least in (("me", 2.0 ** -14), ("x", 2.0 ** -14), ("w", 2.0 ** -30)):
        v = np.abs(d[k].astype(np.float32))
        if not (np.isfinite(v).all() and ((v == 0) | (v >= least) & (v <= 2.0 ** 30)).all()): b.append("a value of " + k)
    return b
def reference(me, x, w):
    mem = [mx_ref.quantize(np.ascontiguousarray(me[r])) for r in range(N)]
    q = join(*[mx_ref.quantize(np.ascontiguousarray(x[r])) for r in range(N)])
    wi = np.zeros((N, R, 128), np.float32)
    for t in range(R):
        s = np.concatenate([mx_ref.matmul(q, mem[r]) for r in range(N)], axis=1) + np.float32(0)
        win = np.argmax(s, axis=1)
        answered = np.zeros(128, bool)
        for r in range(N): answered[np.flatnonzero(win // M == r)[:E]] = True
        wi[:, t] = np.where(answered, win, -1 - win)
        half = decode(pick(join(*mem), win)) * np.float32(0.5)
        new = mx_ref.quantize((half + decode(q) * np.float32(0.5)).astype(BF))
        a = np.flatnonzero(answered)
        q = put(q, a, pick(new, a))
        for r in range(N):
            j = a[win[a] // M == r]
            if j.size:
                c, i = np.unique(win[j] - r * M, return_index=True)
                mem[r] = put(mem[r], c, pick(new, j[i]))
    oc, osc, y = np.zeros((N, 128, 4 * M), np.uint8), np.zeros((N, 16, M), np.uint8), np.zeros((N, 128, 128 * O), np.float32)
    for r in range(N):
        oc[r], osc[r] = emit(mem[r])
        for o in range(O): y[r, :, 128 * o:128 * o + 128] = mx_ref.matmul(mx_ref.quantize(np.ascontiguousarray(cut(w[r], o))), q)
    return {"oc": oc, "osc": osc, "wi": wi, "y": y}

@@ -1,0 +1,486 @@
+from concourse.bass import DstId, RemoteDMATransfer
+from concourse.mybir import dt, AluOpType, AxisListType, ActivationFunctionType
+
+F8 = "float8_e4m3fn_x4"
+SCRATCH = {
+    "ps": ("psum", [128, 4096], "float32"),
+    "xt": ("sbuf", [128, 512], "bfloat16"), "mt": ("sbuf", [128, 512], "bfloat16"), "wt": ("sbuf", [128, 512], "bfloat16"),
+    "xq": ("sbuf", [128, 128], F8), "xqs": ("sbuf", [128, 128], "uint8"),
+    "wq": ("sbuf", [128, 128], F8), "wqs": ("sbuf", [128, 128], "uint8"),
+    "rx": ("sbuf", [128, 32], F8), "rxs": ("sbuf", [128, 32], "uint8"),
+    "rm": ("sbuf", [128, 128], F8), "rms": ("sbuf", [128, 128], "uint8"),
+    "ld0": ("sbuf", [128, 384], F8), "ld0s": ("sbuf", [128, 384], "uint8"),
+    "ld1": ("sbuf", [128, 384], F8), "ld1s": ("sbuf", [128, 384], "uint8"),
+    "qf": ("sbuf", [128, 128], F8), "qfs": ("sbuf", [128, 128], "uint8"),
+    "mc0": ("sbuf", [128, 416], F8), "mc0s": ("sbuf", [128, 416], "uint8"),
+    "mc1": ("sbuf", [128, 416], F8), "mc1s": ("sbuf", [128, 416], "uint8"),
+    "fm": ("sbuf", [128, 128], F8), "fms": ("sbuf", [128, 128], "uint8"),
+    "mp0": ("sbuf", [128, 128], F8), "mp0s": ("sbuf", [128, 128], "uint8"),
+    "mp1": ("sbuf", [128, 128], F8), "mp1s": ("sbuf", [128, 128], "uint8"),
+    "wc": ("sbuf", [128, 640], F8), "wcs": ("sbuf", [128, 640], "uint8"),
+    "ec": ("sbuf", [128, 512], F8), "ecs": ("sbuf", [128, 512], "uint8"),
+    "hac": ("sbuf", [128, 136], F8), "has": ("sbuf", [128, 136], "uint8"),
+    "hcc": ("sbuf", [128, 136], F8), "hcs": ("sbuf", [128, 136], "uint8"),
+    "h2c": ("sbuf", [128, 136], F8), "h2s": ("sbuf", [128, 136], "uint8"),
+    "h3c": ("sbuf", [128, 264], F8), "h3s": ("sbuf", [128, 264], "uint8"),
+    "ha": ("sbuf", [128, 520], "bfloat16"), "hc": ("sbuf", [128, 520], "bfloat16"),
+    "h2": ("sbuf", [128, 520], "bfloat16"), "h3": ("sbuf", [128, 1032], "bfloat16"),
+    "ht": ("sbuf", [128, 520], "bfloat16"),
+    "wtile": ("sbuf", [128, 2560], "bfloat16"), "et": ("sbuf", [128, 2048], "bfloat16"),
+    "zz": ("sbuf", [128, 512], "bfloat16"),
+    "wina": ("sbuf", [128, 512], "bfloat16"), "d1": ("sbuf", [128, 512], "bfloat16"), "d2": ("sbuf", [128, 512], "bfloat16"),
+    "winc": ("sbuf", [128, 256], "bfloat16"),
+    "tc1": ("sbuf", [128, 256], "bfloat16"), "tc2": ("sbuf", [128, 256], "bfloat16"), "tc3": ("sbuf", [128, 256], "bfloat16"),
+    "tri": ("sbuf", [128, 128], "bfloat16"), "m1": ("sbuf", [128, 256], "bfloat16"), "hold": ("sbuf", [128, 256], "bfloat16"),
+    "jf": ("sbuf", [128, 128], "float32"), "jm": ("sbuf", [128, 256], "bfloat16"), "b8": ("sbuf", [128, 8], "float32"),
+    "pint": ("sbuf", [128, 4], "int32"), "pf": ("sbuf", [128, 4], "float32"), "rmk": ("sbuf", [128, 8], "float32"),
+    "dg": ("sbuf", [128, 8], "float32"), "kb": ("sbuf", [128, 8], "float32"), "cc": ("sbuf", [128, 8], "float32"),
+    "vd": ("sbuf", [128, 8], "float32"), "wd": ("sbuf", [128, 8], "float32"), "ox": ("sbuf", [128, 2], "uint16"),
+    "lm0": ("sbuf", [128, 16], "float32"), "lm1": ("sbuf", [128, 16], "float32"), "nl": ("sbuf", [128, 16], "float32"),
+    "cm": ("sbuf", [128, 256], "float32"), "jk": ("sbuf", [128, 256], "bfloat16"),
+    "aa": ("sbuf", [128, 2], "float32"), "vv": ("sbuf", [128, 2], "float32"), "an": ("sbuf", [128, 2], "float32"),
+    "oa": ("sbuf", [128, 8], "uint16"), "oaw": ("sbuf", [128, 8], "uint16"),
+    "w1": ("sbuf", [128, 256], "float32"), "w2": ("sbuf", [128, 256], "float32"),
+    "fra": ("sbuf", [128, 128], "bfloat16"),
+    "mx": ("sbuf", [128, 1], "float32"), "eq": ("sbuf", [128, 8], "float32"), "sc": ("sbuf", [128, 8], "float32"),
+    "oc8": ("sbuf", [128, 8], "uint16"), "clo": ("sbuf", [128, 128], "bfloat16"), "chi": ("sbuf", [128, 128], "bfloat16"),
+    "acc": ("sbuf", [128, 4], "float32"), "acv": ("sbuf", [128, 1], "float32"), "le": ("sbuf", [128, 128], "bfloat16"),
+    "os": ("sbuf", [128, 4], "uint16"), "pv": ("sbuf", [128, 8], "float32"),
+    "same": ("sbuf", [128, 128], "bfloat16"), "sc2": ("sbuf", [128, 128], "bfloat16"),
+    "kk": ("sbuf", [128, 4], "float32"), "bi": ("sbuf", [128, 2], "int32"),
+    "o2": ("sbuf", [128, 8], "uint16"), "oq": ("sbuf", [128, 8], "uint16"),
+    "tg": ("sbuf", [128, 128], "bfloat16"), "ep": ("sbuf", [128, 256], "bfloat16"), "co": ("sbuf", [128, 256], "bfloat16"),
+    "jc": ("sbuf", [128, 8], "float32"), "ta": ("sbuf", [128, 2], "float32"),
+    "o3": ("sbuf", [128, 16], "uint16"), "om": ("sbuf", [128, 16], "uint16"),
+    "wv": ("sbuf", [128, 16], "float32"), "wo": ("sbuf", [128, 2], "float32"), "ysb": ("sbuf", [128, 128], "float32"),
+}
+SCRATCH["oslot"] = SCRATCH.pop("os")
+SEMAPHORES = ["V", "S", "P", "G", "ls", "xa", "ma", "mr", "ms", "m0", "m1", "nn", "c0", "c1",
+              "dx", "dm", "dw", "t0", "t1", "t2", "t3", "t4", "u0", "u1", "u2", "u3", "u4", "u5", "u6", "u7"]
+A = 16
+E = 32
+QO = 256
+
+
+def plan(T, topo):
+    cores = T.cores
+    n = len(cores)
+    near = [[q for q in range(n) if q == r or topo.may_write(cores[r], cores[q])] for r in range(n)]
+    far = [[q for q in range(n) if q not in near[r]] for r in range(n)]
+    chip = [[q for q in range(n) if cores[q] in topo.cores_of(cores[r])] for r in range(n)]
+    partner = [[q for q in far[r] if topo.host(cores[q]) == topo.host(cores[r]) and topo.die(cores[q]) == topo.die(cores[r])][0]
+               for r in range(n)]
+    port = [[c for c in topo.cores_of(cores[r]) if c not in cores and topo.die(c) == topo.die(cores[r])
+             and topo.may_write(c, cores[far[r][0]])] for r in range(n)]
+    xrel = [(port[chip[r][0]][0], port[chip[r][1]][0]) for r in range(n)]
+    mrel = [port[r][1] for r in range(n)]
+    return near, far, chip, partner, xrel, mrel
+
+
+def bits(engines):
+    return sum(1 << e for e in engines)
+
+
+def make_send(g, core, T, topo, count):
+    def send(sem, parts):
+        tr = []
+        for src, dst, eng in parts:
+            ids = []
+            for c, _ in dst:
+                rid, pid = topo.addr(c, core)
+                ids.append(DstId(rid=rid, pnc=pid))
+            tr.append(RemoteDMATransfer(dst_ids=ids, dma_engine_mask=bits(eng), remote_sem=T.sem[sem],
+                                        srcs=[src], dsts=[d for _, d in dst], alu_op=0))
+            count[0] += len(eng)
+        g.remote_dma_fused(tr, local_sem=T.sem.ls)
+    return send
+
+
+def relay(g, core, T, topo, pl):
+    near, far, chip, partner, xrel, mrel = pl
+    cores = T.cores
+    n = [0]
+    send = make_send(g, core, T, topo, n)
+    for r in range(len(cores)):
+        off = topo.engines(core, cores[far[r][0]])
+        on = [e for e in topo.engines(core, cores[r]) if e not in off] if core in topo.cores_of(cores[r]) else []
+        if chip[r][0] == r and core in xrel[r]:
+            g.wait_ge(T.sem.xa, len(on) * len(chip[r]))
+            a, b = QO + A * r, QO + A * r + A * len(chip[r])
+            if core == xrel[r][0]:
+                send("xa", [(T.rx[:].bitcast(dt.uint8), [(cores[q], T.ld0[:, a:b].bitcast(dt.uint8)) for q in far[r]], off)])
+            else:
+                send("xa", [(T.rxs[:], [(cores[q], T.ld0s[:, a:b]) for q in far[r]], off)])
+        if core == mrel[r]:
+            p = partner[r]
+            h = 128 if r > p else 0
+            g.wait_ge(T.sem.mr, len(on) + len(off))
+            send("ma", [(T.rm[:].bitcast(dt.uint8), [(cores[p], T.mc0[:, h:h + 128].bitcast(dt.uint8))], off)])
+            g.wait_ge(T.sem.ms, len(on) + len(off))
+            send("ma", [(T.rms[:], [(cores[p], T.mc0s[:, h:h + 128])], off)])
+    if n[0]:
+        g.wait_ge(T.sem.ls, n[0])
+
+
+def rank_program(g, core, T, topo):
+    pl = plan(T, topo)
+    near, far, chip, partner, xrel, mrel = pl
+    cores = T.cores
+    N = len(cores)
+    rank = T.rank_of(core)
+    if rank is None:
+        relay(g, core, T, topo, pl)
+        return
+    op, X, AF = AluOpType, AxisListType.X, ActivationFunctionType
+    V, S, P = g.vector, g.scalar, g.tensor
+    queue = {"V": g.vector, "S": g.scalar, "P": g.tensor, "G": g, "Y": g.sync}
+    cnt, known = {}, {q: {} for q in queue}
+    wr, rd = {}, {}
+    ls = [0]
+    fused = make_send(g, core, T, topo, ls)
+
+    def need(q, deps):
+        want = {}
+        for e in deps:
+            if known[q].get(e[0], 0) < e[1]:
+                want[e[0]] = max(want.get(e[0], (0, None))[0], e[1]), e
+        for s, (v, e) in want.items():
+            if known[q].get(s, 0) < v:
+                queue[q].wait_ge(T.sem[s], v)
+                known[q][s] = v
+        for e in deps:
+            for s, v in e[3].items():
+                if known[q].get(s, 0) < v:
+                    known[q][s] = v
+
+    def deps_of(q, r, w, acc):
+        d = []
+        for k in r:
+            d += [e for e in wr.get(k, [])]
+            if k[0] == "#":
+                d += [e for e in rd.get(k, []) if e[2] != q]
+        for k in w:
+            d += [e for e in wr.get(k, []) if not (acc and e[2] == q)]
+            d += [e for e in rd.get(k, []) if e[2] != q]
+        return d
+
+    def note(e, r, w):
+        for k in w:
+            wr[k], rd[k] = [e], []
+        for k in r:
+            rd.setdefault(k, []).append(e)
+
+    def do(q, r, w, call, acc=False):
+        r, w = r.split(), w.split()
+        need(q, deps_of(q, r, w, acc))
+        call().then_inc(T.sem[q], 1)
+        cnt[q] = cnt.get(q, 0) + 1
+        note((q, cnt[q], q, dict(known[q])), r, w)
+
+    def dma(q, sem, r, w, pairs):
+        r, w = r.split(), w.split()
+        need(q, deps_of(q, r, w, False))
+        for o, i in pairs:
+            queue[q].dma_start(o, i).then_inc(T.sem[sem], 16)
+            cnt[sem] = cnt.get(sem, 0) + 16
+        note((sem, cnt[sem], "dma", dict(known[q])), r, w)
+
+    def arrive(sem, n, w):
+        cnt[sem] = n
+        for k in w.split():
+            wr[k], rd[k] = [(sem, n, "far", {})], []
+
+    def send(sem, r, parts):
+        need("G", deps_of("G", r.split(), [], False))
+        fused(sem, parts)
+
+    def ts(q, r, w, out, in0, s1, s2, o0, o1=None):
+        if o1 is None:
+            do(q, r, w, lambda: V.tensor_scalar(out, in0, s1, s2, o0))
+        else:
+            do(q, r, w, lambda: V.tensor_scalar(out, in0, s1, s2, o0, o1))
+
+    def fill(w, ap, c):
+        do("V", "", w, lambda: V.memset(ap, c))
+
+    def pick(out, outs, win, wins, off, r, rs, w, ws, ro):
+        do("V", r + " " + ro, w, lambda: V.tensor_copy(out.bitcast(dt.uint32), win.bitcast(dt.uint32).indirect(off)))
+        do("S", rs + " " + ro, ws, lambda: S.activation(outs, wins.indirect(off), AF.Copy))
+
+    def bank(k, n):
+        return T.ps[:, 512 * k:512 * k + n]
+
+    def mm(k, n, lc, lsc, rc, rsc, r, start=True, stop=True):
+        do("P", r, "#%d" % k, lambda: P.matmul_mx(bank(k, n), lc, lsc, rc, rsc, start, stop), acc=not start)
+
+    grp = near[rank]
+    mates = [q for q in grp if q != rank]
+    on_mates = [q for q in mates if q in chip[rank]]
+    off_mates = [q for q in mates if q not in chip[rank]]
+    eoff = topo.engines(core, cores[off_mates[0]])
+    eon = [e for e in topo.engines(core, cores[on_mates[0]]) if e not in eoff]
+    eall = topo.engines(core, mrel[rank])
+    hosted = {q: sorted((q, partner[q])) for q in grp}
+    h = grp.index(rank)
+    lo, hi = hosted[rank]
+    own = 0 if rank == lo else 1
+    order = [s for q in grp for s in hosted[q]]
+    weight = [2.0 ** (N - 1 - s) for s in order]
+
+    def spread(sem, r, src, dst):
+        send(sem, r, [(src, [(cores[q], dst) for q in off_mates], eoff), (src, [(cores[q], dst) for q in on_mates], eon)])
+
+    dma("Y", "dx", "", "xt", [(T.xt[:, 0:64], T.x[:, :])])
+    dma("S", "dm", "", "mt", [(T.mt[:, :], T.me[:, :])])
+    dma("Y", "dw", "", "wt", [(T.wt[:, :], T.w[:, :])])
+    do("G", "", "pint0", lambda: g.iota(T.pint[:, 0:1], [[0, 1]], 0, 1))
+    do("G", "", "b8", lambda: g.iota(T.b8[:, :], [[1, 8]], 0, 0, allow_small_or_imprecise_dtypes=True))
+    do("G", "", "jf", lambda: g.iota(T.jf[:, :], [[1, 128]], 0, 0, allow_small_or_imprecise_dtypes=True))
+    do("G", "", "jm", lambda: g.iota(T.jm[:, :], [[0, 16], [1, 16]], 0, 0, allow_small_or_imprecise_dtypes=True))
+    fill("xz", T.xt[:, 64:512], 0.0)
+    fill("zz", T.zz[:, :], 0.0)
+    for t in range(2):
+        lm = T["lm%d" % t]
+        fill("lmo%d" % t, lm[:, 4 * h:4 * h + 4], 0.0)
+    ts("V", "pint0", "p16i", T.pint[:, 1:2], T.pint[:, 0:1], 15, None, op.bitwise_and)
+    ts("V", "pint0", "g16i", T.pint[:, 2:3], T.pint[:, 0:1], 4, None, op.logical_shift_right)
+    do("V", "pint0", "pf0", lambda: V.tensor_copy(T.pf[:, 0:1], T.pint[:, 0:1]))
+    do("V", "p16i", "p16", lambda: V.tensor_copy(T.pf[:, 1:2], T.pint[:, 1:2]))
+    do("V", "g16i", "g16", lambda: V.tensor_copy(T.pf[:, 2:3], T.pint[:, 2:3]))
+    do("V", "p16i", "ox", lambda: V.tensor_copy(T.ox[:, 0:1], T.pint[:, 1:2]))
+    pf, p16, g16 = T.pf[:, 0:1], T.pf[:, 1:2], T.pf[:, 2:3]
+    for k in range(4):
+        ts("V", "p16", "rm%d" % k, T.rmk[:, k:k + 1], p16, float(k), None, op.is_equal)
+    ts("V", "p16", "rm4", T.rmk[:, 4:5], p16, 2.0, None, op.is_lt)
+    ts("V", "p16", "rm5", T.rmk[:, 5:6], p16, 3.0, None, op.is_lt)
+    do("V", "rm2 rm3", "rm6", lambda: V.tensor_tensor(T.rmk[:, 6:7], T.rmk[:, 2:3], T.rmk[:, 3:4], op.add))
+    do("V", "xt xz", "xq xqs", lambda: V.quantize_mx(T.xq[:, 0:128], T.xqs[:, 0:128], T.xt[:, :]))
+    mo = 128 * own
+    do("V", "mt", "mcown0 mcown0s", lambda: V.quantize_mx(T.mc0[:, mo:mo + 128], T.mc0s[:, mo:mo + 128], T.mt[:, :]))
+    qa = QO + A * rank
+    ra = A * chip[rank].index(rank)
+    xs = T.xq[:, 0:A].bitcast(dt.uint8)
+    xd = T.ld0[:, qa:qa + A].bitcast(dt.uint8)
+    send("xa", "xq", [(xs, [(xrel[rank][0], T.rx[:, ra:ra + A].bitcast(dt.uint8))] + [(cores[q], xd) for q in on_mates], eon),
+                      (xs, [(cores[q], xd) for q in off_mates], eoff)])
+    xs, xd = T.xqs[:, 0:A], T.ld0s[:, qa:qa + A]
+    send("xa", "xqs", [(xs, [(xrel[rank][1], T.rxs[:, ra:ra + A])] + [(cores[q], xd) for q in on_mates], eon),
+                       (xs, [(cores[q], xd) for q in off_mates], eoff)])
+    send("mr", "mcown0", [(T.mc0[:, mo:mo + 128].bitcast(dt.uint8), [(mrel[rank], T.rm[:].bitcast(dt.uint8))], eall)])
+    send("ms", "mcown0s", [(T.mc0s[:, mo:mo + 128], [(mrel[rank], T.rms[:])], eall)])
+    pick(T.ld0[:, qa:qa + A], T.ld0s[:, qa:qa + A], T.xq[:, 0:128], T.xqs[:, 0:128], T.ox[:, 0:1],
+         "xq", "xqs", "qown0", "qown0s", "ox")
+    foff = len(eoff)
+    arrive("xa", 2 * (len(off_mates) * foff + len(on_mates) * len(eon) + foff * (len(far[rank]) // len(chip[rank]))), "qfar0 qfar0s")
+    arrive("ma", 2 * foff, "mcfar0 mcfar0s")
+    do("G", "", "wina", lambda: g.iota(T.wina[:, :], [[0, 32], [1, 16]], 0, 0, allow_small_or_imprecise_dtypes=True))
+    do("G", "", "d1", lambda: g.iota(T.d1[:, :], [[0, 2], [16, 16], [0, 16]], 0, 0, allow_small_or_imprecise_dtypes=True))
+    do("G", "", "d2", lambda: g.iota(T.d2[:, :], [[256, 2], [0, 256]], 0, 0, allow_small_or_imprecise_dtypes=True))
+    dma("Y", "t0", "d1", "wina", [(T.wina[1:128:16, :], T.d1[1:128:16, :])])
+    dma("Y", "t1", "d2", "wina", [(T.wina[2:128:16, :], T.d2[2:128:16, :])])
+    for i, k in enumerate((5, 0, 1, 4, 6)):
+        do("S", "zz rm%d" % k, "wt%d" % i,
+           lambda i=i, k=k: S.activation(T.wtile[:, 512 * i:512 * i + 512], T.zz[:, :], AF.Identity, bias=T.rmk[:, k:k + 1]))
+    for nm, n in (("ha", 520), ("hc", 520), ("h2", 520), ("h3", 1032), ("ht", 520)):
+        for a in range(0, n, 512):
+            b = min(n, a + 512)
+            do("S", "zz", nm + "z%d" % (a // 512), lambda nm=nm, a=a, b=b: S.activation(T[nm][:, a:b], T.zz[:, 0:b - a], AF.Copy))
+    ts("V", "b8 g16", "dg", T.dg[:, :], T.b8[:, :], g16, None, op.is_equal)
+    ts("V", "jm p16", "m1", T.m1[:, :], T.jm[:, :], p16, None, op.is_equal)
+    ts("V", "jm", "hold", T.hold[:, :], T.jm[:, :], 0.0, None, op.is_gt)
+    fill("et", T.et[:, :], 0.0)
+    for b in range(4):
+        ts("V", "jf pf0 et", "et%d" % b, T.et[:, 512 * b + b:512 * b + 512:4], T.jf[:, :], pf, 0.5, op.is_equal, op.mult)
+    do("V", "et et0 et1 et2 et3", "ec ecs", lambda: V.quantize_mx(T.ec[:, :], T.ecs[:, :], T.et[:, :]))
+    do("V", "wt0 wt1 wt2 wt3", "wc wcs", lambda: V.quantize_mx(T.wc[:, 0:512], T.wcs[:, 0:512], T.wtile[:, 0:2048]))
+    do("V", "wt4", "wc4 wcs4", lambda: V.quantize_mx(T.wc[:, 512:640], T.wcs[:, 512:640], T.wtile[:, 2048:2560]))
+    for nm, n in (("ha", 520), ("hc", 520), ("h2", 520), ("h3", 1032)):
+        do("V", "xt %sz%d" % (nm, (n - 1) // 512), nm + "x", lambda nm=nm, n=n: V.tensor_copy(T[nm][:, n - 8:n], T.xt[:, 0:8]))
+    for i, (nm, val) in enumerate((("winc", lambda s: float(s == lo)), ("tc1", lambda s: float(s == hi)),
+                                   ("tc2", lambda s: 256.0 * (N - s)), ("tc3", lambda s: 32.0 * order.index(s)))):
+        fill(nm + "z", T[nm][:, 0:256], 0.0)
+        for s in range(N):
+            if val(s):
+                do("V", nm + "z", nm + "_%d" % s,
+                   lambda nm=nm, s=s, val=val: V.memset(T[nm][:, 2 ** (N - 1 - s):2 ** (N - s)], val(s)))
+    keys = lambda nm: " ".join([nm + "z"] + [nm + "_%d" % s for s in range(N)])
+    for k in (1, 2, 3):
+        dma("Y", "t%d" % (k + 1), keys("tc%d" % k) + " " + keys("winc"), "wincr%d" % k,
+            [(T.winc[k:128:16, :], T["tc%d" % k][k:128:16, :])])
+    WINC = keys("winc") + " wincr1 wincr2 wincr3"
+    for i in range(N):
+        fill("vd%d" % i, T.vd[:, i:i + 1], 256.0 * (N - order[i]) + 32.0 * i)
+        fill("wd%d" % i, T.wd[:, i:i + 1], weight[i - 1] / weight[i] if i else 1.0)
+    VD, WD = " ".join("vd%d" % i for i in range(N)), " ".join("wd%d" % i for i in range(N))
+    ts("V", "jf pf0", "tri", T.tri[:, :], T.jf[:, :], pf, None, op.is_lt)
+    for k in range(4):
+        ts("V", "p16", "kb%d" % k, T.kb[:, k:k + 1], p16, 16.0 * (k % 2) + 0.5, None, op.add)
+    fill("kb4", T.kb[:, 4:5], E + 0.5)
+    ts("V", "pf0", "old", T.kb[:, 5:6], pf, float(QO), None, op.add)
+    ts("V", "pf0", "nold", T.kb[:, 6:7], pf, -1.0, -float(QO), op.mult, op.add)
+    for e in range(2):
+        ts("V", "pf0", "cp%d" % e, T.cc[:, e:e + 1], pf, 128.0 * e + 1, None, op.add)
+        ts("V", "pf0", "cl%d" % e, T.cc[:, 2 + e:3 + e], pf, 128.0 * e, None, op.add)
+        ts("V", "pf0", "cd%d" % e, T.cc[:, 4 + e:5 + e], pf, -1.0, 384.0 - 128.0 * e, op.mult, op.add)
+    do("V", "wt", "wq wqs", lambda: V.quantize_mx(T.wq[:, :], T.wqs[:, :], T.wt[:, :]))
+
+    def rows(off, ro, n, h_, hk, hcod, hsc, win, wk):
+        do("V", "%s %sz0 %sx %s" % (ro, hk, hk, wk), hk + "g",
+           lambda: V.tensor_copy(h_[:, 0:4 * n:4], win.indirect(off)))
+        do("V", "%sg %sz0 %sx" % (hk, hk, hk) + (" h3z1 h3z2" if n > 128 else ""), hk + "c",
+           lambda: V.quantize_mx(hcod[:, 0:n + 2], hsc[:, 0:n + 2], h_[:, 0:4 * n + 8]))
+
+    def wrap(k, n, out, wo):
+        do("V", "#%d m1" % k, "w1", lambda: V.tensor_tensor_scan(T.w1[:, 0:n], bank(k, n), T.m1[:, 0:n], 0.0, op.add, op.mult))
+        do("V", "w1 hold", "w2", lambda: V.tensor_tensor_scan(T.w2[:, 0:n], T.hold[:, 0:n], T.w1[:, 0:n], 0.0, op.mult, op.add))
+        do("V", "w2", wo, lambda: V.tensor_copy(out, T.w2[:, 15:n:16]))
+
+    W3 = (T.wc[:, 0:128], T.wcs[:, 0:128])
+    for t in range(2):
+        ld, lds = T["ld%d" % t], T["ld%ds" % t]
+        mc, mcs = T["mc%d" % t], T["mc%ds" % t]
+        mp, mps = T["mp%d" % t], T["mp%ds" % t]
+        lm = T["lm%d" % t]
+        q, qs = ld[:, QO:QO + 128], lds[:, QO:QO + 128]
+        Q = "qown%d qown%ds qfar%d qfar%ds" % (t, t, t, t)
+        MEM = "mcown%d mcfar%d" % (t, t)
+        MEMS = "mcown%ds mcfar%ds" % (t, t)
+        mm(0, 256, q, qs, mc[:, 0:256], mcs[:, 0:256], Q + " " + MEM + " " + MEMS)
+        for e in range(2):
+            do("V", "#0", "lmo%d" % t if e == 0 else "lmp%d" % t,
+               lambda e=e: V.tensor_reduce(lm[:, 4 * h + 2 * e:4 * h + 2 * e + 1], T.ps[:, 128 * e:128 * e + 128], X, op.max))
+        spread("m%d" % t, "lmo%d lmp%d" % (t, t), lm[:, 4 * h:4 * h + 4], lm[:, 4 * h:4 * h + 4])
+        arrive("m%d" % t, len(off_mates) * foff + len(on_mates) * len(eon), "lma%d" % t)
+        for b in range(4):
+            mm(1 + b, 128, T.ec[:, 128 * b:128 * b + 128], T.ecs[:, 128 * b:128 * b + 128], q, qs, "ec ecs " + Q, True, False)
+        do("V", "#0 zz", "cm", lambda: V.tensor_tensor_scan(T.cm[:, :], T.ps[:, 0:256], T.zz[:, 0:256], -1e29, op.max, op.add))
+        a = T.aa[:, t:t + 1]
+        do("S", "cm", "jk a%d" % t, lambda: S.activation(T.jk[:, :], T.cm[:, :], AF.Sign, bias=T.cm[:, 255:256], scale=-1.0, accum_out=a))
+        ts("V", "dg a%d" % t, "oa", T.oa[:, :], T.dg[:, :], a, None, op.mult)
+        rows(T.oa[:, 0:8], "oa", 128, T.ha, "ha", T.hac, T.has, T.wina[:, :], "wina")
+        mm(7, 130, W3[0], W3[1], T.hac[:, 0:130], T.has[:, 0:130], "wc wcs hac")
+        wrap(7, 128, T.oaw[:, :], "oaw")
+        do("S", "#7", "fra", lambda: S.activation(T.fra[:, :], bank(7, 128), AF.Identity, bias=1.0))
+        pick(mp[:, :], mps[:, :], mc[:, 0:256], mcs[:, 0:256], T.oaw[:, 0:8], MEM, MEMS, "mp%d" % t, "mp%ds" % t, "oaw")
+        for b in range(4):
+            mm(1 + b, 128, T.ec[:, 128 * b:128 * b + 128], T.ecs[:, 128 * b:128 * b + 128], mp[:, :], mps[:, :],
+               "ec ecs mp%d mp%ds" % (t, t), False, True)
+        for b in range(4):
+            if b % 2 == 0:
+                do("V", "#%d htz0" % (1 + b), "ht%d" % b, lambda b=b: V.tensor_copy(T.ht[:, b:512:4], bank(1 + b, 128)))
+            else:
+                do("S", "#%d htz0" % (1 + b), "ht%d" % b, lambda b=b: S.activation(T.ht[:, b:512:4], bank(1 + b, 128), AF.Copy))
+        do("V", "ht0 ht1 ht2 ht3 htz0 htz1", "cand%d cand%ds" % (t, t),
+           lambda: V.quantize_mx(mc[:, 256:386], mcs[:, 256:386], T.ht[:, :]))
+        ts("V", "a%d" % t, "wv0", T.wv[:, 0:1], a, 128.0, 128.0 * (hi - 1 - lo), op.is_ge, op.mult)
+        for c in (t, t + 2):
+            ts("V", "wv0 a%d" % t, "nlo%d" % c, T.nl[:, 4 * h + c:4 * h + c + 1], a, T.wv[:, 0:1], 128.0 * lo, op.add, op.add)
+        if t == 1:
+            spread("nn", "nlo0 nlo1 nlo2 nlo3", T.nl[:, 4 * h:4 * h + 4], T.nl[:, 4 * h:4 * h + 4])
+            arrive("nn", len(off_mates) * foff + len(on_mates) * len(eon), "nla")
+        LM = "lmo%d lmp%d lma%d" % (t, t, t)
+        do("V", LM, "mx", lambda: V.tensor_reduce(T.mx[:, :], lm[:, 0:16:2], X, op.max))
+        ts("V", LM + " mx", "eq", T.eq[:, :], lm[:, 0:16:2], T.mx[:, 0:1], None, op.is_equal)
+        do("V", "eq " + WD, "sc", lambda: V.tensor_tensor_scan(T.sc[:, :], T.wd[:, :], T.eq[:, :], 0.0, op.mult, op.add))
+        ts("V", "dg sc", "oc8", T.oc8[:, :], T.dg[:, :], T.sc[:, 7:8], None, op.mult)
+        rows(T.oc8[:, 0:8], "oc8", 128, T.hc, "hc", T.hcc, T.hcs, T.winc[:, :], WINC)
+        for k, i in ((5, 1), (6, 2), (0, 4), (7, 3)):
+            mm(k, 130, T.wc[:, 128 * i:128 * i + 128], T.wcs[:, 128 * i:128 * i + 128], T.hcc[:, 0:130], T.hcs[:, 0:130],
+               "wc wcs wc4 wcs4 hcc")
+        do("V", "#5 zz", "clo", lambda: V.tensor_tensor_scan(T.clo[:, :], bank(5, 128), T.zz[:, 0:128], 0.0, op.add, op.add))
+        do("V", "#6 zz", "chi", lambda: V.tensor_tensor_scan(T.chi[:, :], bank(6, 128), T.zz[:, 0:128], 0.0, op.add, op.add))
+        for c, src, nm in ((0, T.clo, "clo"), (1, T.clo, "clo"), (2, T.chi, "chi")):
+            do("S", "%s kb%d" % (nm, c), "jk acc%d" % c,
+               lambda c=c, src=src: S.activation(T.jk[:, 0:128], src[:, :], AF.Sign, bias=T.kb[:, c:c + 1], scale=-1.0,
+                                                 accum_out=T.acc[:, c:c + 1]))
+        ts("V", "chi kb3", "le", T.le[:, :], T.chi[:, :], T.kb[:, 3:4], None, op.is_le)
+        do("V", "le", "acv", lambda: V.tensor_reduce(T.acv[:, :], T.le[:, :], X, op.add))
+        do("V", "acv", "os3", lambda: V.tensor_copy(T.oslot[:, 3:4], T.acv[:, :]))
+        ts("V", "acc0 acc1 acc2", "os0", T.oslot[:, 0:3], T.acc[:, 0:3], 0.5, 64.0, op.mult, op.add)
+        pick(ld[:, 64 * h:64 * h + 64], lds[:, 64 * h:64 * h + 64], mc[:, 256:386], mcs[:, 256:386], T.oslot[:, 0:4],
+             "cand%d" % t, "cand%ds" % t, "slot%d" % t, "slot%ds" % t, "os0 os3")
+        spread("c%d" % t, "slot%d" % t, ld[:, 64 * h:64 * h + 64].bitcast(dt.uint8), ld[:, 64 * h:64 * h + 64].bitcast(dt.uint8))
+        spread("c%d" % t, "slot%ds" % t, lds[:, 64 * h:64 * h + 64], lds[:, 64 * h:64 * h + 64])
+        arrive("c%d" % t, 2 * (len(off_mates) * foff + len(on_mates) * len(eon)), "land%d land%ds" % (t, t))
+        for c, src, nm in ((0, T.clo, "clo"), (1, T.chi, "chi")):
+            do("S", "%s kb4" % nm, "jk ta%d" % c,
+               lambda c=c, src=src: S.activation(T.jk[:, 0:128], src[:, :], AF.Sign, bias=T.kb[:, 4:5], scale=-1.0,
+                                                 accum_out=T.ta[:, c:c + 1]))
+        v, an = T.vv[:, t:t + 1], T.an[:, t:t + 1]
+        do("V", "eq " + VD, "pv", lambda: V.tensor_tensor(T.pv[:, :], T.eq[:, :], T.vd[:, :], op.mult))
+        do("V", "pv", "v%d" % t, lambda: V.tensor_reduce(v, T.pv[:, :], X, op.max))
+        ts("V", "#0 v%d" % t, "same", T.same[:, :], bank(0, 128), v, None, op.is_equal)
+        do("V", "same tri", "sc2", lambda: V.tensor_tensor_scan(T.sc2[:, :], T.same[:, :], T.tri[:, :], 0.0, op.add, op.mult))
+        do("V", "v%d" % t, "bi0", lambda: V.tensor_copy(T.bi[:, 0:1], v))
+        do("V", "sc2", "kk0", lambda: V.tensor_reduce(T.kk[:, 0:1], T.sc2[:, :], X, op.max))
+        ts("V", "bi0", "bi1", T.bi[:, 1:2], T.bi[:, 0:1], 255, None, op.bitwise_and)
+        ts("V", "kk0", "an%d" % t, an, T.kk[:, 0:1], float(E), None, op.is_lt)
+        do("V", "bi1", "kk1", lambda: V.tensor_copy(T.kk[:, 1:2], T.bi[:, 1:2]))
+        ts("V", "kk0 kk1 nold", "kk2", T.kk[:, 2:3], T.kk[:, 0:1], T.kk[:, 1:2], T.kb[:, 6:7], op.add, op.add)
+        ts("V", "kk2 an%d old" % t, "kk3", T.kk[:, 3:4], T.kk[:, 2:3], an, T.kb[:, 5:6], op.mult, op.add)
+        ts("V", "dg kk3", "o2", T.o2[:, :], T.dg[:, :], T.kk[:, 3:4], None, op.mult)
+        rows(T.o2[:, 0:8], "o2", 128, T.h2, "h2", T.h2c, T.h2s, T.wina[:, :], "wina")
+        mm(1, 130, W3[0], W3[1], T.h2c[:, 0:130], T.h2s[:, 0:130], "wc wcs h2c")
+        do("V", "#7 fra", "tg", lambda: V.tensor_tensor(T.tg[:, :], bank(7, 128), T.fra[:, :], op.mult))
+        halves = (0, 1) if t == 0 else (own,)
+        for e in halves:
+            ts("V", "tg cp%d" % e, "ep%d" % e, T.ep[:, 128 * e:128 * e + 128], T.tg[:, :], T.cc[:, e:e + 1], None, op.is_equal)
+        for e in halves:
+            do("V", "ep%d zz" % e, "co%d" % e,
+               lambda e=e: V.tensor_tensor_scan(T.co[:, 128 * e:128 * e + 128], T.ep[:, 128 * e:128 * e + 128], T.zz[:, 0:128],
+                                                0.0, op.max, op.add))
+        for e in halves:
+            do("V", "co%d" % e, "jc%d" % e, lambda e=e: V.tensor_reduce(T.jc[:, e:e + 1], T.co[:, 128 * e:128 * e + 128], X, op.add))
+        wrap(1, 128, T.oq[:, :], "oq")
+        c0, c1 = halves[0], halves[-1] + 1
+        ks = lambda nm: " ".join(nm + "%d" % e for e in halves)
+        ts("V", ks("jc"), "ju", T.jc[:, 2 + c0:2 + c1], T.jc[:, c0:c1], -2.0, 128.0, op.mult, op.add)
+        do("V", ks("jc") + " " + ks("cd"), "jd", lambda: V.tensor_tensor(T.jc[:, 4 + c0:4 + c1], T.cc[:, 4 + c0:4 + c1], T.jc[:, c0:c1], op.subtract))
+        do("V", "ju " + ks("ta"), "jg", lambda: V.tensor_tensor(T.jc[:, 6 + c0:6 + c1], T.jc[:, 2 + c0:2 + c1], T.ta[:, c0:c1], op.is_lt))
+        do("V", "jd jg", "jh", lambda: V.tensor_tensor(T.wv[:, 4 + c0:4 + c1], T.jc[:, 4 + c0:4 + c1], T.jc[:, 6 + c0:6 + c1], op.mult))
+        do("V", "jh " + ks("cl"), "l3", lambda: V.tensor_tensor(T.wv[:, 6 + c0:6 + c1], T.wv[:, 4 + c0:4 + c1], T.cc[:, 2 + c0:2 + c1], op.add))
+        n3 = 128 * len(halves)
+        for i, e in enumerate(halves):
+            ts("V", "dg l3", "o3_%d" % i, T.o3[:, 8 * i:8 * i + 8], T.dg[:, :], T.wv[:, 6 + e:7 + e], None, op.mult)
+        o3k = " ".join("o3_%d" % i for i in range(len(halves)))
+        if t == 0:
+            rows(T.o3[:, 0:16], o3k, 256, T.h3, "h3", T.h3c, T.h3s, T.wina[:, :], "wina")
+            mm(2, 258, W3[0], W3[1], T.h3c[:, 0:258], T.h3s[:, 0:258], "wc wcs h3c")
+            wrap(2, 256, T.om[:, :], "om")
+            pick(T.mc1[:, 0:256], T.mc1s[:, 0:256], mc[:, 0:386], mcs[:, 0:386], T.om[:, 0:16],
+                 MEM + " cand0", MEMS + " cand0s", "mcown1", "mcown1s", "om")
+            note(("V", cnt["V"], "V", dict(known["V"])), [], ["mcfar1"])
+            note(("S", cnt["S"], "S", dict(known["S"])), [], ["mcfar1s"])
+            pick(T.ld1[:, QO:QO + 128], T.ld1s[:, QO:QO + 128], ld[:, 0:384], lds[:, 0:384], T.oq[:, 0:8],
+                 "slot0 land0 qown0 qfar0", "slot0s land0s qown0s qfar0s", "qown1", "qown1s", "oq")
+            note(("V", cnt["V"], "V", dict(known["V"])), [], ["qfar1"])
+            note(("S", cnt["S"], "S", dict(known["S"])), [], ["qfar1s"])
+        else:
+            rows(T.o3[:, 0:8], o3k, 128, T.ha, "ha", T.hac, T.has, T.wina[:, :], "wina")
+            mm(2, 130, W3[0], W3[1], T.hac[:, 0:130], T.has[:, 0:130], "wc wcs hac")
+            wrap(2, 128, T.om[:, 0:8], "om")
+            pick(T.fm[:, :], T.fms[:, :], mc[:, 0:386], mcs[:, 0:386], T.om[:, 0:8],
+                 MEM + " cand1", MEMS + " cand1s", "fm", "fms", "om")
+            dma("Y", "u0", "fm", "out0", [(T.oc[:, :], T.fm[:, :].bitcast(dt.uint8))])
+            for k in range(4):
+                dma("Y", "u%d" % (1 + k), "fms", "out%d" % (1 + k), [(T.osc[4 * k:4 * k + 4, :], T.fms[32 * k:32 * k + 4, :])])
+
+    for t in range(2):
+        v, an = T.vv[:, t:t + 1], T.an[:, t:t + 1]
+        z = 8 * t
+        ts("V", VD + " v%d" % t, "pv", T.pv[:, :], T.vd[:, :], v, None, op.is_equal)
+        do("V", "pv nla nlo%d nlo%d" % (t, t + 2), "eq", lambda: V.tensor_tensor(T.eq[:, :], T.pv[:, :], T.nl[:, t:16:2], op.mult))
+        do("V", "eq", "wg", lambda: V.tensor_reduce(T.wv[:, 1:2], T.eq[:, :], X, op.add))
+        ts("V", "wg", "wh", T.wv[:, 2:3], T.wv[:, 1:2], 2.0, 1.0, op.mult, op.add)
+        ts("V", "wh an%d" % t, "wk", T.wv[:, 3:4], T.wv[:, 2:3], an, None, op.mult)
+        ts("V", "wk wg", "wo%d" % t, T.wo[:, t:t + 1], T.wv[:, 3:4], T.wv[:, 1:2], 1.0, op.subtract, op.subtract)
+        dma("Y", "u%d" % (5 + t), "wo%d" % t, "out%d" % (5 + t), [(T.wi[t:t + 1, :], T.wo[:, t:t + 1])])
+    pick(T.qf[:, :], T.qfs[:, :], T.ld1[:, 0:384], T.ld1s[:, 0:384], T.oq[:, 0:8],
+         "slot1 land1 qown1 qfar1", "slot1s land1s qown1s qfar1s", "qf", "qfs", "oq")
+    mm(3, 128, T.wq[:, :], T.wqs[:, :], T.qf[:, :], T.qfs[:, :], "wq wqs qf qfs")
+    do("V", "#3", "ysb", lambda: V.tensor_copy(T.ysb[:, :], bank(3, 128)))
+    dma("Y", "u7", "ysb", "outy", [(T.y[:, :], T.ysb[:, :])])
+    for s, n in cnt.items():
+        if known["G"].get(s, 0) < n:
+            g.wait_ge(T.sem[s], n)
+    g.wait_ge(T.sem.ls, ls[0])

@@ -2,59 +2,27 @@ from concourse.bass import DstId, RemoteDMATransfer
 from concourse.mybir import dt, AluOpType, AxisListType, ActivationFunctionType
 
 F8 = "float8_e4m3fn_x4"
-SCRATCH = {
-    "ps": ("psum", [128, 4096], "float32"),
-    "xt": ("sbuf", [128, 512], "bfloat16"), "mt": ("sbuf", [128, 512], "bfloat16"), "wt": ("sbuf", [128, 512], "bfloat16"),
-    "xq": ("sbuf", [128, 128], F8), "xqs": ("sbuf", [128, 128], "uint8"),
-    "wq": ("sbuf", [128, 128], F8), "wqs": ("sbuf", [128, 128], "uint8"),
-    "rx": ("sbuf", [128, 32], F8), "rxs": ("sbuf", [128, 32], "uint8"),
-    "rm": ("sbuf", [128, 128], F8), "rms": ("sbuf", [128, 128], "uint8"),
-    "ld0": ("sbuf", [128, 384], F8), "ld0s": ("sbuf", [128, 384], "uint8"),
-    "ld1": ("sbuf", [128, 384], F8), "ld1s": ("sbuf", [128, 384], "uint8"),
-    "qf": ("sbuf", [128, 128], F8), "qfs": ("sbuf", [128, 128], "uint8"),
-    "mc0": ("sbuf", [128, 416], F8), "mc0s": ("sbuf", [128, 416], "uint8"),
-    "mc1": ("sbuf", [128, 416], F8), "mc1s": ("sbuf", [128, 416], "uint8"),
-    "fm": ("sbuf", [128, 128], F8), "fms": ("sbuf", [128, 128], "uint8"),
-    "mp0": ("sbuf", [128, 128], F8), "mp0s": ("sbuf", [128, 128], "uint8"),
-    "mp1": ("sbuf", [128, 128], F8), "mp1s": ("sbuf", [128, 128], "uint8"),
-    "wc": ("sbuf", [128, 640], F8), "wcs": ("sbuf", [128, 640], "uint8"),
-    "ec": ("sbuf", [128, 512], F8), "ecs": ("sbuf", [128, 512], "uint8"),
-    "hac": ("sbuf", [128, 136], F8), "has": ("sbuf", [128, 136], "uint8"),
-    "hcc": ("sbuf", [128, 136], F8), "hcs": ("sbuf", [128, 136], "uint8"),
-    "h2c": ("sbuf", [128, 136], F8), "h2s": ("sbuf", [128, 136], "uint8"),
-    "h3c": ("sbuf", [128, 264], F8), "h3s": ("sbuf", [128, 264], "uint8"),
-    "ha": ("sbuf", [128, 520], "bfloat16"), "hc": ("sbuf", [128, 520], "bfloat16"),
-    "h2": ("sbuf", [128, 520], "bfloat16"), "h3": ("sbuf", [128, 1032], "bfloat16"),
-    "ht": ("sbuf", [128, 520], "bfloat16"),
-    "wtile": ("sbuf", [128, 2560], "bfloat16"), "et": ("sbuf", [128, 2048], "bfloat16"),
-    "zz": ("sbuf", [128, 512], "bfloat16"),
-    "wina": ("sbuf", [128, 512], "bfloat16"), "d1": ("sbuf", [128, 512], "bfloat16"), "d2": ("sbuf", [128, 512], "bfloat16"),
-    "winc": ("sbuf", [128, 256], "bfloat16"),
-    "tc1": ("sbuf", [128, 256], "bfloat16"), "tc2": ("sbuf", [128, 256], "bfloat16"), "tc3": ("sbuf", [128, 256], "bfloat16"),
-    "tri": ("sbuf", [128, 128], "bfloat16"), "m1": ("sbuf", [128, 256], "bfloat16"), "hold": ("sbuf", [128, 256], "bfloat16"),
-    "jf": ("sbuf", [128, 128], "float32"), "jm": ("sbuf", [128, 256], "bfloat16"), "b8": ("sbuf", [128, 8], "float32"),
-    "pint": ("sbuf", [128, 4], "int32"), "pf": ("sbuf", [128, 4], "float32"), "rmk": ("sbuf", [128, 8], "float32"),
-    "dg": ("sbuf", [128, 8], "float32"), "kb": ("sbuf", [128, 8], "float32"), "cc": ("sbuf", [128, 8], "float32"),
-    "vd": ("sbuf", [128, 8], "float32"), "wd": ("sbuf", [128, 8], "float32"), "ox": ("sbuf", [128, 2], "uint16"),
-    "lm0": ("sbuf", [128, 16], "float32"), "lm1": ("sbuf", [128, 16], "float32"), "nl": ("sbuf", [128, 16], "float32"),
-    "cm": ("sbuf", [128, 256], "float32"), "jk": ("sbuf", [128, 256], "bfloat16"),
-    "aa": ("sbuf", [128, 2], "float32"), "vv": ("sbuf", [128, 2], "float32"), "an": ("sbuf", [128, 2], "float32"),
-    "oa": ("sbuf", [128, 8], "uint16"), "oaw": ("sbuf", [128, 8], "uint16"),
-    "w1": ("sbuf", [128, 256], "float32"), "w2": ("sbuf", [128, 256], "float32"),
-    "fra": ("sbuf", [128, 128], "bfloat16"),
-    "mx": ("sbuf", [128, 1], "float32"), "eq": ("sbuf", [128, 8], "float32"), "sc": ("sbuf", [128, 8], "float32"),
-    "oc8": ("sbuf", [128, 8], "uint16"), "clo": ("sbuf", [128, 128], "bfloat16"), "chi": ("sbuf", [128, 128], "bfloat16"),
-    "acc": ("sbuf", [128, 4], "float32"), "acv": ("sbuf", [128, 1], "float32"), "le": ("sbuf", [128, 128], "bfloat16"),
-    "os": ("sbuf", [128, 4], "uint16"), "pv": ("sbuf", [128, 8], "float32"),
-    "same": ("sbuf", [128, 128], "bfloat16"), "sc2": ("sbuf", [128, 128], "bfloat16"),
-    "kk": ("sbuf", [128, 4], "float32"), "bi": ("sbuf", [128, 2], "int32"),
-    "o2": ("sbuf", [128, 8], "uint16"), "oq": ("sbuf", [128, 8], "uint16"),
-    "tg": ("sbuf", [128, 128], "bfloat16"), "ep": ("sbuf", [128, 256], "bfloat16"), "co": ("sbuf", [128, 256], "bfloat16"),
-    "jc": ("sbuf", [128, 8], "float32"), "ta": ("sbuf", [128, 2], "float32"),
-    "o3": ("sbuf", [128, 16], "uint16"), "om": ("sbuf", [128, 16], "uint16"),
-    "wv": ("sbuf", [128, 16], "float32"), "wo": ("sbuf", [128, 2], "float32"), "ysb": ("sbuf", [128, 128], "float32"),
-}
-SCRATCH["oslot"] = SCRATCH.pop("os")
+SCRATCH = {"ps": ("psum", [128, 4096], "float32")}
+for _n, _w in (("xq", 128), ("wq", 128), ("rx", 32), ("rm", 128), ("ld0", 384), ("ld1", 384), ("qf", 128), ("mc0", 416),
+               ("mc1", 416), ("fm", 128), ("mp0", 128), ("mp1", 128), ("wc", 896), ("ec", 512), ("hac", 128), ("hfc", 128),
+               ("hcc", 136), ("hlc", 128)):
+    SCRATCH[_n] = ("sbuf", [128, _w], F8)
+    SCRATCH[_n + "s"] = ("sbuf", [128, _w], "uint8")
+for _n, _w in (("xt", 512), ("mt", 512), ("wt", 512), ("ha", 512), ("hf", 512), ("hc", 520), ("hl", 512), ("ht", 520),
+               ("wtile", 3584), ("et", 2048), ("zz", 512), ("wina", 512), ("d1", 512), ("d2", 512), ("winc", 256), ("tc1", 256),
+               ("tc2", 256), ("tc3", 256), ("tri", 128), ("m1", 96), ("hold", 96), ("jm", 128), ("jt", 512), ("jw", 96),
+               ("idn", 128), ("jk", 256), ("fra", 128), ("clo", 128), ("chi", 128), ("le", 128), ("eqt", 128), ("tg", 128),
+               ("ep", 256), ("co", 256)):
+    SCRATCH[_n] = ("sbuf", [128, _w], "bfloat16")
+for _n, _w in (("jf", 128), ("b8", 8), ("pf", 4), ("rmk", 8), ("dg", 8), ("kb", 8), ("cc", 8), ("vd", 8), ("wd", 8), ("lm0", 16),
+               ("lm1", 16), ("nl", 16), ("cm", 256), ("aa", 4), ("lw", 2), ("vv", 2), ("an", 2), ("w1", 96), ("w2", 96),
+               ("mx", 1), ("eq", 8), ("sc", 8), ("acc", 4), ("acv", 1), ("pv", 8), ("triv", 128), ("kk", 4), ("jc", 2),
+               ("ta", 2), ("jg", 2), ("jd", 2), ("l3", 2), ("un", 2), ("nm", 2), ("wv", 8), ("oh", 16), ("wo", 2), ("ysb", 128)):
+    SCRATCH[_n] = ("sbuf", [128, _w], "float32")
+for _n, _w in (("ox", 2), ("oaw", 8), ("oc8", 8), ("oslot", 4), ("o2", 8), ("o3", 16), ("ol", 24)):
+    SCRATCH[_n] = ("sbuf", [128, _w], "uint16")
+for _n, _w in (("pint", 4), ("bi", 2)):
+    SCRATCH[_n] = ("sbuf", [128, _w], "int32")
 SEMAPHORES = ["V", "S", "P", "G", "ls", "xa", "ma", "mr", "ms", "m0", "m1", "nn", "c0", "c1",
               "dx", "dm", "dw", "t0", "t1", "t2", "t3", "t4", "u0", "u1", "u2", "u3", "u4", "u5", "u6", "u7"]
 A = 16
@@ -73,7 +41,7 @@ def plan(T, topo):
     port = [[c for c in topo.cores_of(cores[r]) if c not in cores and topo.die(c) == topo.die(cores[r])
              and topo.may_write(c, cores[far[r][0]])] for r in range(n)]
     xrel = [(port[chip[r][0]][0], port[chip[r][1]][0]) for r in range(n)]
-    mrel = [port[r][1] for r in range(n)]
+    mrel = [(port[r][1], port[r][0]) for r in range(n)]
     return near, far, chip, partner, xrel, mrel
 
 
@@ -101,22 +69,26 @@ def relay(g, core, T, topo, pl):
     cores = T.cores
     n = [0]
     send = make_send(g, core, T, topo, n)
-    for r in range(len(cores)):
+    here = [r for r in range(len(cores)) if core in topo.cores_of(cores[r])]
+    for r in here[:1]:
         off = topo.engines(core, cores[far[r][0]])
-        on = [e for e in topo.engines(core, cores[r]) if e not in off] if core in topo.cores_of(cores[r]) else []
-        if chip[r][0] == r and core in xrel[r]:
-            g.wait_ge(T.sem.xa, len(on) * len(chip[r]))
-            a, b = QO + A * r, QO + A * r + A * len(chip[r])
+        on = [e for e in topo.engines(core, cores[r]) if e not in off]
+        if core in xrel[r]:
+            g.wait_ge(T.sem.xa, len(on) * len(here))
+            a, b = QO + A * r, QO + A * r + A * len(here)
             if core == xrel[r][0]:
                 send("xa", [(T.rx[:].bitcast(dt.uint8), [(cores[q], T.ld0[:, a:b].bitcast(dt.uint8)) for q in far[r]], off)])
             else:
                 send("xa", [(T.rxs[:], [(cores[q], T.ld0s[:, a:b]) for q in far[r]], off)])
-        if core == mrel[r]:
-            p = partner[r]
-            h = 128 if r > p else 0
-            g.wait_ge(T.sem.mr, len(on) + len(off))
+    for r in here:
+        p = partner[r]
+        h = 128 if r > p else 0
+        off, every = topo.engines(core, cores[p]), topo.engines(core, cores[r])
+        if core == mrel[r][0]:
+            g.wait_ge(T.sem.mr, len(every))
             send("ma", [(T.rm[:].bitcast(dt.uint8), [(cores[p], T.mc0[:, h:h + 128].bitcast(dt.uint8))], off)])
-            g.wait_ge(T.sem.ms, len(on) + len(off))
+        if core == mrel[r][1]:
+            g.wait_ge(T.sem.ms, len(every))
             send("ma", [(T.rms[:], [(cores[p], T.mc0s[:, h:h + 128])], off)])
     if n[0]:
         g.wait_ge(T.sem.ls, n[0])
@@ -143,11 +115,14 @@ def rank_program(g, core, T, topo):
         want = {}
         for e in deps:
             if known[q].get(e[0], 0) < e[1]:
-                want[e[0]] = max(want.get(e[0], (0, None))[0], e[1]), e
-        for s, (v, e) in want.items():
-            if known[q].get(s, 0) < v:
-                queue[q].wait_ge(T.sem[s], v)
-                known[q][s] = v
+                want[e[0]] = max(want.get(e[0], 0), e[1])
+        for e in deps:
+            for s, v in e[3].items():
+                if s in want and e[0] != s and want[s] <= v:
+                    del want[s]
+        for s, v in want.items():
+            queue[q].wait_ge(T.sem[s], v)
+            known[q][s] = v
         for e in deps:
             for s, v in e[3].items():
                 if known[q].get(s, 0) < v:
@@ -156,7 +131,7 @@ def rank_program(g, core, T, topo):
     def deps_of(q, r, w, acc):
         d = []
         for k in r:
-            d += [e for e in wr.get(k, [])]
+            d += wr.get(k, [])
             if k[0] == "#":
                 d += [e for e in rd.get(k, []) if e[2] != q]
         for k in w:
@@ -177,12 +152,11 @@ def rank_program(g, core, T, topo):
         cnt[q] = cnt.get(q, 0) + 1
         note((q, cnt[q], q, dict(known[q])), r, w)
 
-    def dma(q, sem, r, w, pairs):
+    def dma(q, sem, r, w, o, i):
         r, w = r.split(), w.split()
         need(q, deps_of(q, r, w, False))
-        for o, i in pairs:
-            queue[q].dma_start(o, i).then_inc(T.sem[sem], 16)
-            cnt[sem] = cnt.get(sem, 0) + 16
+        queue[q].dma_start(o, i).then_inc(T.sem[sem], 16)
+        cnt[sem] = cnt.get(sem, 0) + 16
         note((sem, cnt[sem], "dma", dict(known[q])), r, w)
 
     def arrive(sem, n, w):
@@ -194,11 +168,29 @@ def rank_program(g, core, T, topo):
         need("G", deps_of("G", r.split(), [], False))
         fused(sem, parts)
 
-    def ts(q, r, w, out, in0, s1, s2, o0, o1=None):
+    def ts(r, w, out, in0, s1, s2, o0, o1=None):
         if o1 is None:
-            do(q, r, w, lambda: V.tensor_scalar(out, in0, s1, s2, o0))
+            do("V", r, w, lambda: V.tensor_scalar(out, in0, s1, s2, o0))
         else:
-            do(q, r, w, lambda: V.tensor_scalar(out, in0, s1, s2, o0, o1))
+            do("V", r, w, lambda: V.tensor_scalar(out, in0, s1, s2, o0, o1))
+
+    def tt(r, w, out, in0, in1, o):
+        do("V", r, w, lambda: V.tensor_tensor(out, in0, in1, o))
+
+    def scan(r, w, out, d0, d1, init, o0, o1):
+        do("V", r, w, lambda: V.tensor_tensor_scan(out, d0, d1, init, o0, o1))
+
+    def red(r, w, out, in_, o):
+        do("V", r, w, lambda: V.tensor_reduce(out, in_, X, o))
+
+    def cp(r, w, out, in_):
+        do("V", r, w, lambda: V.tensor_copy(out, in_))
+
+    def act(r, w, out, in_, f, bias=0.0, scale=1.0, accum=None):
+        do("S", r, w, lambda: S.activation(out, in_, f, bias=bias, scale=scale, accum_out=accum))
+
+    def quant(r, w, c, s, in_):
+        do("V", r, w, lambda: V.quantize_mx(c, s, in_))
 
     def fill(w, ap, c):
         do("V", "", w, lambda: V.memset(ap, c))
@@ -207,7 +199,7 @@ def rank_program(g, core, T, topo):
         do("V", r + " " + ro, w, lambda: V.tensor_copy(out.bitcast(dt.uint32), win.bitcast(dt.uint32).indirect(off)))
         do("S", rs + " " + ro, ws, lambda: S.activation(outs, wins.indirect(off), AF.Copy))
 
-    def bank(k, n):
+    def bank(k, n=128):
         return T.ps[:, 512 * k:512 * k + n]
 
     def mm(k, n, lc, lsc, rc, rsc, r, start=True, stop=True):
@@ -219,44 +211,55 @@ def rank_program(g, core, T, topo):
     off_mates = [q for q in mates if q not in chip[rank]]
     eoff = topo.engines(core, cores[off_mates[0]])
     eon = [e for e in topo.engines(core, cores[on_mates[0]]) if e not in eoff]
-    eall = topo.engines(core, mrel[rank])
+    eall = topo.engines(core, mrel[rank][0])
     hosted = {q: sorted((q, partner[q])) for q in grp}
     h = grp.index(rank)
     lo, hi = hosted[rank]
     own = 0 if rank == lo else 1
     order = [s for q in grp for s in hosted[q]]
     weight = [2.0 ** (N - 1 - s) for s in order]
+    foff = len(eoff)
+    from_mates = len(off_mates) * foff + len(on_mates) * len(eon)
 
     def spread(sem, r, src, dst):
         send(sem, r, [(src, [(cores[q], dst) for q in off_mates], eoff), (src, [(cores[q], dst) for q in on_mates], eon)])
 
-    dma("Y", "dx", "", "xt", [(T.xt[:, 0:64], T.x[:, :])])
-    dma("S", "dm", "", "mt", [(T.mt[:, :], T.me[:, :])])
-    dma("Y", "dw", "", "wt", [(T.wt[:, :], T.w[:, :])])
-    do("G", "", "pint0", lambda: g.iota(T.pint[:, 0:1], [[0, 1]], 0, 1))
-    do("G", "", "b8", lambda: g.iota(T.b8[:, :], [[1, 8]], 0, 0, allow_small_or_imprecise_dtypes=True))
-    do("G", "", "jf", lambda: g.iota(T.jf[:, :], [[1, 128]], 0, 0, allow_small_or_imprecise_dtypes=True))
-    do("G", "", "jm", lambda: g.iota(T.jm[:, :], [[0, 16], [1, 16]], 0, 0, allow_small_or_imprecise_dtypes=True))
+    def iota(w, ap, pat, base=0, mul=0, flag=True):
+        if flag:
+            do("G", "", w, lambda: g.iota(ap, pat, base, mul, allow_small_or_imprecise_dtypes=True))
+        else:
+            do("G", "", w, lambda: g.iota(ap, pat, base, mul))
+
+    dma("Y", "dx", "", "xt", T.xt[:, 0:64], T.x[:, :])
+    dma("S", "dm", "", "mt", T.mt[:, :], T.me[:, :])
+    dma("Y", "dw", "", "wt", T.wt[:, :], T.w[:, :])
+    iota("pint0", T.pint[:, 0:1], [[0, 1]], 0, 1, False)
+    iota("b8", T.b8[:, :], [[1, 8]])
+    iota("jf", T.jf[:, :], [[1, 128]])
+    iota("jm", T.jm[:, :], [[0, 8], [1, 16]])
+    iota("jw", T.jw[:, :], [[0, 24], [1, 4]])
     fill("xz", T.xt[:, 64:512], 0.0)
     fill("zz", T.zz[:, :], 0.0)
     for t in range(2):
-        lm = T["lm%d" % t]
-        fill("lmo%d" % t, lm[:, 4 * h:4 * h + 4], 0.0)
-    ts("V", "pint0", "p16i", T.pint[:, 1:2], T.pint[:, 0:1], 15, None, op.bitwise_and)
-    ts("V", "pint0", "g16i", T.pint[:, 2:3], T.pint[:, 0:1], 4, None, op.logical_shift_right)
-    do("V", "pint0", "pf0", lambda: V.tensor_copy(T.pf[:, 0:1], T.pint[:, 0:1]))
-    do("V", "p16i", "p16", lambda: V.tensor_copy(T.pf[:, 1:2], T.pint[:, 1:2]))
-    do("V", "g16i", "g16", lambda: V.tensor_copy(T.pf[:, 2:3], T.pint[:, 2:3]))
-    do("V", "p16i", "ox", lambda: V.tensor_copy(T.ox[:, 0:1], T.pint[:, 1:2]))
-    pf, p16, g16 = T.pf[:, 0:1], T.pf[:, 1:2], T.pf[:, 2:3]
+        fill("lmz%d" % t, T["lm%d" % t][:, 4 * h:4 * h + 4], 0.0)
+    fill("nlz", T.nl[:, 4 * h:4 * h + 4], 0.0)
+    ts("pint0", "p16i", T.pint[:, 1:2], T.pint[:, 0:1], 15, None, op.bitwise_and)
+    ts("pint0", "g16i", T.pint[:, 2:3], T.pint[:, 0:1], 4, None, op.logical_shift_right)
+    cp("pint0", "pf0", T.pf[:, 0:1], T.pint[:, 0:1])
+    ts("p16i", "p4i", T.pint[:, 3:4], T.pint[:, 1:2], 2, None, op.logical_shift_right)
+    cp("p16i", "p16", T.pf[:, 1:2], T.pint[:, 1:2])
+    cp("g16i", "g16", T.pf[:, 2:3], T.pint[:, 2:3])
+    cp("p4i", "p4", T.pf[:, 3:4], T.pint[:, 3:4])
+    cp("p16i", "ox", T.ox[:, 0:1], T.pint[:, 1:2])
+    pf, p16, g16, p4 = T.pf[:, 0:1], T.pf[:, 1:2], T.pf[:, 2:3], T.pf[:, 3:4]
     for k in range(4):
-        ts("V", "p16", "rm%d" % k, T.rmk[:, k:k + 1], p16, float(k), None, op.is_equal)
-    ts("V", "p16", "rm4", T.rmk[:, 4:5], p16, 2.0, None, op.is_lt)
-    ts("V", "p16", "rm5", T.rmk[:, 5:6], p16, 3.0, None, op.is_lt)
-    do("V", "rm2 rm3", "rm6", lambda: V.tensor_tensor(T.rmk[:, 6:7], T.rmk[:, 2:3], T.rmk[:, 3:4], op.add))
-    do("V", "xt xz", "xq xqs", lambda: V.quantize_mx(T.xq[:, 0:128], T.xqs[:, 0:128], T.xt[:, :]))
+        ts("p16", "rm%d" % k, T.rmk[:, k:k + 1], p16, float(k), None, op.is_equal)
+    ts("p16", "rm4", T.rmk[:, 4:5], p16, 2.0, None, op.is_lt)
+    ts("p16", "rm5", T.rmk[:, 5:6], p16, 3.0, None, op.is_lt)
+    tt("rm2 rm3", "rm6", T.rmk[:, 6:7], T.rmk[:, 2:3], T.rmk[:, 3:4], op.add)
+    quant("xt xz", "xq xqs", T.xq[:, 0:128], T.xqs[:, 0:128], T.xt[:, :])
     mo = 128 * own
-    do("V", "mt", "mcown0 mcown0s", lambda: V.quantize_mx(T.mc0[:, mo:mo + 128], T.mc0s[:, mo:mo + 128], T.mt[:, :]))
+    quant("mt", "mcown0 mcown0s", T.mc0[:, mo:mo + 128], T.mc0s[:, mo:mo + 128], T.mt[:, :])
     qa = QO + A * rank
     ra = A * chip[rank].index(rank)
     xs = T.xq[:, 0:A].bitcast(dt.uint8)
@@ -266,36 +269,41 @@ def rank_program(g, core, T, topo):
     xs, xd = T.xqs[:, 0:A], T.ld0s[:, qa:qa + A]
     send("xa", "xqs", [(xs, [(xrel[rank][1], T.rxs[:, ra:ra + A])] + [(cores[q], xd) for q in on_mates], eon),
                        (xs, [(cores[q], xd) for q in off_mates], eoff)])
-    send("mr", "mcown0", [(T.mc0[:, mo:mo + 128].bitcast(dt.uint8), [(mrel[rank], T.rm[:].bitcast(dt.uint8))], eall)])
-    send("ms", "mcown0s", [(T.mc0s[:, mo:mo + 128], [(mrel[rank], T.rms[:])], eall)])
+    send("mr", "mcown0", [(T.mc0[:, mo:mo + 128].bitcast(dt.uint8), [(mrel[rank][0], T.rm[:].bitcast(dt.uint8))], eall)])
+    send("ms", "mcown0s", [(T.mc0s[:, mo:mo + 128], [(mrel[rank][1], T.rms[:])], eall)])
     pick(T.ld0[:, qa:qa + A], T.ld0s[:, qa:qa + A], T.xq[:, 0:128], T.xqs[:, 0:128], T.ox[:, 0:1],
          "xq", "xqs", "qown0", "qown0s", "ox")
-    foff = len(eoff)
-    arrive("xa", 2 * (len(off_mates) * foff + len(on_mates) * len(eon) + foff * (len(far[rank]) // len(chip[rank]))), "qfar0 qfar0s")
+    arrive("xa", 2 * (from_mates + foff * (len(far[rank]) // len(chip[rank]))), "qfar0 qfar0s")
     arrive("ma", 2 * foff, "mcfar0 mcfar0s")
-    do("G", "", "wina", lambda: g.iota(T.wina[:, :], [[0, 32], [1, 16]], 0, 0, allow_small_or_imprecise_dtypes=True))
-    do("G", "", "d1", lambda: g.iota(T.d1[:, :], [[0, 2], [16, 16], [0, 16]], 0, 0, allow_small_or_imprecise_dtypes=True))
-    do("G", "", "d2", lambda: g.iota(T.d2[:, :], [[256, 2], [0, 256]], 0, 0, allow_small_or_imprecise_dtypes=True))
-    dma("Y", "t0", "d1", "wina", [(T.wina[1:128:16, :], T.d1[1:128:16, :])])
-    dma("Y", "t1", "d2", "wina", [(T.wina[2:128:16, :], T.d2[2:128:16, :])])
-    for i, k in enumerate((5, 0, 1, 4, 6)):
-        do("S", "zz rm%d" % k, "wt%d" % i,
-           lambda i=i, k=k: S.activation(T.wtile[:, 512 * i:512 * i + 512], T.zz[:, :], AF.Identity, bias=T.rmk[:, k:k + 1]))
-    for nm, n in (("ha", 520), ("hc", 520), ("h2", 520), ("h3", 1032), ("ht", 520)):
-        for a in range(0, n, 512):
-            b = min(n, a + 512)
-            do("S", "zz", nm + "z%d" % (a // 512), lambda nm=nm, a=a, b=b: S.activation(T[nm][:, a:b], T.zz[:, 0:b - a], AF.Copy))
-    ts("V", "b8 g16", "dg", T.dg[:, :], T.b8[:, :], g16, None, op.is_equal)
-    ts("V", "jm p16", "m1", T.m1[:, :], T.jm[:, :], p16, None, op.is_equal)
-    ts("V", "jm", "hold", T.hold[:, :], T.jm[:, :], 0.0, None, op.is_gt)
+    iota("jt", T.jt[:, :], [[0, 32], [-1, 4], [1, 4]])
+    iota("wina", T.wina[:, :], [[0, 32], [1, 16]])
+    iota("d1", T.d1[:, :], [[0, 2], [16, 16], [0, 16]])
+    iota("d2", T.d2[:, :], [[256, 2], [0, 256]])
+    for i, k in ((1, 0), (2, 1), (3, 4), (4, 6)):
+        act("zz rm%d" % k, "wt%d" % i, T.wtile[:, 512 * i:512 * i + 512], T.zz[:, :], AF.Identity, bias=T.rmk[:, k:k + 1])
+    for nm, a, b in (("wt5", 2560, 3072), ("wt6", 3072, 3584)):
+        act("zz", nm, T.wtile[:, a:b], T.zz[:, 0:b - a], AF.Copy)
+    for nm in ("ha", "hf", "hc", "hl", "ht"):
+        act("zz", nm + "z", T[nm][:, 0:512], T.zz[:, 0:512], AF.Copy)
+    act("zz", "htz1", T.ht[:, 512:520], T.zz[:, 0:8], AF.Copy)
+    ts("b8 g16", "dg", T.dg[:, :], T.b8[:, :], g16, None, op.is_equal)
+    ts("jw p4", "m1", T.m1[:, :], T.jw[:, :], p4, None, op.is_equal)
+    ts("jw", "hold", T.hold[:, :], T.jw[:, :], 0.0, None, op.is_gt)
+    ts("jf pf0", "idn", T.idn[:, :], T.jf[:, :], pf, None, op.is_equal)
     fill("et", T.et[:, :], 0.0)
     for b in range(4):
-        ts("V", "jf pf0 et", "et%d" % b, T.et[:, 512 * b + b:512 * b + 512:4], T.jf[:, :], pf, 0.5, op.is_equal, op.mult)
-    do("V", "et et0 et1 et2 et3", "ec ecs", lambda: V.quantize_mx(T.ec[:, :], T.ecs[:, :], T.et[:, :]))
-    do("V", "wt0 wt1 wt2 wt3", "wc wcs", lambda: V.quantize_mx(T.wc[:, 0:512], T.wcs[:, 0:512], T.wtile[:, 0:2048]))
-    do("V", "wt4", "wc4 wcs4", lambda: V.quantize_mx(T.wc[:, 512:640], T.wcs[:, 512:640], T.wtile[:, 2048:2560]))
-    for nm, n in (("ha", 520), ("hc", 520), ("h2", 520), ("h3", 1032)):
-        do("V", "xt %sz%d" % (nm, (n - 1) // 512), nm + "x", lambda nm=nm, n=n: V.tensor_copy(T[nm][:, n - 8:n], T.xt[:, 0:8]))
+        ts("idn et", "et%d" % b, T.et[:, 512 * b + b:512 * b + 512:4], T.idn[:, :], 0.5, None, op.mult)
+    quant("et et0 et1 et2 et3", "ec ecs", T.ec[:, :], T.ecs[:, :], T.et[:, :])
+    ts("jf pf0", "tri", T.tri[:, :], T.jf[:, :], pf, None, op.is_lt)
+    for k in range(4):
+        ts("p16", "kb%d" % k, T.kb[:, k:k + 1], p16, 16.0 * (k % 2) + 0.5, None, op.add)
+    fill("kb4", T.kb[:, 4:5], E + 0.5)
+    ts("pf0", "old", T.kb[:, 5:6], pf, float(QO), None, op.add)
+    ts("pf0", "nold", T.kb[:, 6:7], pf, -1.0, -float(QO), op.mult, op.add)
+    for e in range(2):
+        ts("pf0", "cp%d" % e, T.cc[:, e:e + 1], pf, 128.0 * e + 1, None, op.add)
+        ts("pf0", "cl%d" % e, T.cc[:, 2 + e:3 + e], pf, 128.0 * e, None, op.add)
+        ts("pf0", "cd%d" % e, T.cc[:, 4 + e:5 + e], pf, -1.0, 320.0 - 128.0 * e, op.mult, op.add)
     for i, (nm, val) in enumerate((("winc", lambda s: float(s == lo)), ("tc1", lambda s: float(s == hi)),
                                    ("tc2", lambda s: 256.0 * (N - s)), ("tc3", lambda s: 32.0 * order.index(s)))):
         fill(nm + "z", T[nm][:, 0:256], 0.0)
@@ -304,38 +312,50 @@ def rank_program(g, core, T, topo):
                 do("V", nm + "z", nm + "_%d" % s,
                    lambda nm=nm, s=s, val=val: V.memset(T[nm][:, 2 ** (N - 1 - s):2 ** (N - s)], val(s)))
     keys = lambda nm: " ".join([nm + "z"] + [nm + "_%d" % s for s in range(N)])
-    for k in (1, 2, 3):
-        dma("Y", "t%d" % (k + 1), keys("tc%d" % k) + " " + keys("winc"), "wincr%d" % k,
-            [(T.winc[k:128:16, :], T["tc%d" % k][k:128:16, :])])
-    WINC = keys("winc") + " wincr1 wincr2 wincr3"
     for i in range(N):
         fill("vd%d" % i, T.vd[:, i:i + 1], 256.0 * (N - order[i]) + 32.0 * i)
         fill("wd%d" % i, T.wd[:, i:i + 1], weight[i - 1] / weight[i] if i else 1.0)
     VD, WD = " ".join("vd%d" % i for i in range(N)), " ".join("wd%d" % i for i in range(N))
-    ts("V", "jf pf0", "tri", T.tri[:, :], T.jf[:, :], pf, None, op.is_lt)
-    for k in range(4):
-        ts("V", "p16", "kb%d" % k, T.kb[:, k:k + 1], p16, 16.0 * (k % 2) + 0.5, None, op.add)
-    fill("kb4", T.kb[:, 4:5], E + 0.5)
-    ts("V", "pf0", "old", T.kb[:, 5:6], pf, float(QO), None, op.add)
-    ts("V", "pf0", "nold", T.kb[:, 6:7], pf, -1.0, -float(QO), op.mult, op.add)
-    for e in range(2):
-        ts("V", "pf0", "cp%d" % e, T.cc[:, e:e + 1], pf, 128.0 * e + 1, None, op.add)
-        ts("V", "pf0", "cl%d" % e, T.cc[:, 2 + e:3 + e], pf, 128.0 * e, None, op.add)
-        ts("V", "pf0", "cd%d" % e, T.cc[:, 4 + e:5 + e], pf, -1.0, 384.0 - 128.0 * e, op.mult, op.add)
-    do("V", "wt", "wq wqs", lambda: V.quantize_mx(T.wq[:, :], T.wqs[:, :], T.wt[:, :]))
+    ts("jt rm5", "wt0", T.wtile[:, 0:512], T.jt[:, :], 0.0, T.rmk[:, 5:6], op.is_equal, op.mult)
+    ts("jm p16 wt5", "wt5a", T.wtile[:, 2560:3072:4], T.jm[:, :], p16, 16.0, op.is_equal, op.mult)
+    ts("jm p16 wt5", "wt5b", T.wtile[:, 2561:3072:4], T.jm[:, :], p16, None, op.is_equal)
+    ts("zz wt6", "wt6a", T.wtile[:, 3072:3584:4], T.zz[:, 0:128], 16.0, None, op.add)
+    ts("zz wt6", "wt6b", T.wtile[:, 3073:3584:4], T.zz[:, 0:128], 1.0, None, op.add)
+    quant("wt0 wt1 wt2 wt3", "wc wcs", T.wc[:, 0:512], T.wcs[:, 0:512], T.wtile[:, 0:2048])
+    quant("wt4 wt5 wt6 wt5a wt5b wt6a wt6b", "wc4 wcs4", T.wc[:, 512:896], T.wcs[:, 512:896], T.wtile[:, 2048:3584])
+    cp("xt", "hcx", T.hc[:, 512:520], T.xt[:, 0:8])
+    cp("xt hlz", "hlx", T.hl[:, 504:512], T.xt[:, 0:8])
+    quant("wt", "wq wqs", T.wq[:, :], T.wqs[:, :], T.wt[:, :])
+    dma("Y", "t0", "d1", "wina", T.wina[1:128:16, :], T.d1[1:128:16, :])
+    dma("Y", "t1", "d2", "wina", T.wina[2:128:16, :], T.d2[2:128:16, :])
+    for k in (1, 2, 3):
+        dma("Y", "t%d" % (k + 1), keys("tc%d" % k) + " " + keys("winc"), "wincr%d" % k,
+            T.winc[k:128:16, :], T["tc%d" % k][k:128:16, :])
+    WINC = keys("winc") + " wincr1 wincr2 wincr3"
 
-    def rows(off, ro, n, h_, hk, hcod, hsc, win, wk):
-        do("V", "%s %sz0 %sx %s" % (ro, hk, hk, wk), hk + "g",
-           lambda: V.tensor_copy(h_[:, 0:4 * n:4], win.indirect(off)))
-        do("V", "%sg %sz0 %sx" % (hk, hk, hk) + (" h3z1 h3z2" if n > 128 else ""), hk + "c",
-           lambda: V.quantize_mx(hcod[:, 0:n + 2], hsc[:, 0:n + 2], h_[:, 0:4 * n + 8]))
+    def W(i):
+        return T.wc[:, 128 * i:128 * i + 128], T.wcs[:, 128 * i:128 * i + 128]
 
-    def wrap(k, n, out, wo):
-        do("V", "#%d m1" % k, "w1", lambda: V.tensor_tensor_scan(T.w1[:, 0:n], bank(k, n), T.m1[:, 0:n], 0.0, op.add, op.mult))
-        do("V", "w1 hold", "w2", lambda: V.tensor_tensor_scan(T.w2[:, 0:n], T.hold[:, 0:n], T.w1[:, 0:n], 0.0, op.mult, op.add))
-        do("V", "w2", wo, lambda: V.tensor_copy(out, T.w2[:, 15:n:16]))
+    def both(nm):
+        return "%s %ss" % (nm, nm)
 
-    W3 = (T.wc[:, 0:128], T.wcs[:, 0:128])
+    def wi_steps(rounds):
+        nums = {0: (T.lm1, "lmn1 lmz1 lma1"), 1: (T.nl, "nlo nlz nla")}
+        for t in rounds:
+            ts(VD + " v%d" % t, "oh%d" % t, T.oh[:, 8 * t:8 * t + 8], T.vd[:, :], T.vv[:, t:t + 1], None, op.is_equal)
+        for t in rounds:
+            tt("oh%d %s" % (t, nums[t][1]), "oh%d" % t, T.oh[:, 8 * t:8 * t + 8], T.oh[:, 8 * t:8 * t + 8], nums[t][0][:, 1:16:2], op.mult)
+        for t in rounds:
+            red("oh%d" % t, "wg%d" % t, T.wv[:, t:t + 1], T.oh[:, 8 * t:8 * t + 8], op.add)
+        for t in rounds:
+            ts("wg%d" % t, "wh%d" % t, T.wv[:, 2 + t:3 + t], T.wv[:, t:t + 1], 2.0, 1.0, op.mult, op.add)
+        for t in rounds:
+            ts("wh%d an%d" % (t, t), "wk%d" % t, T.wv[:, 4 + t:5 + t], T.wv[:, 2 + t:3 + t], T.an[:, t:t + 1], None, op.mult)
+        for t in rounds:
+            ts("wk%d wg%d" % (t, t), "wo%d" % t, T.wo[:, t:t + 1], T.wv[:, 4 + t:5 + t], T.wv[:, t:t + 1], 1.0, op.subtract, op.subtract)
+        for t in rounds:
+            dma("Y", "u%d" % (5 + t), "wo%d" % t, "out%d" % (5 + t), T.wi[t:t + 1, :], T.wo[:, t:t + 1])
+
     for t in range(2):
         ld, lds = T["ld%d" % t], T["ld%ds" % t]
         mc, mcs = T["mc%d" % t], T["mc%ds" % t]
@@ -347,139 +367,135 @@ def rank_program(g, core, T, topo):
         MEMS = "mcown%ds mcfar%ds" % (t, t)
         mm(0, 256, q, qs, mc[:, 0:256], mcs[:, 0:256], Q + " " + MEM + " " + MEMS)
         for e in range(2):
-            do("V", "#0", "lmo%d" % t if e == 0 else "lmp%d" % t,
-               lambda e=e: V.tensor_reduce(lm[:, 4 * h + 2 * e:4 * h + 2 * e + 1], T.ps[:, 128 * e:128 * e + 128], X, op.max))
-        spread("m%d" % t, "lmo%d lmp%d" % (t, t), lm[:, 4 * h:4 * h + 4], lm[:, 4 * h:4 * h + 4])
-        arrive("m%d" % t, len(off_mates) * foff + len(on_mates) * len(eon), "lma%d" % t)
+            red("#0 lmz%d" % t, "lmo%d%d" % (t, e), lm[:, 4 * h + 2 * e:4 * h + 2 * e + 1], T.ps[:, 128 * e:128 * e + 128], op.max)
+        OWN = "lmz%d lmo%d0 lmo%d1" % (t, t, t) + (" lmn1" if t else "")
+        spread("m%d" % t, OWN, lm[:, 4 * h:4 * h + 4], lm[:, 4 * h:4 * h + 4])
+        arrive("m%d" % t, from_mates, "lma%d" % t)
         for b in range(4):
             mm(1 + b, 128, T.ec[:, 128 * b:128 * b + 128], T.ecs[:, 128 * b:128 * b + 128], q, qs, "ec ecs " + Q, True, False)
-        do("V", "#0 zz", "cm", lambda: V.tensor_tensor_scan(T.cm[:, :], T.ps[:, 0:256], T.zz[:, 0:256], -1e29, op.max, op.add))
-        a = T.aa[:, t:t + 1]
-        do("S", "cm", "jk a%d" % t, lambda: S.activation(T.jk[:, :], T.cm[:, :], AF.Sign, bias=T.cm[:, 255:256], scale=-1.0, accum_out=a))
-        ts("V", "dg a%d" % t, "oa", T.oa[:, :], T.dg[:, :], a, None, op.mult)
-        rows(T.oa[:, 0:8], "oa", 128, T.ha, "ha", T.hac, T.has, T.wina[:, :], "wina")
-        mm(7, 130, W3[0], W3[1], T.hac[:, 0:130], T.has[:, 0:130], "wc wcs hac")
-        wrap(7, 128, T.oaw[:, :], "oaw")
-        do("S", "#7", "fra", lambda: S.activation(T.fra[:, :], bank(7, 128), AF.Identity, bias=1.0))
+        scan("#0 zz", "cm", T.cm[:, :], T.ps[:, 0:256], T.zz[:, 0:256], -1e29, op.max, op.add)
+        a, hi16, low = T.aa[:, t:t + 1], T.aa[:, 2 + t:3 + t], T.lw[:, t:t + 1]
+        act("cm", "jk ah%d" % t, T.jk[:, 0:16], T.cm[:, 15:256:16], AF.Sign, bias=T.cm[:, 255:256], scale=-1.0, accum=hi16)
+        act("cm", "jk a%d" % t, T.jk[:, :], T.cm[:, :], AF.Sign, bias=T.cm[:, 255:256], scale=-1.0, accum=a)
+        ts("dg haz ah%d" % t, "hah", T.ha[:, 0:32:4], T.dg[:, :], hi16, None, op.mult)
+        ts("ah%d a%d" % (t, t), "low%d" % t, low, hi16, -16.0, a, op.mult, op.add)
+        ts("idn hfz ah%d" % t, "hfh", T.hf[:, 0:512:4], T.idn[:, :], hi16, None, op.mult)
+        ts("dg haz low%d" % t, "hal", T.ha[:, 1:32:4], T.dg[:, :], low, None, op.mult)
+        ts("idn hfz low%d" % t, "hfl", T.hf[:, 1:512:4], T.idn[:, :], low, None, op.mult)
+        quant("haz hah hal", both("hac"), T.hac[:, :], T.hacs[:, :], T.ha[:, :])
+        mm(7, 128, *W(5), T.hac[:, :], T.hacs[:, :], "wc4 wcs4 " + both("hac"))
+        ts("a%d" % t, "nm0", T.nm[:, 0:1], a, 128.0, 128.0 * (hi - 1 - lo), op.is_ge, op.mult)
+        quant("hfz hfh hfl", both("hfc"), T.hfc[:, :], T.hfcs[:, :], T.hf[:, :])
+        cp("#7", "oaw", T.oaw[:, :], bank(7, 8))
         pick(mp[:, :], mps[:, :], mc[:, 0:256], mcs[:, 0:256], T.oaw[:, 0:8], MEM, MEMS, "mp%d" % t, "mp%ds" % t, "oaw")
+        nt, nk = ((T.lm1, "lmn1"), (T.nl, "nlo"))[t]
+        ts("nm0 a%d" % t, "nm1", T.nm[:, 1:2], a, T.nm[:, 0:1], 128.0 * lo, op.add, op.add)
+        for c in (1, 3):
+            cp("nm1 lmz1 nlz", nk, nt[:, 4 * h + c:4 * h + c + 1], T.nm[:, 1:2])
+        mm(7, 128, *W(6), T.hfc[:, :], T.hfcs[:, :], "wc4 wcs4 " + both("hfc"))
         for b in range(4):
             mm(1 + b, 128, T.ec[:, 128 * b:128 * b + 128], T.ecs[:, 128 * b:128 * b + 128], mp[:, :], mps[:, :],
                "ec ecs mp%d mp%ds" % (t, t), False, True)
         for b in range(4):
             if b % 2 == 0:
-                do("V", "#%d htz0" % (1 + b), "ht%d" % b, lambda b=b: V.tensor_copy(T.ht[:, b:512:4], bank(1 + b, 128)))
+                cp("#%d htz" % (1 + b), "ht%d" % b, T.ht[:, b:512:4], bank(1 + b))
             else:
-                do("S", "#%d htz0" % (1 + b), "ht%d" % b, lambda b=b: S.activation(T.ht[:, b:512:4], bank(1 + b, 128), AF.Copy))
-        do("V", "ht0 ht1 ht2 ht3 htz0 htz1", "cand%d cand%ds" % (t, t),
-           lambda: V.quantize_mx(mc[:, 256:386], mcs[:, 256:386], T.ht[:, :]))
-        ts("V", "a%d" % t, "wv0", T.wv[:, 0:1], a, 128.0, 128.0 * (hi - 1 - lo), op.is_ge, op.mult)
-        for c in (t, t + 2):
-            ts("V", "wv0 a%d" % t, "nlo%d" % c, T.nl[:, 4 * h + c:4 * h + c + 1], a, T.wv[:, 0:1], 128.0 * lo, op.add, op.add)
-        if t == 1:
-            spread("nn", "nlo0 nlo1 nlo2 nlo3", T.nl[:, 4 * h:4 * h + 4], T.nl[:, 4 * h:4 * h + 4])
-            arrive("nn", len(off_mates) * foff + len(on_mates) * len(eon), "nla")
-        LM = "lmo%d lmp%d lma%d" % (t, t, t)
-        do("V", LM, "mx", lambda: V.tensor_reduce(T.mx[:, :], lm[:, 0:16:2], X, op.max))
-        ts("V", LM + " mx", "eq", T.eq[:, :], lm[:, 0:16:2], T.mx[:, 0:1], None, op.is_equal)
-        do("V", "eq " + WD, "sc", lambda: V.tensor_tensor_scan(T.sc[:, :], T.wd[:, :], T.eq[:, :], 0.0, op.mult, op.add))
-        ts("V", "dg sc", "oc8", T.oc8[:, :], T.dg[:, :], T.sc[:, 7:8], None, op.mult)
-        rows(T.oc8[:, 0:8], "oc8", 128, T.hc, "hc", T.hcc, T.hcs, T.winc[:, :], WINC)
+                act("#%d htz" % (1 + b), "ht%d" % b, T.ht[:, b:512:4], bank(1 + b), AF.Copy)
+        act("#7", "fra", T.fra[:, :], bank(7), AF.Identity, bias=1.0)
+        quant("ht0 ht1 ht2 ht3 htz htz1", "cand%d cand%ds" % (t, t), mc[:, 256:386], mcs[:, 256:386], T.ht[:, :])
+        LM = OWN + " lma%d" % t
+        red(LM, "mx", T.mx[:, :], lm[:, 0:16:2], op.max)
+        ts(LM + " mx", "eq", T.eq[:, :], lm[:, 0:16:2], T.mx[:, 0:1], None, op.is_equal)
+        scan("eq " + WD, "sc", T.sc[:, :], T.wd[:, :], T.eq[:, :], 0.0, op.mult, op.add)
+        tt("eq " + VD, "pv", T.pv[:, :], T.eq[:, :], T.vd[:, :], op.mult)
+        ts("dg sc", "oc8", T.oc8[:, :], T.dg[:, :], T.sc[:, 7:8], None, op.mult)
+        v, an = T.vv[:, t:t + 1], T.an[:, t:t + 1]
+        red("pv", "v%d" % t, v, T.pv[:, :], op.max)
+        cp("oc8 hcz hcx " + WINC, "hcg", T.hc[:, 0:512:4], T.winc[:, :].indirect(T.oc8[:, 0:8]))
+        cp("v%d" % t, "bi0", T.bi[:, 0:1], v)
+        quant("hcg hcz hcx", both("hcc"), T.hcc[:, 0:130], T.hccs[:, 0:130], T.hc[:, :])
         for k, i in ((5, 1), (6, 2), (0, 4), (7, 3)):
-            mm(k, 130, T.wc[:, 128 * i:128 * i + 128], T.wcs[:, 128 * i:128 * i + 128], T.hcc[:, 0:130], T.hcs[:, 0:130],
-               "wc wcs wc4 wcs4 hcc")
-        do("V", "#5 zz", "clo", lambda: V.tensor_tensor_scan(T.clo[:, :], bank(5, 128), T.zz[:, 0:128], 0.0, op.add, op.add))
-        do("V", "#6 zz", "chi", lambda: V.tensor_tensor_scan(T.chi[:, :], bank(6, 128), T.zz[:, 0:128], 0.0, op.add, op.add))
+            mm(k, 130, *W(i), T.hcc[:, 0:130], T.hccs[:, 0:130], "wc wcs wc4 wcs4 " + both("hcc"))
+        ts("tri v%d" % t, "triv", T.triv[:, :], T.tri[:, :], v, None, op.mult)
+        ts("bi0", "bi1", T.bi[:, 1:2], T.bi[:, 0:1], 255, None, op.bitwise_and)
+        scan("#5 zz", "clo", T.clo[:, :], bank(5), T.zz[:, 0:128], 0.0, op.add, op.add)
+        scan("#6 zz", "chi", T.chi[:, :], bank(6), T.zz[:, 0:128], 0.0, op.add, op.add)
         for c, src, nm in ((0, T.clo, "clo"), (1, T.clo, "clo"), (2, T.chi, "chi")):
-            do("S", "%s kb%d" % (nm, c), "jk acc%d" % c,
-               lambda c=c, src=src: S.activation(T.jk[:, 0:128], src[:, :], AF.Sign, bias=T.kb[:, c:c + 1], scale=-1.0,
-                                                 accum_out=T.acc[:, c:c + 1]))
-        ts("V", "chi kb3", "le", T.le[:, :], T.chi[:, :], T.kb[:, 3:4], None, op.is_le)
-        do("V", "le", "acv", lambda: V.tensor_reduce(T.acv[:, :], T.le[:, :], X, op.add))
-        do("V", "acv", "os3", lambda: V.tensor_copy(T.oslot[:, 3:4], T.acv[:, :]))
-        ts("V", "acc0 acc1 acc2", "os0", T.oslot[:, 0:3], T.acc[:, 0:3], 0.5, 64.0, op.mult, op.add)
+            act("%s kb%d" % (nm, c), "jk acc%d" % c, T.jk[:, 0:128], src[:, :], AF.Sign, bias=T.kb[:, c:c + 1], scale=-1.0,
+                accum=T.acc[:, c:c + 1])
+        tt("#0 triv", "eqt", T.eqt[:, :], bank(0), T.triv[:, :], op.is_equal)
+        ts("chi kb3", "le", T.le[:, :], T.chi[:, :], T.kb[:, 3:4], None, op.is_le)
+        tt("#7 fra", "tg", T.tg[:, :], bank(7), T.fra[:, :], op.mult)
+        red("le", "acv", T.acv[:, :], T.le[:, :], op.add)
+        cp("bi1", "kk1", T.kk[:, 1:2], T.bi[:, 1:2])
+        cp("acv", "os3", T.oslot[:, 3:4], T.acv[:, :])
+        ts("acc0 acc1 acc2", "os0", T.oslot[:, 0:3], T.acc[:, 0:3], 0.5, 64.0, op.mult, op.add)
         pick(ld[:, 64 * h:64 * h + 64], lds[:, 64 * h:64 * h + 64], mc[:, 256:386], mcs[:, 256:386], T.oslot[:, 0:4],
              "cand%d" % t, "cand%ds" % t, "slot%d" % t, "slot%ds" % t, "os0 os3")
         spread("c%d" % t, "slot%d" % t, ld[:, 64 * h:64 * h + 64].bitcast(dt.uint8), ld[:, 64 * h:64 * h + 64].bitcast(dt.uint8))
         spread("c%d" % t, "slot%ds" % t, lds[:, 64 * h:64 * h + 64], lds[:, 64 * h:64 * h + 64])
-        arrive("c%d" % t, 2 * (len(off_mates) * foff + len(on_mates) * len(eon)), "land%d land%ds" % (t, t))
-        for c, src, nm in ((0, T.clo, "clo"), (1, T.chi, "chi")):
-            do("S", "%s kb4" % nm, "jk ta%d" % c,
-               lambda c=c, src=src: S.activation(T.jk[:, 0:128], src[:, :], AF.Sign, bias=T.kb[:, 4:5], scale=-1.0,
-                                                 accum_out=T.ta[:, c:c + 1]))
-        v, an = T.vv[:, t:t + 1], T.an[:, t:t + 1]
-        do("V", "eq " + VD, "pv", lambda: V.tensor_tensor(T.pv[:, :], T.eq[:, :], T.vd[:, :], op.mult))
-        do("V", "pv", "v%d" % t, lambda: V.tensor_reduce(v, T.pv[:, :], X, op.max))
-        ts("V", "#0 v%d" % t, "same", T.same[:, :], bank(0, 128), v, None, op.is_equal)
-        do("V", "same tri", "sc2", lambda: V.tensor_tensor_scan(T.sc2[:, :], T.same[:, :], T.tri[:, :], 0.0, op.add, op.mult))
-        do("V", "v%d" % t, "bi0", lambda: V.tensor_copy(T.bi[:, 0:1], v))
-        do("V", "sc2", "kk0", lambda: V.tensor_reduce(T.kk[:, 0:1], T.sc2[:, :], X, op.max))
-        ts("V", "bi0", "bi1", T.bi[:, 1:2], T.bi[:, 0:1], 255, None, op.bitwise_and)
-        ts("V", "kk0", "an%d" % t, an, T.kk[:, 0:1], float(E), None, op.is_lt)
-        do("V", "bi1", "kk1", lambda: V.tensor_copy(T.kk[:, 1:2], T.bi[:, 1:2]))
-        ts("V", "kk0 kk1 nold", "kk2", T.kk[:, 2:3], T.kk[:, 0:1], T.kk[:, 1:2], T.kb[:, 6:7], op.add, op.add)
-        ts("V", "kk2 an%d old" % t, "kk3", T.kk[:, 3:4], T.kk[:, 2:3], an, T.kb[:, 5:6], op.mult, op.add)
-        ts("V", "dg kk3", "o2", T.o2[:, :], T.dg[:, :], T.kk[:, 3:4], None, op.mult)
-        rows(T.o2[:, 0:8], "o2", 128, T.h2, "h2", T.h2c, T.h2s, T.wina[:, :], "wina")
-        mm(1, 130, W3[0], W3[1], T.h2c[:, 0:130], T.h2s[:, 0:130], "wc wcs h2c")
-        do("V", "#7 fra", "tg", lambda: V.tensor_tensor(T.tg[:, :], bank(7, 128), T.fra[:, :], op.mult))
+        arrive("c%d" % t, 2 * from_mates, "land%d land%ds" % (t, t))
+        if t == 1:
+            spread("nn", "nlo nlz", T.nl[:, 4 * h:4 * h + 4], T.nl[:, 4 * h:4 * h + 4])
+            arrive("nn", from_mates, "nla")
         halves = (0, 1) if t == 0 else (own,)
+        for e, (src, nm) in enumerate(((T.clo, "clo"), (T.chi, "chi"))):
+            if e in halves:
+                act("%s kb4" % nm, "jk ta%d" % e, T.jk[:, 0:128], src[:, :], AF.Sign, bias=T.kb[:, 4:5], scale=-1.0,
+                    accum=T.ta[:, e:e + 1])
         for e in halves:
-            ts("V", "tg cp%d" % e, "ep%d" % e, T.ep[:, 128 * e:128 * e + 128], T.tg[:, :], T.cc[:, e:e + 1], None, op.is_equal)
+            ts("tg cp%d" % e, "ep%d" % e, T.ep[:, 128 * e:128 * e + 128], T.tg[:, :], T.cc[:, e:e + 1], None, op.is_equal)
+        red("eqt", "kk0", T.kk[:, 0:1], T.eqt[:, :], op.add)
         for e in halves:
-            do("V", "ep%d zz" % e, "co%d" % e,
-               lambda e=e: V.tensor_tensor_scan(T.co[:, 128 * e:128 * e + 128], T.ep[:, 128 * e:128 * e + 128], T.zz[:, 0:128],
-                                                0.0, op.max, op.add))
+            scan("ep%d zz" % e, "co%d" % e, T.co[:, 128 * e:128 * e + 128], T.ep[:, 128 * e:128 * e + 128], T.zz[:, 0:128],
+                 0.0, op.max, op.add)
+            act("co%d" % e, "jk un%d" % e, T.jk[:, 0:128], T.co[:, 128 * e:128 * e + 128], AF.Identity, bias=1.0, scale=-2.0,
+                accum=T.un[:, e:e + 1])
+        ts("kk0", "an%d" % t, an, T.kk[:, 0:1], float(E), None, op.is_lt)
+        ts("kk0 kk1 nold", "kk2", T.kk[:, 2:3], T.kk[:, 0:1], T.kk[:, 1:2], T.kb[:, 6:7], op.add, op.add)
+        ts("kk2 an%d old" % t, "kk3", T.kk[:, 3:4], T.kk[:, 2:3], an, T.kb[:, 5:6], op.mult, op.add)
+        ts("dg kk3", "o2", T.o2[:, :], T.dg[:, :], T.kk[:, 3:4], None, op.mult)
         for e in halves:
-            do("V", "co%d" % e, "jc%d" % e, lambda e=e: V.tensor_reduce(T.jc[:, e:e + 1], T.co[:, 128 * e:128 * e + 128], X, op.add))
-        wrap(1, 128, T.oq[:, :], "oq")
-        c0, c1 = halves[0], halves[-1] + 1
-        ks = lambda nm: " ".join(nm + "%d" % e for e in halves)
-        ts("V", ks("jc"), "ju", T.jc[:, 2 + c0:2 + c1], T.jc[:, c0:c1], -2.0, 128.0, op.mult, op.add)
-        do("V", ks("jc") + " " + ks("cd"), "jd", lambda: V.tensor_tensor(T.jc[:, 4 + c0:4 + c1], T.cc[:, 4 + c0:4 + c1], T.jc[:, c0:c1], op.subtract))
-        do("V", "ju " + ks("ta"), "jg", lambda: V.tensor_tensor(T.jc[:, 6 + c0:6 + c1], T.jc[:, 2 + c0:2 + c1], T.ta[:, c0:c1], op.is_lt))
-        do("V", "jd jg", "jh", lambda: V.tensor_tensor(T.wv[:, 4 + c0:4 + c1], T.jc[:, 4 + c0:4 + c1], T.jc[:, 6 + c0:6 + c1], op.mult))
-        do("V", "jh " + ks("cl"), "l3", lambda: V.tensor_tensor(T.wv[:, 6 + c0:6 + c1], T.wv[:, 4 + c0:4 + c1], T.cc[:, 2 + c0:2 + c1], op.add))
-        n3 = 128 * len(halves)
+            tt("un%d ta%d" % (e, e), "jg%d" % e, T.jg[:, e:e + 1], T.un[:, e:e + 1], T.ta[:, e:e + 1], op.is_lt)
+            ts("un%d cd%d" % (e, e), "jd%d" % e, T.jd[:, e:e + 1], T.un[:, e:e + 1], 0.5, T.cc[:, 4 + e:5 + e], op.mult, op.add)
+        for e in halves:
+            ts("jd%d jg%d cl%d" % (e, e, e), "l3%d" % e, T.l3[:, e:e + 1], T.jd[:, e:e + 1], T.jg[:, e:e + 1], T.cc[:, 2 + e:3 + e],
+               op.mult, op.add)
+        cp("o2 wina hlz", "hl0", T.hl[:, 0:128], T.wina[:, :].indirect(T.o2[:, 0:8]))
         for i, e in enumerate(halves):
-            ts("V", "dg l3", "o3_%d" % i, T.o3[:, 8 * i:8 * i + 8], T.dg[:, :], T.wv[:, 6 + e:7 + e], None, op.mult)
-        o3k = " ".join("o3_%d" % i for i in range(len(halves)))
+            ts("dg l3%d" % e, "o3%d" % i, T.o3[:, 8 * i:8 * i + 8], T.dg[:, :], T.l3[:, e:e + 1], None, op.mult)
+        cp("o30 wina hlz", "hl1", T.hl[:, 128:256], T.wina[:, :].indirect(T.o3[:, 0:8]))
         if t == 0:
-            rows(T.o3[:, 0:16], o3k, 256, T.h3, "h3", T.h3c, T.h3s, T.wina[:, :], "wina")
-            mm(2, 258, W3[0], W3[1], T.h3c[:, 0:258], T.h3s[:, 0:258], "wc wcs h3c")
-            wrap(2, 256, T.om[:, :], "om")
-            pick(T.mc1[:, 0:256], T.mc1s[:, 0:256], mc[:, 0:386], mcs[:, 0:386], T.om[:, 0:16],
-                 MEM + " cand0", MEMS + " cand0s", "mcown1", "mcown1s", "om")
+            act("o31 wina hlz", "hl2", T.hl[:, 256:384], T.wina[:, :].indirect(T.o3[:, 8:16]), AF.Copy)
+        quant("hl0 hl1 hl2 hlz hlx", both("hlc"), T.hlc[:, :], T.hlcs[:, :], T.hl[:, :])
+        mm(1, 128, *W(0), T.hlc[:, :], T.hlcs[:, :], "wc wcs " + both("hlc"))
+        n = 96 if t == 0 else 64
+        scan("#1 m1", "w1", T.w1[:, 0:n], bank(1, n), T.m1[:, 0:n], 0.0, op.add, op.mult)
+        scan("w1 hold", "w2", T.w2[:, 0:n], T.hold[:, 0:n], T.w1[:, 0:n], 0.0, op.mult, op.add)
+        cp("w2", "ol", T.ol[:, 0:n // 4], T.w2[:, 3:n:4])
+        if t == 0:
+            pick(T.mc1[:, 0:256], T.mc1s[:, 0:256], mc[:, 0:386], mcs[:, 0:386], T.ol[:, 8:24],
+                 MEM + " cand0", MEMS + " cand0s", "mcown1", "mcown1s", "ol")
             note(("V", cnt["V"], "V", dict(known["V"])), [], ["mcfar1"])
             note(("S", cnt["S"], "S", dict(known["S"])), [], ["mcfar1s"])
-            pick(T.ld1[:, QO:QO + 128], T.ld1s[:, QO:QO + 128], ld[:, 0:384], lds[:, 0:384], T.oq[:, 0:8],
-                 "slot0 land0 qown0 qfar0", "slot0s land0s qown0s qfar0s", "qown1", "qown1s", "oq")
+            pick(T.ld1[:, QO:QO + 128], T.ld1s[:, QO:QO + 128], ld[:, 0:384], lds[:, 0:384], T.ol[:, 0:8],
+                 "slot0 land0 qown0 qfar0", "slot0s land0s qown0s qfar0s", "qown1", "qown1s", "ol")
             note(("V", cnt["V"], "V", dict(known["V"])), [], ["qfar1"])
             note(("S", cnt["S"], "S", dict(known["S"])), [], ["qfar1s"])
         else:
-            rows(T.o3[:, 0:8], o3k, 128, T.ha, "ha", T.hac, T.has, T.wina[:, :], "wina")
-            mm(2, 130, W3[0], W3[1], T.hac[:, 0:130], T.has[:, 0:130], "wc wcs hac")
-            wrap(2, 128, T.om[:, 0:8], "om")
-            pick(T.fm[:, :], T.fms[:, :], mc[:, 0:386], mcs[:, 0:386], T.om[:, 0:8],
-                 MEM + " cand1", MEMS + " cand1s", "fm", "fms", "om")
-            dma("Y", "u0", "fm", "out0", [(T.oc[:, :], T.fm[:, :].bitcast(dt.uint8))])
+            pick(T.fm[:, :], T.fms[:, :], mc[:, 0:386], mcs[:, 0:386], T.ol[:, 8:16],
+                 MEM + " cand1", MEMS + " cand1s", "fm", "fms", "ol")
+            dma("Y", "u0", "fm", "out0", T.oc[:, :], T.fm[:, :].bitcast(dt.uint8))
             for k in range(4):
-                dma("Y", "u%d" % (1 + k), "fms", "out%d" % (1 + k), [(T.osc[4 * k:4 * k + 4, :], T.fms[32 * k:32 * k + 4, :])])
+                dma("Y", "u%d" % (1 + k), "fms", "out%d" % (1 + k), T.osc[4 * k:4 * k + 4, :], T.fms[32 * k:32 * k + 4, :])
 
-    for t in range(2):
-        v, an = T.vv[:, t:t + 1], T.an[:, t:t + 1]
-        z = 8 * t
-        ts("V", VD + " v%d" % t, "pv", T.pv[:, :], T.vd[:, :], v, None, op.is_equal)
-        do("V", "pv nla nlo%d nlo%d" % (t, t + 2), "eq", lambda: V.tensor_tensor(T.eq[:, :], T.pv[:, :], T.nl[:, t:16:2], op.mult))
-        do("V", "eq", "wg", lambda: V.tensor_reduce(T.wv[:, 1:2], T.eq[:, :], X, op.add))
-        ts("V", "wg", "wh", T.wv[:, 2:3], T.wv[:, 1:2], 2.0, 1.0, op.mult, op.add)
-        ts("V", "wh an%d" % t, "wk", T.wv[:, 3:4], T.wv[:, 2:3], an, None, op.mult)
-        ts("V", "wk wg", "wo%d" % t, T.wo[:, t:t + 1], T.wv[:, 3:4], T.wv[:, 1:2], 1.0, op.subtract, op.subtract)
-        dma("Y", "u%d" % (5 + t), "wo%d" % t, "out%d" % (5 + t), [(T.wi[t:t + 1, :], T.wo[:, t:t + 1])])
-    pick(T.qf[:, :], T.qfs[:, :], T.ld1[:, 0:384], T.ld1s[:, 0:384], T.oq[:, 0:8],
-         "slot1 land1 qown1 qfar1", "slot1s land1s qown1s qfar1s", "qf", "qfs", "oq")
+    wi_steps((0,))
+    pick(T.qf[:, :], T.qfs[:, :], T.ld1[:, 0:384], T.ld1s[:, 0:384], T.ol[:, 0:8],
+         "slot1 land1 qown1 qfar1", "slot1s land1s qown1s qfar1s", "qf", "qfs", "ol")
     mm(3, 128, T.wq[:, :], T.wqs[:, :], T.qf[:, :], T.qfs[:, :], "wq wqs qf qfs")
-    do("V", "#3", "ysb", lambda: V.tensor_copy(T.ysb[:, :], bank(3, 128)))
-    dma("Y", "u7", "ysb", "outy", [(T.y[:, :], T.ysb[:, :])])
+    wi_steps((1,))
+    act("#3", "ysb", T.ysb[:, :], bank(3), AF.Copy)
+    dma("S", "u7", "ysb", "outy", T.y[:, :], T.ysb[:, :])
     for s, n in cnt.items():
         if known["G"].get(s, 0) < n:
             g.wait_ge(T.sem[s], n)

@@ -5,21 +5,22 @@ F8 = "float8_e4m3fn_x4"
 SCRATCH = {"ps": ("psum", [128, 4096], "float32")}
 for _n, _w in (("xq", 128), ("wq", 128), ("rx", 32), ("rm", 128), ("ld0", 384), ("ld1", 384), ("qf", 128), ("mc0", 416),
                ("mc1", 416), ("fm", 128), ("mp0", 128), ("mp1", 128), ("wc", 896), ("ec", 512), ("hac", 128), ("hfc", 128),
-               ("hcc", 136), ("hlc", 128)):
+               ("hcc", 136), ("hlc", 128), ("hmc", 128)):
     SCRATCH[_n] = ("sbuf", [128, _w], F8)
     SCRATCH[_n + "s"] = ("sbuf", [128, _w], "uint8")
-for _n, _w in (("xt", 512), ("mt", 512), ("wt", 512), ("ha", 512), ("hf", 512), ("hc", 520), ("hl", 512), ("ht", 520),
+for _n, _w in (("xt", 512), ("mt", 512), ("wt", 512), ("ha", 512), ("hf", 512), ("hc", 520), ("hl", 512), ("hm", 512), ("ht", 520),
                ("wtile", 3584), ("et", 2048), ("zz", 512), ("wina", 512), ("d1", 512), ("d2", 512), ("winc", 256), ("tc1", 256),
                ("tc2", 256), ("tc3", 256), ("tri", 128), ("m1", 96), ("hold", 96), ("jm", 128), ("jt", 512), ("jw", 96),
-               ("idn", 128), ("jk", 256), ("fra", 128), ("clo", 128), ("chi", 128), ("le", 128), ("eqt", 128), ("tg", 128),
+               ("idn", 128), ("jk", 5120), ("fra", 128), ("clo", 128), ("chi", 128), ("le", 128), ("eqt", 128), ("tg", 128),
                ("ep", 256), ("co", 256)):
     SCRATCH[_n] = ("sbuf", [128, _w], "bfloat16")
 for _n, _w in (("jf", 128), ("b8", 8), ("pf", 4), ("rmk", 8), ("dg", 8), ("kb", 8), ("cc", 8), ("vd", 8), ("wd", 8), ("lm0", 16),
-               ("lm1", 16), ("nl", 16), ("cm", 256), ("aa", 4), ("lw", 2), ("vv", 2), ("an", 2), ("w1", 96), ("w2", 96),
-               ("mx", 1), ("eq", 8), ("sc", 8), ("acc", 4), ("acv", 1), ("pv", 8), ("triv", 128), ("kk", 4), ("jc", 2),
-               ("ta", 2), ("jg", 2), ("jd", 2), ("l3", 2), ("un", 2), ("nm", 2), ("wv", 8), ("oh", 16), ("wo", 2), ("ysb", 128)):
+               ("lm1", 16), ("nl", 16), ("cm", 256), ("aa", 4), ("lw", 2), ("vv", 2), ("an", 2), ("w1", 128), ("w2", 128),
+               ("mx", 1), ("eq", 8), ("sc", 8), ("acc", 4), ("acv", 1), ("pv", 8), ("triv", 128), ("kk", 4),
+               ("ta", 2), ("jg", 2), ("jd", 2), ("l3", 2), ("un", 2), ("nm", 2), ("wv", 8), ("oh", 16), ("og", 16), ("wo", 2),
+               ("ysb", 128)):
     SCRATCH[_n] = ("sbuf", [128, _w], "float32")
-for _n, _w in (("ox", 2), ("oaw", 8), ("oc8", 8), ("oslot", 4), ("o2", 8), ("o3", 16), ("ol", 24)):
+for _n, _w in (("ox", 2), ("oaw", 8), ("oc8", 8), ("oslot", 4), ("o2", 8), ("o3", 16), ("ol", 24), ("om", 8)):
     SCRATCH[_n] = ("sbuf", [128, _w], "uint16")
 for _n, _w in (("pint", 4), ("bi", 2)):
     SCRATCH[_n] = ("sbuf", [128, _w], "int32")
@@ -28,6 +29,9 @@ SEMAPHORES = ["V", "S", "P", "G", "ls", "xa", "ma", "mr", "ms", "m0", "m1", "nn"
 A = 16
 E = 32
 QO = 256
+WAKE = 0.2
+DMA, CALL = 1.8, 0.5
+HOP = {"xa": 6.0, "ma": 7.0, "m0": 1.6, "m1": 1.6, "nn": 1.6, "c0": 2.4, "c1": 2.4}
 
 
 def plan(T, topo):
@@ -83,15 +87,83 @@ def relay(g, core, T, topo, pl):
     for r in here:
         p = partner[r]
         h = 128 if r > p else 0
-        off, every = topo.engines(core, cores[p]), topo.engines(core, cores[r])
+        off = topo.engines(core, cores[p])
+        on = [e for e in topo.engines(core, cores[r]) if e not in off]
         if core == mrel[r][0]:
-            g.wait_ge(T.sem.mr, len(every))
+            g.wait_ge(T.sem.mr, len(on))
             send("ma", [(T.rm[:].bitcast(dt.uint8), [(cores[p], T.mc0[:, h:h + 128].bitcast(dt.uint8))], off)])
         if core == mrel[r][1]:
-            g.wait_ge(T.sem.ms, len(every))
+            g.wait_ge(T.sem.ms, len(on))
             send("ma", [(T.rms[:], [(cores[p], T.mc0s[:, h:h + 128])], off)])
     if n[0]:
         g.wait_ge(T.sem.ls, n[0])
+
+
+def conflicts(q, r, w, wr, rd, acc, strict):
+    d = []
+    for k in r:
+        d += wr.get(k, [])
+        if k[0] == "#":
+            d += [e for e in rd.get(k, []) if e[2] != q]
+    for k in w:
+        d += [e for e in wr.get(k, []) if strict or not (acc and e[2] == q)]
+        d += [e for e in rd.get(k, []) if strict or e[2] != q]
+    return d
+
+
+def note(e, r, w, wr, rd):
+    for k in w:
+        wr[k], rd[k] = [e], []
+    for k in r:
+        rd.setdefault(k, []).append(e)
+
+
+def in_order(ops):
+    n = len(ops)
+    wr, rd, pred = {}, {}, []
+    last = {}
+    for i, o in enumerate(ops):
+        p = {e[0] for e in conflicts(o["q"], o["r"], o["w"], wr, rd, False, True)}
+        p.update(last[s] for s in o["after"])
+        if o["tag"]:
+            last[o["tag"]] = i
+        pred.append(p)
+        note((i, 0, o["q"]), o["r"], o["w"], wr, rd)
+    prio = [o["dur"] for o in ops]
+    for i in range(n - 1, -1, -1):
+        for p in pred[i]:
+            prio[p] = max(prio[p], ops[p]["dur"] + WAKE + prio[i])
+    free, done, out = {}, {}, []
+    succ = [[] for _ in range(n)]
+    wait = [len(p) for p in pred]
+    for i in range(n):
+        for p in pred[i]:
+            succ[p].append(i)
+    ready = {i for i in range(n) if wait[i] == 0}
+    while ready:
+        best = None
+        byq = {}
+        for i in sorted(ready):
+            byq.setdefault(ops[i]["q"], []).append(i)
+        for q, c in byq.items():
+            st = {i: max([free.get(q, 0.0)] + [done[p] + WAKE for p in pred[i]]) for i in c}
+            b = min(c, key=lambda i: (st[i], -prio[i], i))
+            better = [i for i in c if prio[i] > prio[b] and st[i] < st[b] + ops[b]["hold"] - 0.03]
+            if better:
+                b = max(better, key=lambda i: (prio[i], -i))
+            if best is None or (st[b], b) < best:
+                best = (st[b], b)
+        s, i = best
+        ready.discard(i)
+        free[ops[i]["q"]] = s + ops[i]["hold"]
+        done[i] = s + ops[i]["dur"]
+        out.append(ops[i])
+        for j in succ[i]:
+            wait[j] -= 1
+            if wait[j] == 0:
+                ready.add(j)
+    assert len(out) == n
+    return out
 
 
 def rank_program(g, core, T, topo):
@@ -106,12 +178,366 @@ def rank_program(g, core, T, topo):
     op, X, AF = AluOpType, AxisListType.X, ActivationFunctionType
     V, S, P = g.vector, g.scalar, g.tensor
     queue = {"V": g.vector, "S": g.scalar, "P": g.tensor, "G": g, "Y": g.sync}
-    cnt, known = {}, {q: {} for q in queue}
-    wr, rd = {}, {}
+    ops = []
     ls = [0]
     fused = make_send(g, core, T, topo, ls)
 
-    def need(q, deps):
+    def add(q, r, w, call, sem, inc, dur, hold=None, acc=False, after=(), tag=None):
+        ops.append({"q": q, "r": r.split(), "w": w.split(), "call": call, "sem": sem, "inc": inc, "dur": dur,
+                    "hold": dur if hold is None else hold, "acc": acc, "after": after, "tag": tag})
+
+    def do(q, r, w, call, dur, acc=False):
+        add(q, r, w, call, q, 1, dur, acc=acc)
+
+    def ew(n):
+        return max(64, n) * 0.00083
+
+    def dma(q, sem, r, w, o, i):
+        add(q, r, w, lambda: queue[q].dma_start(o, i), sem, 16, DMA, 0.06)
+
+    def send(sem, r, parts, after=(), tag=None):
+        add("G", r, "", lambda: fused(sem, parts), None, 0, CALL, after=after, tag=tag or sem)
+
+    def arrive(sem, n, w, after=None):
+        add("far " + sem, "", w, None, sem, n, HOP[sem], after=(after or sem,))
+
+    def ts(r, w, out, in0, s1, s2, o0, o1=None, n=8):
+        if o1 is None:
+            do("V", r, w, lambda: V.tensor_scalar(out, in0, s1, s2, o0), ew(n))
+        else:
+            do("V", r, w, lambda: V.tensor_scalar(out, in0, s1, s2, o0, o1), ew(n))
+
+    def tt(r, w, out, in0, in1, o, n=8):
+        do("V", r, w, lambda: V.tensor_tensor(out, in0, in1, o), ew(n))
+
+    def scan(r, w, out, d0, d1, init, o0, o1, n=8):
+        do("V", r, w, lambda: V.tensor_tensor_scan(out, d0, d1, init, o0, o1), ew(n))
+
+    def red(r, w, out, in_, o, n=8):
+        do("V", r, w, lambda: V.tensor_reduce(out, in_, X, o), ew(n))
+
+    def cp(r, w, out, in_, n=8):
+        do("V", r, w, lambda: V.tensor_copy(out, in_), ew(n))
+
+    def gather(r, w, out, win, off, n):
+        do("V", r, w, lambda: V.tensor_copy(out, win.indirect(off)), 0.05 + n * 0.00125)
+
+    def act(r, w, out, in_, f, bias=0.0, scale=1.0, accum=None, n=128):
+        do("S", r, w, lambda: S.activation(out, in_, f, bias=bias, scale=scale, accum_out=accum), ew(n) + 0.02)
+
+    junk = [0]
+
+    def count(r, w, in_, f, bias, scale, accum, n=128):
+        j = junk[0] % 20
+        junk[0] += 1
+        act(r, "%s jk%d" % (w, j), T.jk[:, 256 * j:256 * j + n], in_, f, bias, scale, accum, n)
+
+    def quant(r, w, c, s, in_, n=128):
+        do("V", r, w, lambda: V.quantize_mx(c, s, in_), 0.012 + 0.00088 * n)
+
+    def fill(w, ap, c, n=8):
+        do("V", "", w, lambda: V.memset(ap, c), ew(n))
+
+    def pick(out, outs, win, wins, off, r, rs, w, ws, ro, n):
+        do("V", r + " " + ro, w, lambda: V.tensor_copy(out.bitcast(dt.uint32), win.bitcast(dt.uint32).indirect(off)), 0.05 + n * 0.00125)
+        do("S", rs + " " + ro, ws, lambda: S.activation(outs, wins.indirect(off), AF.Copy), 0.07 + n * 0.00125)
+
+    def bank(k, n=128):
+        return T.ps[:, 512 * k:512 * k + n]
+
+    def mm(k, n, lc, lsc, rc, rsc, r, start=True, stop=True):
+        do("P", r, "#%d" % k, lambda: P.matmul_mx(bank(k, n), lc, lsc, rc, rsc, start, stop), (n + 16) * 0.0008, acc=not start)
+
+    grp = near[rank]
+    mates = [q for q in grp if q != rank]
+    on_mates = [q for q in mates if q in chip[rank]]
+    off_mates = [q for q in mates if q not in chip[rank]]
+    eoff = topo.engines(core, cores[off_mates[0]])
+    eon = [e for e in topo.engines(core, cores[on_mates[0]]) if e not in eoff]
+    hosted = {q: sorted((q, partner[q])) for q in grp}
+    h = grp.index(rank)
+    lo, hi = hosted[rank]
+    own = 0 if rank == lo else 1
+    order = [s for q in grp for s in hosted[q]]
+    weight = [2.0 ** (N - 1 - s) for s in order]
+    foff = len(eoff)
+    from_mates = len(off_mates) * foff + len(on_mates) * len(eon)
+
+    def spread(sem, r, src, dst):
+        send(sem, r, [(src, [(cores[q], dst) for q in off_mates], eoff), (src, [(cores[q], dst) for q in on_mates], eon)])
+
+    def iota(w, ap, pat, n, base=0, mul=0, flag=True):
+        if flag:
+            do("G", "", w, lambda: g.iota(ap, pat, base, mul, allow_small_or_imprecise_dtypes=True), 0.13 + 0.00166 * n)
+        else:
+            do("G", "", w, lambda: g.iota(ap, pat, base, mul), 0.13 + 0.00166 * n)
+        if n > 128:
+            ops[-1]["after"] = ("last",)
+
+    dma("Y", "dx", "", "xt", T.xt[:, 0:64], T.x[:, :])
+    dma("S", "dm", "", "mt", T.mt[:, :], T.me[:, :])
+    dma("Y", "dw", "", "wt", T.wt[:, :], T.w[:, :])
+    fill("xz", T.xt[:, 64:512], 0.0, 448)
+    quant("xt xz", "xq xqs", T.xq[:, 0:128], T.xqs[:, 0:128], T.xt[:, :])
+    mo = 128 * own
+    quant("mt", "mcown0 mcown0s", T.mc0[:, mo:mo + 128], T.mc0s[:, mo:mo + 128], T.mt[:, :])
+    qa = QO + A * rank
+    ra = A * chip[rank].index(rank)
+    xs, xd = T.xq[:, 0:A].bitcast(dt.uint8), T.ld0[:, qa:qa + A].bitcast(dt.uint8)
+    ys, yd = T.xqs[:, 0:A], T.ld0s[:, qa:qa + A]
+    send("xa", "xq", [(xs, [(xrel[rank][0], T.rx[:, ra:ra + A].bitcast(dt.uint8))] + [(cores[q], xd) for q in on_mates], eon)],
+         tag="s0")
+    send("xa", "xqs", [(ys, [(xrel[rank][1], T.rxs[:, ra:ra + A])] + [(cores[q], yd) for q in on_mates], eon)],
+         after=("s0",), tag="s1")
+    send("mr", "mcown0", [(T.mc0[:, mo:mo + 128].bitcast(dt.uint8), [(mrel[rank][0], T.rm[:].bitcast(dt.uint8))], eon)],
+         after=("s1",), tag="s2")
+    send("ms", "mcown0s", [(T.mc0s[:, mo:mo + 128], [(mrel[rank][1], T.rms[:])], eon)], after=("s2",), tag="s3")
+    send("xa", "xq", [(xs, [(cores[q], xd) for q in off_mates], eoff)], after=("s3",), tag="s4")
+    send("xa", "xqs", [(ys, [(cores[q], yd) for q in off_mates], eoff)], after=("s4",), tag="last")
+    arrive("xa", 2 * (from_mates + foff * (len(far[rank]) // len(chip[rank]))), "qfar0 qfar0s", "s1")
+    arrive("ma", 2 * foff, "mcfar0 mcfar0s", "s3")
+    iota("pint0", T.pint[:, 0:1], [[0, 1]], 1, 0, 1, False)
+    iota("b8", T.b8[:, :], [[1, 8]], 8)
+    iota("jf", T.jf[:, :], [[1, 128]], 128)
+    iota("jm", T.jm[:, :], [[0, 8], [1, 16]], 128)
+    iota("jw", T.jw[:, :], [[0, 24], [1, 4]], 96)
+    iota("jt", T.jt[:, :], [[0, 32], [-1, 4], [1, 4]], 512)
+    iota("wina", T.wina[:, :], [[0, 32], [1, 16]], 512)
+    iota("d1", T.d1[:, :], [[0, 2], [16, 16], [0, 16]], 512)
+    iota("d2", T.d2[:, :], [[256, 2], [0, 256]], 512)
+    fill("zz", T.zz[:, :], 0.0, 256)
+    ts("pint0", "p16i", T.pint[:, 1:2], T.pint[:, 0:1], 15, None, op.bitwise_and)
+    ts("pint0", "g16i", T.pint[:, 2:3], T.pint[:, 0:1], 4, None, op.logical_shift_right)
+    cp("pint0", "pf0", T.pf[:, 0:1], T.pint[:, 0:1])
+    ts("p16i", "p4i", T.pint[:, 3:4], T.pint[:, 1:2], 2, None, op.logical_shift_right)
+    cp("p16i", "p16", T.pf[:, 1:2], T.pint[:, 1:2])
+    cp("g16i", "g16", T.pf[:, 2:3], T.pint[:, 2:3])
+    cp("p4i", "p4", T.pf[:, 3:4], T.pint[:, 3:4])
+    cp("p16i", "ox", T.ox[:, 0:1], T.pint[:, 1:2])
+    pick(T.ld0[:, qa:qa + A], T.ld0s[:, qa:qa + A], T.xq[:, 0:128], T.xqs[:, 0:128], T.ox[:, 0:1],
+         "xq", "xqs", "qown0", "qown0s", "ox", 16)
+    pf, p16, g16, p4 = T.pf[:, 0:1], T.pf[:, 1:2], T.pf[:, 2:3], T.pf[:, 3:4]
+    for k in range(4):
+        ts("p16", "rm%d" % k, T.rmk[:, k:k + 1], p16, float(k), None, op.is_equal)
+    ts("p16", "rm4", T.rmk[:, 4:5], p16, 2.0, None, op.is_lt)
+    ts("p16", "rm5", T.rmk[:, 5:6], p16, 3.0, None, op.is_lt)
+    tt("rm2 rm3", "rm6", T.rmk[:, 6:7], T.rmk[:, 2:3], T.rmk[:, 3:4], op.add)
+    for t in range(2):
+        fill("lmz%d" % t, T["lm%d" % t][:, 4 * h:4 * h + 4], 0.0)
+    fill("nlz", T.nl[:, 4 * h:4 * h + 4], 0.0)
+    for i, k in ((1, 0), (2, 1), (3, 4), (4, 6)):
+        act("zz rm%d" % k, "wt%d" % i, T.wtile[:, 512 * i:512 * i + 512], T.zz[:, :], AF.Identity, bias=T.rmk[:, k:k + 1], n=512)
+    for nm, a, b in (("wt5", 2560, 3072), ("wt6", 3072, 3584)):
+        act("zz", nm, T.wtile[:, a:b], T.zz[:, 0:b - a], AF.Copy, n=512)
+    for nm in ("ha", "hf", "hc", "hl", "ht", "hm"):
+        act("zz", nm + "z", T[nm][:, 0:512], T.zz[:, 0:512], AF.Copy, n=512)
+    act("zz", "htz1", T.ht[:, 512:520], T.zz[:, 0:8], AF.Copy, n=8)
+    ts("b8 g16", "dg", T.dg[:, :], T.b8[:, :], g16, None, op.is_equal)
+    ts("jw p4", "m1", T.m1[:, :], T.jw[:, :], p4, None, op.is_equal)
+    ts("jw", "hold", T.hold[:, :], T.jw[:, :], 0.0, None, op.is_gt)
+    ts("jf pf0", "idn", T.idn[:, :], T.jf[:, :], pf, None, op.is_equal, n=128)
+    fill("et", T.et[:, :], 0.0, 1024)
+    for b in range(4):
+        ts("idn et", "et%d" % b, T.et[:, 512 * b + b:512 * b + 512:4], T.idn[:, :], 0.5, None, op.mult)
+    quant("et et0 et1 et2 et3", "ec ecs", T.ec[:, :], T.ecs[:, :], T.et[:, :], 512)
+    ts("jf pf0", "tri", T.tri[:, :], T.jf[:, :], pf, None, op.is_lt, n=128)
+    for k in range(4):
+        ts("p16", "kb%d" % k, T.kb[:, k:k + 1], p16, 16.0 * (k % 2) + 0.5, None, op.add)
+    fill("kb4", T.kb[:, 4:5], E + 0.5)
+    ts("pf0", "old", T.kb[:, 5:6], pf, float(QO), None, op.add)
+    ts("pf0", "nold", T.kb[:, 6:7], pf, -1.0, -float(QO), op.mult, op.add)
+    for e in range(2):
+        ts("pf0", "cp%d" % e, T.cc[:, e:e + 1], pf, 128.0 * e + 1, None, op.add)
+        ts("pf0", "cl%d" % e, T.cc[:, 2 + e:3 + e], pf, 128.0 * e, None, op.add)
+        ts("pf0", "cd%d" % e, T.cc[:, 4 + e:5 + e], pf, -1.0, 320.0 - 128.0 * e, op.mult, op.add)
+    for i, (nm, val) in enumerate((("winc", lambda s: float(s == lo)), ("tc1", lambda s: float(s == hi)),
+                                   ("tc2", lambda s: 256.0 * (N - s)), ("tc3", lambda s: 32.0 * order.index(s)))):
+        fill(nm + "z", T[nm][:, 0:256], 0.0, 128)
+        for s in range(N):
+            if val(s):
+                do("V", nm + "z", nm + "_%d" % s,
+                   lambda nm=nm, s=s, val=val: V.memset(T[nm][:, 2 ** (N - 1 - s):2 ** (N - s)], val(s)), ew(8))
+    keys = lambda nm: " ".join([nm + "z"] + [nm + "_%d" % s for s in range(N)])
+    for i in range(N):
+        fill("vd%d" % i, T.vd[:, i:i + 1], 256.0 * (N - order[i]) + 32.0 * i)
+        fill("wd%d" % i, T.wd[:, i:i + 1], weight[i - 1] / weight[i] if i else 1.0)
+    VD, WD = " ".join("vd%d" % i for i in range(N)), " ".join("wd%d" % i for i in range(N))
+    ts("jt rm5", "wt0", T.wtile[:, 0:512], T.jt[:, :], 0.0, T.rmk[:, 5:6], op.is_equal, op.mult, n=256)
+    ts("jm p16 wt5", "wt5a", T.wtile[:, 2560:3072:4], T.jm[:, :], p16, 16.0, op.is_equal, op.mult)
+    ts("jm p16 wt5", "wt5b", T.wtile[:, 2561:3072:4], T.jm[:, :], p16, None, op.is_equal)
+    ts("zz wt6", "wt6a", T.wtile[:, 3072:3584:4], T.zz[:, 0:128], 16.0, None, op.add)
+    ts("zz wt6", "wt6b", T.wtile[:, 3073:3584:4], T.zz[:, 0:128], 1.0, None, op.add)
+    quant("wt0 wt1 wt2 wt3", "wc wcs", T.wc[:, 0:512], T.wcs[:, 0:512], T.wtile[:, 0:2048], 512)
+    quant("wt4 wt5 wt6 wt5a wt5b wt6a wt6b", "wc4 wcs4", T.wc[:, 512:896], T.wcs[:, 512:896], T.wtile[:, 2048:3584], 384)
+    cp("xt", "hcx", T.hc[:, 512:520], T.xt[:, 0:8])
+    cp("xt hlz", "hlx", T.hl[:, 504:512], T.xt[:, 0:8])
+    cp("xt hmz", "hmx", T.hm[:, 504:512], T.xt[:, 0:8])
+    quant("wt", "wq wqs", T.wq[:, :], T.wqs[:, :], T.wt[:, :])
+    dma("Y", "t0", "d1", "wina", T.wina[1:128:16, :], T.d1[1:128:16, :])
+    dma("Y", "t1", "d2", "wina", T.wina[2:128:16, :], T.d2[2:128:16, :])
+    for k in (1, 2, 3):
+        dma("Y", "t%d" % (k + 1), keys("tc%d" % k) + " " + keys("winc"), "wincr%d" % k,
+            T.winc[k:128:16, :], T["tc%d" % k][k:128:16, :])
+    WINC = keys("winc") + " wincr1 wincr2 wincr3"
+
+    def W(i):
+        return T.wc[:, 128 * i:128 * i + 128], T.wcs[:, 128 * i:128 * i + 128]
+
+    def both(nm):
+        return "%s %ss" % (nm, nm)
+
+    def wrapped(k, z, n, out, w, hk, hcod, hsc, h_, r):
+        quant("%s %sz %sx" % (r, hk, hk), both(hk + "c"), hcod[:, :], hsc[:, :], h_[:, :])
+        mm(k, 128, *W(0), hcod[:, :], hsc[:, :], "wc wcs " + both(hk + "c"))
+        scan("#%d m1" % k, "w1" + hk, T.w1[:, z:z + n], bank(k, n), T.m1[:, 0:n], 0.0, op.add, op.mult, n=n)
+        scan("w1%s hold" % hk, "w2" + hk, T.w2[:, z:z + n], T.hold[:, 0:n], T.w1[:, z:z + n], 0.0, op.mult, op.add, n=n)
+        cp("w2" + hk, w, out, T.w2[:, z + 3:z + n:4])
+
+    def one_round(t):
+        ld, lds = T["ld%d" % t], T["ld%ds" % t]
+        mc, mcs = T["mc%d" % t], T["mc%ds" % t]
+        mp, mps = T["mp%d" % t], T["mp%ds" % t]
+        lm = T["lm%d" % t]
+        q, qs = ld[:, QO:QO + 128], lds[:, QO:QO + 128]
+        Q = "qown%d qown%ds qfar%d qfar%ds" % (t, t, t, t)
+        MEM = "mcown%d mcfar%d" % (t, t)
+        MEMS = "mcown%ds mcfar%ds" % (t, t)
+        mm(0, 256, q, qs, mc[:, 0:256], mcs[:, 0:256], Q + " " + MEM + " " + MEMS)
+        for e in range(2):
+            red("#0 lmz%d" % t, "lmo%d%d" % (t, e), lm[:, 4 * h + 2 * e:4 * h + 2 * e + 1], T.ps[:, 128 * e:128 * e + 128], op.max, n=128)
+        OWN = "lmz%d lmo%d0 lmo%d1" % (t, t, t) + (" lmn1" if t else "")
+        spread("m%d" % t, OWN, lm[:, 4 * h:4 * h + 4], lm[:, 4 * h:4 * h + 4])
+        arrive("m%d" % t, from_mates, "lma%d" % t)
+        for b in range(4):
+            mm(1 + b, 128, T.ec[:, 128 * b:128 * b + 128], T.ecs[:, 128 * b:128 * b + 128], q, qs, "ec ecs " + Q, True, False)
+        scan("#0 zz", "cm", T.cm[:, :], T.ps[:, 0:256], T.zz[:, 0:256], -1e29, op.max, op.add, n=256)
+        a, hi16, low = T.aa[:, t:t + 1], T.aa[:, 2 + t:3 + t], T.lw[:, t:t + 1]
+        count("cm", "ah%d" % t, T.cm[:, 15:256:16], AF.Sign, T.cm[:, 255:256], -1.0, hi16, n=16)
+        count("cm", "a%d" % t, T.cm[:, :], AF.Sign, T.cm[:, 255:256], -1.0, a, n=256)
+        ts("dg haz ah%d" % t, "hah", T.ha[:, 0:32:4], T.dg[:, :], hi16, None, op.mult)
+        ts("ah%d a%d" % (t, t), "low%d" % t, low, hi16, -16.0, a, op.mult, op.add)
+        ts("dg haz low%d" % t, "hal", T.ha[:, 1:32:4], T.dg[:, :], low, None, op.mult)
+        quant("haz hah hal", both("hac"), T.hac[:, :], T.hacs[:, :], T.ha[:, :])
+        mm(7, 128, *W(5), T.hac[:, :], T.hacs[:, :], "wc4 wcs4 " + both("hac"))
+        cp("#7", "oaw", T.oaw[:, :], bank(7, 8))
+        pick(mp[:, :], mps[:, :], mc[:, 0:256], mcs[:, 0:256], T.oaw[:, 0:8], MEM, MEMS, "mp%d" % t, "mp%ds" % t, "oaw", 128)
+        for b in range(4):
+            mm(1 + b, 128, T.ec[:, 128 * b:128 * b + 128], T.ecs[:, 128 * b:128 * b + 128], mp[:, :], mps[:, :],
+               "ec ecs mp%d mp%ds" % (t, t), False, True)
+        for b in range(4):
+            if b % 2 == 0:
+                cp("#%d htz" % (1 + b), "ht%d" % b, T.ht[:, b:512:4], bank(1 + b), n=128)
+            else:
+                act("#%d htz" % (1 + b), "ht%d" % b, T.ht[:, b:512:4], bank(1 + b), AF.Copy)
+        quant("ht0 ht1 ht2 ht3 htz htz1", "cand%d cand%ds" % (t, t), mc[:, 256:386], mcs[:, 256:386], T.ht[:, :], 130)
+        ts("idn hfz ah%d" % t, "hfh", T.hf[:, 0:512:4], T.idn[:, :], hi16, None, op.mult)
+        ts("idn hfz low%d" % t, "hfl", T.hf[:, 1:512:4], T.idn[:, :], low, None, op.mult)
+        quant("hfz hfh hfl", both("hfc"), T.hfc[:, :], T.hfcs[:, :], T.hf[:, :])
+        mm(7, 128, *W(6), T.hfc[:, :], T.hfcs[:, :], "wc4 wcs4 " + both("hfc"))
+        act("#7", "fra", T.fra[:, :], bank(7), AF.Identity, bias=1.0)
+        ts("a%d" % t, "nm0", T.nm[:, 0:1], a, 128.0, 128.0 * (hi - 1 - lo), op.is_ge, op.mult)
+        ts("nm0 a%d" % t, "nm1", T.nm[:, 1:2], a, T.nm[:, 0:1], 128.0 * lo, op.add, op.add)
+        nt, nk = ((T.lm1, "lmn1"), (T.nl, "nlo"))[t]
+        ts("nm1 lmz1 nlz", nk, nt[:, 4 * h + 1:4 * h + 4:2], T.zz[:, 0:2], T.nm[:, 1:2], None, op.add)
+        if t == 1:
+            spread("nn", "nlo nlz", T.nl[:, 4 * h:4 * h + 4], T.nl[:, 4 * h:4 * h + 4])
+            arrive("nn", from_mates, "nla")
+        LM = OWN + " lma%d" % t
+        red(LM, "mx", T.mx[:, :], lm[:, 0:16:2], op.max)
+        ts(LM + " mx", "eq", T.eq[:, :], lm[:, 0:16:2], T.mx[:, 0:1], None, op.is_equal)
+        scan("eq " + WD, "sc", T.sc[:, :], T.wd[:, :], T.eq[:, :], 0.0, op.mult, op.add)
+        ts("dg sc", "oc8", T.oc8[:, :], T.dg[:, :], T.sc[:, 7:8], None, op.mult)
+        gather("oc8 hcz hcx " + WINC, "hcg", T.hc[:, 0:512:4], T.winc[:, :], T.oc8[:, 0:8], 128)
+        quant("hcg hcz hcx", both("hcc"), T.hcc[:, 0:130], T.hccs[:, 0:130], T.hc[:, :], 130)
+        for k, i in ((5, 1), (6, 2), (7, 3), (0, 4)):
+            mm(k, 130, *W(i), T.hcc[:, 0:130], T.hccs[:, 0:130], "wc wcs wc4 wcs4 " + both("hcc"))
+        scan("#5 zz", "clo", T.clo[:, :], bank(5), T.zz[:, 0:128], 0.0, op.add, op.add, n=128)
+        scan("#6 zz", "chi", T.chi[:, :], bank(6), T.zz[:, 0:128], 0.0, op.add, op.add, n=128)
+        for c, src, nm in ((0, T.clo, "clo"), (1, T.clo, "clo"), (2, T.chi, "chi")):
+            count("%s kb%d" % (nm, c), "acc%d" % c, src[:, :], AF.Sign, T.kb[:, c:c + 1], -1.0, T.acc[:, c:c + 1])
+        ts("chi kb3", "le", T.le[:, :], T.chi[:, :], T.kb[:, 3:4], None, op.is_le)
+        red("le", "acv", T.acv[:, :], T.le[:, :], op.add, n=128)
+        cp("acv", "os3", T.oslot[:, 3:4], T.acv[:, :])
+        ts("acc0 acc1 acc2", "os0", T.oslot[:, 0:3], T.acc[:, 0:3], 0.5, 64.0, op.mult, op.add)
+        pick(ld[:, 64 * h:64 * h + 64], lds[:, 64 * h:64 * h + 64], mc[:, 256:386], mcs[:, 256:386], T.oslot[:, 0:4],
+             "cand%d" % t, "cand%ds" % t, "slot%d" % t, "slot%ds" % t, "os0 os3", 64)
+        spread("c%d" % t, "slot%d" % t, ld[:, 64 * h:64 * h + 64].bitcast(dt.uint8), ld[:, 64 * h:64 * h + 64].bitcast(dt.uint8))
+        spread("c%d" % t, "slot%ds" % t, lds[:, 64 * h:64 * h + 64], lds[:, 64 * h:64 * h + 64])
+        arrive("c%d" % t, 2 * from_mates, "land%d land%ds" % (t, t))
+        halves = (0, 1) if t == 0 else (own,)
+        tt("#7 fra", "tg", T.tg[:, :], bank(7), T.fra[:, :], op.mult, n=128)
+        for e in halves:
+            src, nm = ((T.clo, "clo"), (T.chi, "chi"))[e]
+            count("%s kb4" % nm, "ta%d" % e, src[:, :], AF.Sign, T.kb[:, 4:5], -1.0, T.ta[:, e:e + 1])
+            ts("tg cp%d" % e, "ep%d" % e, T.ep[:, 128 * e:128 * e + 128], T.tg[:, :], T.cc[:, e:e + 1], None, op.is_equal)
+            scan("ep%d zz" % e, "co%d" % e, T.co[:, 128 * e:128 * e + 128], T.ep[:, 128 * e:128 * e + 128], T.zz[:, 0:128],
+                 0.0, op.max, op.add)
+            count("co%d" % e, "un%d" % e, T.co[:, 128 * e:128 * e + 128], AF.Identity, 1.0, -2.0, T.un[:, e:e + 1])
+            tt("un%d ta%d" % (e, e), "jg%d" % e, T.jg[:, e:e + 1], T.un[:, e:e + 1], T.ta[:, e:e + 1], op.is_lt)
+            ts("un%d cd%d" % (e, e), "jd%d" % e, T.jd[:, e:e + 1], T.un[:, e:e + 1], 0.5, T.cc[:, 4 + e:5 + e], op.mult, op.add)
+            ts("jd%d jg%d cl%d" % (e, e, e), "l3%d" % e, T.l3[:, e:e + 1], T.jd[:, e:e + 1], T.jg[:, e:e + 1],
+               T.cc[:, 2 + e:3 + e], op.mult, op.add)
+        for i, e in enumerate(halves):
+            ts("dg l3%d" % e, "o3%d" % i, T.o3[:, 8 * i:8 * i + 8], T.dg[:, :], T.l3[:, e:e + 1], None, op.mult)
+        v, an = T.vv[:, t:t + 1], T.an[:, t:t + 1]
+        tt("eq " + VD, "pv", T.pv[:, :], T.eq[:, :], T.vd[:, :], op.mult)
+        red("pv", "v%d" % t, v, T.pv[:, :], op.max)
+        cp("v%d" % t, "bi0", T.bi[:, 0:1], v)
+        ts("bi0", "bi1", T.bi[:, 1:2], T.bi[:, 0:1], 255, None, op.bitwise_and)
+        cp("bi1", "kk1", T.kk[:, 1:2], T.bi[:, 1:2])
+        ts("tri v%d" % t, "triv", T.triv[:, :], T.tri[:, :], v, None, op.mult, n=128)
+        tt("#0 triv", "eqt", T.eqt[:, :], bank(0), T.triv[:, :], op.is_equal, n=128)
+        red("eqt", "kk0", T.kk[:, 0:1], T.eqt[:, :], op.add, n=128)
+        ts("kk0", "an%d" % t, an, T.kk[:, 0:1], float(E), None, op.is_lt)
+        ts("kk0 kk1 nold", "kk2", T.kk[:, 2:3], T.kk[:, 0:1], T.kk[:, 1:2], T.kb[:, 6:7], op.add, op.add)
+        ts("kk2 an%d old" % t, "kk3", T.kk[:, 3:4], T.kk[:, 2:3], an, T.kb[:, 5:6], op.mult, op.add)
+        ts("dg kk3", "o2", T.o2[:, :], T.dg[:, :], T.kk[:, 3:4], None, op.mult)
+        gather("o2 wina hlz", "hl0", T.hl[:, 0:128], T.wina[:, :], T.o2[:, 0:8], 128)
+        ts(VD + " v%d" % t, "oh%d" % t, T.oh[:, 8 * t:8 * t + 8], T.vd[:, :], v, None, op.is_equal)
+        ts("an%d" % t, "ws%d" % t, T.wv[:, t:t + 1], an, 2.0, -1.0, op.mult, op.add)
+        ts("an%d" % t, "wb%d" % t, T.wv[:, 2 + t:3 + t], an, -1.0, None, op.add)
+        ts("oh%d ws%d" % (t, t), "og%d" % t, T.og[:, 8 * t:8 * t + 8], T.oh[:, 8 * t:8 * t + 8], T.wv[:, t:t + 1], None, op.mult)
+        if t == 0:
+            gather("o30 wina hlz", "hl1", T.hl[:, 128:256], T.wina[:, :], T.o3[:, 0:8], 128)
+            do("S", "o31 wina hlz", "hl2",
+               lambda: S.activation(T.hl[:, 256:384], T.wina[:, :].indirect(T.o3[:, 8:16]), AF.Copy), 0.23)
+            wrapped(1, 0, 96, T.ol[:, 0:24], "ol", "hl", T.hlc, T.hlcs, T.hl, "hl0 hl1 hl2")
+            pick(T.mc1[:, 0:256], T.mc1s[:, 0:256], mc[:, 0:386], mcs[:, 0:386], T.ol[:, 8:24],
+                 MEM + " cand0", MEMS + " cand0s", "mcown1 mcfar1", "mcown1s mcfar1s", "ol", 256)
+            pick(T.ld1[:, QO:QO + 128], T.ld1s[:, QO:QO + 128], ld[:, 0:384], lds[:, 0:384], T.ol[:, 0:8],
+                 "slot0 land0 qown0 qfar0", "slot0s land0s qown0s qfar0s", "qown1 qfar1", "qown1s qfar1s", "ol", 128)
+        else:
+            wrapped(1, 0, 32, T.ol[:, 0:8], "ol", "hl", T.hlc, T.hlcs, T.hl, "hl0 hl1 hl2")
+            gather("o30 wina hmz", "hm0", T.hm[:, 0:128], T.wina[:, :], T.o3[:, 0:8], 128)
+            wrapped(2, 96, 32, T.om[:, 0:8], "om", "hm", T.hmc, T.hmcs, T.hm, "hm0")
+            pick(T.fm[:, :], T.fms[:, :], mc[:, 0:386], mcs[:, 0:386], T.om[:, 0:8],
+                 MEM + " cand1", MEMS + " cand1s", "fm", "fms", "om", 128)
+            dma("Y", "u0", "fm", "out0", T.oc[:, :], T.fm[:, :].bitcast(dt.uint8))
+            for k in range(4):
+                dma("Y", "u%d" % (1 + k), "fms", "out%d" % (1 + k), T.osc[4 * k:4 * k + 4, :], T.fms[32 * k:32 * k + 4, :])
+
+    one_round(0)
+    one_round(1)
+    pick(T.qf[:, :], T.qfs[:, :], T.ld1[:, 0:384], T.ld1s[:, 0:384], T.ol[:, 0:8],
+         "slot1 land1 qown1 qfar1", "slot1s land1s qown1s qfar1s", "qf", "qfs", "ol", 128)
+    mm(3, 128, T.wq[:, :], T.wqs[:, :], T.qf[:, :], T.qfs[:, :], "wq wqs qf qfs")
+    act("#3", "ysb", T.ysb[:, :], bank(3), AF.Copy)
+    dma("S", "u7", "ysb", "outy", T.y[:, :], T.ysb[:, :])
+    for t, nt, nk in ((0, T.lm1, "lmn1 lmz1 lma1"), (1, T.nl, "nlo nlz nla")):
+        tt("og%d %s" % (t, nk), "oh%d" % t, T.oh[:, 8 * t:8 * t + 8], T.og[:, 8 * t:8 * t + 8], nt[:, 1:16:2], op.mult)
+        red("oh%d" % t, "wg%d" % t, T.wv[:, 4 + t:5 + t], T.oh[:, 8 * t:8 * t + 8], op.add)
+        tt("wg%d wb%d" % (t, t), "wo%d" % t, T.wo[:, t:t + 1], T.wv[:, 4 + t:5 + t], T.wv[:, 2 + t:3 + t], op.add)
+        dma("Y", "u%d" % (5 + t), "wo%d" % t, "out%d" % (5 + t), T.wi[t:t + 1, :], T.wo[:, t:t + 1])
+
+    cnt, known = {}, {q: {} for q in queue}
+    wr, rd = {}, {}
+    for o in in_order(ops):
+        q = o["q"]
+        if o["call"] is None:
+            cnt[o["sem"]] = o["inc"]
+            note((o["sem"], o["inc"], "far", {}), [], o["w"], wr, rd)
+            continue
+        deps = conflicts(q, o["r"], o["w"], wr, rd, o["acc"], False)
         want = {}
         for e in deps:
             if known[q].get(e[0], 0) < e[1]:
@@ -127,375 +553,11 @@ def rank_program(g, core, T, topo):
             for s, v in e[3].items():
                 if known[q].get(s, 0) < v:
                     known[q][s] = v
-
-    def deps_of(q, r, w, acc):
-        d = []
-        for k in r:
-            d += wr.get(k, [])
-            if k[0] == "#":
-                d += [e for e in rd.get(k, []) if e[2] != q]
-        for k in w:
-            d += [e for e in wr.get(k, []) if not (acc and e[2] == q)]
-            d += [e for e in rd.get(k, []) if e[2] != q]
-        return d
-
-    def note(e, r, w):
-        for k in w:
-            wr[k], rd[k] = [e], []
-        for k in r:
-            rd.setdefault(k, []).append(e)
-
-    def do(q, r, w, call, acc=False):
-        r, w = r.split(), w.split()
-        need(q, deps_of(q, r, w, acc))
-        call().then_inc(T.sem[q], 1)
-        cnt[q] = cnt.get(q, 0) + 1
-        note((q, cnt[q], q, dict(known[q])), r, w)
-
-    def dma(q, sem, r, w, o, i):
-        r, w = r.split(), w.split()
-        need(q, deps_of(q, r, w, False))
-        queue[q].dma_start(o, i).then_inc(T.sem[sem], 16)
-        cnt[sem] = cnt.get(sem, 0) + 16
-        note((sem, cnt[sem], "dma", dict(known[q])), r, w)
-
-    def arrive(sem, n, w):
-        cnt[sem] = n
-        for k in w.split():
-            wr[k], rd[k] = [(sem, n, "far", {})], []
-
-    def send(sem, r, parts):
-        need("G", deps_of("G", r.split(), [], False))
-        fused(sem, parts)
-
-    def ts(r, w, out, in0, s1, s2, o0, o1=None):
-        if o1 is None:
-            do("V", r, w, lambda: V.tensor_scalar(out, in0, s1, s2, o0))
-        else:
-            do("V", r, w, lambda: V.tensor_scalar(out, in0, s1, s2, o0, o1))
-
-    def tt(r, w, out, in0, in1, o):
-        do("V", r, w, lambda: V.tensor_tensor(out, in0, in1, o))
-
-    def scan(r, w, out, d0, d1, init, o0, o1):
-        do("V", r, w, lambda: V.tensor_tensor_scan(out, d0, d1, init, o0, o1))
-
-    def red(r, w, out, in_, o):
-        do("V", r, w, lambda: V.tensor_reduce(out, in_, X, o))
-
-    def cp(r, w, out, in_):
-        do("V", r, w, lambda: V.tensor_copy(out, in_))
-
-    def act(r, w, out, in_, f, bias=0.0, scale=1.0, accum=None):
-        do("S", r, w, lambda: S.activation(out, in_, f, bias=bias, scale=scale, accum_out=accum))
-
-    def quant(r, w, c, s, in_):
-        do("V", r, w, lambda: V.quantize_mx(c, s, in_))
-
-    def fill(w, ap, c):
-        do("V", "", w, lambda: V.memset(ap, c))
-
-    def pick(out, outs, win, wins, off, r, rs, w, ws, ro):
-        do("V", r + " " + ro, w, lambda: V.tensor_copy(out.bitcast(dt.uint32), win.bitcast(dt.uint32).indirect(off)))
-        do("S", rs + " " + ro, ws, lambda: S.activation(outs, wins.indirect(off), AF.Copy))
-
-    def bank(k, n=128):
-        return T.ps[:, 512 * k:512 * k + n]
-
-    def mm(k, n, lc, lsc, rc, rsc, r, start=True, stop=True):
-        do("P", r, "#%d" % k, lambda: P.matmul_mx(bank(k, n), lc, lsc, rc, rsc, start, stop), acc=not start)
-
-    grp = near[rank]
-    mates = [q for q in grp if q != rank]
-    on_mates = [q for q in mates if q in chip[rank]]
-    off_mates = [q for q in mates if q not in chip[rank]]
-    eoff = topo.engines(core, cores[off_mates[0]])
-    eon = [e for e in topo.engines(core, cores[on_mates[0]]) if e not in eoff]
-    eall = topo.engines(core, mrel[rank][0])
-    hosted = {q: sorted((q, partner[q])) for q in grp}
-    h = grp.index(rank)
-    lo, hi = hosted[rank]
-    own = 0 if rank == lo else 1
-    order = [s for q in grp for s in hosted[q]]
-    weight = [2.0 ** (N - 1 - s) for s in order]
-    foff = len(eoff)
-    from_mates = len(off_mates) * foff + len(on_mates) * len(eon)
-
-    def spread(sem, r, src, dst):
-        send(sem, r, [(src, [(cores[q], dst) for q in off_mates], eoff), (src, [(cores[q], dst) for q in on_mates], eon)])
-
-    def iota(w, ap, pat, base=0, mul=0, flag=True):
-        if flag:
-            do("G", "", w, lambda: g.iota(ap, pat, base, mul, allow_small_or_imprecise_dtypes=True))
-        else:
-            do("G", "", w, lambda: g.iota(ap, pat, base, mul))
-
-    dma("Y", "dx", "", "xt", T.xt[:, 0:64], T.x[:, :])
-    dma("S", "dm", "", "mt", T.mt[:, :], T.me[:, :])
-    dma("Y", "dw", "", "wt", T.wt[:, :], T.w[:, :])
-    iota("pint0", T.pint[:, 0:1], [[0, 1]], 0, 1, False)
-    iota("b8", T.b8[:, :], [[1, 8]])
-    iota("jf", T.jf[:, :], [[1, 128]])
-    iota("jm", T.jm[:, :], [[0, 8], [1, 16]])
-    iota("jw", T.jw[:, :], [[0, 24], [1, 4]])
-    fill("xz", T.xt[:, 64:512], 0.0)
-    fill("zz", T.zz[:, :], 0.0)
-    for t in range(2):
-        fill("lmz%d" % t, T["lm%d" % t][:, 4 * h:4 * h + 4], 0.0)
-    fill("nlz", T.nl[:, 4 * h:4 * h + 4], 0.0)
-    ts("pint0", "p16i", T.pint[:, 1:2], T.pint[:, 0:1], 15, None, op.bitwise_and)
-    ts("pint0", "g16i", T.pint[:, 2:3], T.pint[:, 0:1], 4, None, op.logical_shift_right)
-    cp("pint0", "pf0", T.pf[:, 0:1], T.pint[:, 0:1])
-    ts("p16i", "p4i", T.pint[:, 3:4], T.pint[:, 1:2], 2, None, op.logical_shift_right)
-    cp("p16i", "p16", T.pf[:, 1:2], T.pint[:, 1:2])
-    cp("g16i", "g16", T.pf[:, 2:3], T.pint[:, 2:3])
-    cp("p4i", "p4", T.pf[:, 3:4], T.pint[:, 3:4])
-    cp("p16i", "ox", T.ox[:, 0:1], T.pint[:, 1:2])
-    pf, p16, g16, p4 = T.pf[:, 0:1], T.pf[:, 1:2], T.pf[:, 2:3], T.pf[:, 3:4]
-    for k in range(4):
-        ts("p16", "rm%d" % k, T.rmk[:, k:k + 1], p16, float(k), None, op.is_equal)
-    ts("p16", "rm4", T.rmk[:, 4:5], p16, 2.0, None, op.is_lt)
-    ts("p16", "rm5", T.rmk[:, 5:6], p16, 3.0, None, op.is_lt)
-    tt("rm2 rm3", "rm6", T.rmk[:, 6:7], T.rmk[:, 2:3], T.rmk[:, 3:4], op.add)
-    quant("xt xz", "xq xqs", T.xq[:, 0:128], T.xqs[:, 0:128], T.xt[:, :])
-    mo = 128 * own
-    quant("mt", "mcown0 mcown0s", T.mc0[:, mo:mo + 128], T.mc0s[:, mo:mo + 128], T.mt[:, :])
-    qa = QO + A * rank
-    ra = A * chip[rank].index(rank)
-    xs = T.xq[:, 0:A].bitcast(dt.uint8)
-    xd = T.ld0[:, qa:qa + A].bitcast(dt.uint8)
-    send("xa", "xq", [(xs, [(xrel[rank][0], T.rx[:, ra:ra + A].bitcast(dt.uint8))] + [(cores[q], xd) for q in on_mates], eon),
-                      (xs, [(cores[q], xd) for q in off_mates], eoff)])
-    xs, xd = T.xqs[:, 0:A], T.ld0s[:, qa:qa + A]
-    send("xa", "xqs", [(xs, [(xrel[rank][1], T.rxs[:, ra:ra + A])] + [(cores[q], xd) for q in on_mates], eon),
-                       (xs, [(cores[q], xd) for q in off_mates], eoff)])
-    send("mr", "mcown0", [(T.mc0[:, mo:mo + 128].bitcast(dt.uint8), [(mrel[rank][0], T.rm[:].bitcast(dt.uint8))], eall)])
-    send("ms", "mcown0s", [(T.mc0s[:, mo:mo + 128], [(mrel[rank][1], T.rms[:])], eall)])
-    pick(T.ld0[:, qa:qa + A], T.ld0s[:, qa:qa + A], T.xq[:, 0:128], T.xqs[:, 0:128], T.ox[:, 0:1],
-         "xq", "xqs", "qown0", "qown0s", "ox")
-    arrive("xa", 2 * (from_mates + foff * (len(far[rank]) // len(chip[rank]))), "qfar0 qfar0s")
-    arrive("ma", 2 * foff, "mcfar0 mcfar0s")
-    iota("jt", T.jt[:, :], [[0, 32], [-1, 4], [1, 4]])
-    iota("wina", T.wina[:, :], [[0, 32], [1, 16]])
-    iota("d1", T.d1[:, :], [[0, 2], [16, 16], [0, 16]])
-    iota("d2", T.d2[:, :], [[256, 2], [0, 256]])
-    for i, k in ((1, 0), (2, 1), (3, 4), (4, 6)):
-        act("zz rm%d" % k, "wt%d" % i, T.wtile[:, 512 * i:512 * i + 512], T.zz[:, :], AF.Identity, bias=T.rmk[:, k:k + 1])
-    for nm, a, b in (("wt5", 2560, 3072), ("wt6", 3072, 3584)):
-        act("zz", nm, T.wtile[:, a:b], T.zz[:, 0:b - a], AF.Copy)
-    for nm in ("ha", "hf", "hc", "hl", "ht"):
-        act("zz", nm + "z", T[nm][:, 0:512], T.zz[:, 0:512], AF.Copy)
-    act("zz", "htz1", T.ht[:, 512:520], T.zz[:, 0:8], AF.Copy)
-    ts("b8 g16", "dg", T.dg[:, :], T.b8[:, :], g16, None, op.is_equal)
-    ts("jw p4", "m1", T.m1[:, :], T.jw[:, :], p4, None, op.is_equal)
-    ts("jw", "hold", T.hold[:, :], T.jw[:, :], 0.0, None, op.is_gt)
-    ts("jf pf0", "idn", T.idn[:, :], T.jf[:, :], pf, None, op.is_equal)
-    fill("et", T.et[:, :], 0.0)
-    for b in range(4):
-        ts("idn et", "et%d" % b, T.et[:, 512 * b + b:512 * b + 512:4], T.idn[:, :], 0.5, None, op.mult)
-    quant("et et0 et1 et2 et3", "ec ecs", T.ec[:, :], T.ecs[:, :], T.et[:, :])
-    ts("jf pf0", "tri", T.tri[:, :], T.jf[:, :], pf, None, op.is_lt)
-    for k in range(4):
-        ts("p16", "kb%d" % k, T.kb[:, k:k + 1], p16, 16.0 * (k % 2) + 0.5, None, op.add)
-    fill("kb4", T.kb[:, 4:5], E + 0.5)
-    ts("pf0", "old", T.kb[:, 5:6], pf, float(QO), None, op.add)
-    ts("pf0", "nold", T.kb[:, 6:7], pf, -1.0, -float(QO), op.mult, op.add)
-    for e in range(2):
-        ts("pf0", "cp%d" % e, T.cc[:, e:e + 1], pf, 128.0 * e + 1, None, op.add)
-        ts("pf0", "cl%d" % e, T.cc[:, 2 + e:3 + e], pf, 128.0 * e, None, op.add)
-        ts("pf0", "cd%d" % e, T.cc[:, 4 + e:5 + e], pf, -1.0, 320.0 - 128.0 * e, op.mult, op.add)
-    for i, (nm, val) in enumerate((("winc", lambda s: float(s == lo)), ("tc1", lambda s: float(s == hi)),
-                                   ("tc2", lambda s: 256.0 * (N - s)), ("tc3", lambda s: 32.0 * order.index(s)))):
-        fill(nm + "z", T[nm][:, 0:256], 0.0)
-        for s in range(N):
-            if val(s):
-                do("V", nm + "z", nm + "_%d" % s,
-                   lambda nm=nm, s=s, val=val: V.memset(T[nm][:, 2 ** (N - 1 - s):2 ** (N - s)], val(s)))
-    keys = lambda nm: " ".join([nm + "z"] + [nm + "_%d" % s for s in range(N)])
-    for i in range(N):
-        fill("vd%d" % i, T.vd[:, i:i + 1], 256.0 * (N - order[i]) + 32.0 * i)
-        fill("wd%d" % i, T.wd[:, i:i + 1], weight[i - 1] / weight[i] if i else 1.0)
-    VD, WD = " ".join("vd%d" % i for i in range(N)), " ".join("wd%d" % i for i in range(N))
-    ts("jt rm5", "wt0", T.wtile[:, 0:512], T.jt[:, :], 0.0, T.rmk[:, 5:6], op.is_equal, op.mult)
-    ts("jm p16 wt5", "wt5a", T.wtile[:, 2560:3072:4], T.jm[:, :], p16, 16.0, op.is_equal, op.mult)
-    ts("jm p16 wt5", "wt5b", T.wtile[:, 2561:3072:4], T.jm[:, :], p16, None, op.is_equal)
-    ts("zz wt6", "wt6a", T.wtile[:, 3072:3584:4], T.zz[:, 0:128], 16.0, None, op.add)
-    ts("zz wt6", "wt6b", T.wtile[:, 3073:3584:4], T.zz[:, 0:128], 1.0, None, op.add)
-    quant("wt0 wt1 wt2 wt3", "wc wcs", T.wc[:, 0:512], T.wcs[:, 0:512], T.wtile[:, 0:2048])
-    quant("wt4 wt5 wt6 wt5a wt5b wt6a wt6b", "wc4 wcs4", T.wc[:, 512:896], T.wcs[:, 512:896], T.wtile[:, 2048:3584])
-    cp("xt", "hcx", T.hc[:, 512:520], T.xt[:, 0:8])
-    cp("xt hlz", "hlx", T.hl[:, 504:512], T.xt[:, 0:8])
-    quant("wt", "wq wqs", T.wq[:, :], T.wqs[:, :], T.wt[:, :])
-    dma("Y", "t0", "d1", "wina", T.wina[1:128:16, :], T.d1[1:128:16, :])
-    dma("Y", "t1", "d2", "wina", T.wina[2:128:16, :], T.d2[2:128:16, :])
-    for k in (1, 2, 3):
-        dma("Y", "t%d" % (k + 1), keys("tc%d" % k) + " " + keys("winc"), "wincr%d" % k,
-            T.winc[k:128:16, :], T["tc%d" % k][k:128:16, :])
-    WINC = keys("winc") + " wincr1 wincr2 wincr3"
-
-    def W(i):
-        return T.wc[:, 128 * i:128 * i + 128], T.wcs[:, 128 * i:128 * i + 128]
-
-    def both(nm):
-        return "%s %ss" % (nm, nm)
-
-    def wi_steps(rounds):
-        nums = {0: (T.lm1, "lmn1 lmz1 lma1"), 1: (T.nl, "nlo nlz nla")}
-        for t in rounds:
-            ts(VD + " v%d" % t, "oh%d" % t, T.oh[:, 8 * t:8 * t + 8], T.vd[:, :], T.vv[:, t:t + 1], None, op.is_equal)
-        for t in rounds:
-            tt("oh%d %s" % (t, nums[t][1]), "oh%d" % t, T.oh[:, 8 * t:8 * t + 8], T.oh[:, 8 * t:8 * t + 8], nums[t][0][:, 1:16:2], op.mult)
-        for t in rounds:
-            red("oh%d" % t, "wg%d" % t, T.wv[:, t:t + 1], T.oh[:, 8 * t:8 * t + 8], op.add)
-        for t in rounds:
-            ts("wg%d" % t, "wh%d" % t, T.wv[:, 2 + t:3 + t], T.wv[:, t:t + 1], 2.0, 1.0, op.mult, op.add)
-        for t in rounds:
-            ts("wh%d an%d" % (t, t), "wk%d" % t, T.wv[:, 4 + t:5 + t], T.wv[:, 2 + t:3 + t], T.an[:, t:t + 1], None, op.mult)
-        for t in rounds:
-            ts("wk%d wg%d" % (t, t), "wo%d" % t, T.wo[:, t:t + 1], T.wv[:, 4 + t:5 + t], T.wv[:, t:t + 1], 1.0, op.subtract, op.subtract)
-        for t in rounds:
-            dma("Y", "u%d" % (5 + t), "wo%d" % t, "out%d" % (5 + t), T.wi[t:t + 1, :], T.wo[:, t:t + 1])
-
-    for t in range(2):
-        ld, lds = T["ld%d" % t], T["ld%ds" % t]
-        mc, mcs = T["mc%d" % t], T["mc%ds" % t]
-        mp, mps = T["mp%d" % t], T["mp%ds" % t]
-        lm = T["lm%d" % t]
-        q, qs = ld[:, QO:QO + 128], lds[:, QO:QO + 128]
-        Q = "qown%d qown%ds qfar%d qfar%ds" % (t, t, t, t)
-        MEM = "mcown%d mcfar%d" % (t, t)
-        MEMS = "mcown%ds mcfar%ds" % (t, t)
-        mm(0, 256, q, qs, mc[:, 0:256], mcs[:, 0:256], Q + " " + MEM + " " + MEMS)
-        for e in range(2):
-            red("#0 lmz%d" % t, "lmo%d%d" % (t, e), lm[:, 4 * h + 2 * e:4 * h + 2 * e + 1], T.ps[:, 128 * e:128 * e + 128], op.max)
-        OWN = "lmz%d lmo%d0 lmo%d1" % (t, t, t) + (" lmn1" if t else "")
-        spread("m%d" % t, OWN, lm[:, 4 * h:4 * h + 4], lm[:, 4 * h:4 * h + 4])
-        arrive("m%d" % t, from_mates, "lma%d" % t)
-        for b in range(4):
-            mm(1 + b, 128, T.ec[:, 128 * b:128 * b + 128], T.ecs[:, 128 * b:128 * b + 128], q, qs, "ec ecs " + Q, True, False)
-        scan("#0 zz", "cm", T.cm[:, :], T.ps[:, 0:256], T.zz[:, 0:256], -1e29, op.max, op.add)
-        a, hi16, low = T.aa[:, t:t + 1], T.aa[:, 2 + t:3 + t], T.lw[:, t:t + 1]
-        act("cm", "jk ah%d" % t, T.jk[:, 0:16], T.cm[:, 15:256:16], AF.Sign, bias=T.cm[:, 255:256], scale=-1.0, accum=hi16)
-        act("cm", "jk a%d" % t, T.jk[:, :], T.cm[:, :], AF.Sign, bias=T.cm[:, 255:256], scale=-1.0, accum=a)
-        ts("dg haz ah%d" % t, "hah", T.ha[:, 0:32:4], T.dg[:, :], hi16, None, op.mult)
-        ts("ah%d a%d" % (t, t), "low%d" % t, low, hi16, -16.0, a, op.mult, op.add)
-        ts("idn hfz ah%d" % t, "hfh", T.hf[:, 0:512:4], T.idn[:, :], hi16, None, op.mult)
-        ts("dg haz low%d" % t, "hal", T.ha[:, 1:32:4], T.dg[:, :], low, None, op.mult)
-        ts("idn hfz low%d" % t, "hfl", T.hf[:, 1:512:4], T.idn[:, :], low, None, op.mult)
-        quant("haz hah hal", both("hac"), T.hac[:, :], T.hacs[:, :], T.ha[:, :])
-        mm(7, 128, *W(5), T.hac[:, :], T.hacs[:, :], "wc4 wcs4 " + both("hac"))
-        ts("a%d" % t, "nm0", T.nm[:, 0:1], a, 128.0, 128.0 * (hi - 1 - lo), op.is_ge, op.mult)
-        quant("hfz hfh hfl", both("hfc"), T.hfc[:, :], T.hfcs[:, :], T.hf[:, :])
-        cp("#7", "oaw", T.oaw[:, :], bank(7, 8))
-        pick(mp[:, :], mps[:, :], mc[:, 0:256], mcs[:, 0:256], T.oaw[:, 0:8], MEM, MEMS, "mp%d" % t, "mp%ds" % t, "oaw")
-        nt, nk = ((T.lm1, "lmn1"), (T.nl, "nlo"))[t]
-        ts("nm0 a%d" % t, "nm1", T.nm[:, 1:2], a, T.nm[:, 0:1], 128.0 * lo, op.add, op.add)
-        for c in (1, 3):
-            cp("nm1 lmz1 nlz", nk, nt[:, 4 * h + c:4 * h + c + 1], T.nm[:, 1:2])
-        mm(7, 128, *W(6), T.hfc[:, :], T.hfcs[:, :], "wc4 wcs4 " + both("hfc"))
-        for b in range(4):
-            mm(1 + b, 128, T.ec[:, 128 * b:128 * b + 128], T.ecs[:, 128 * b:128 * b + 128], mp[:, :], mps[:, :],
-               "ec ecs mp%d mp%ds" % (t, t), False, True)
-        for b in range(4):
-            if b % 2 == 0:
-                cp("#%d htz" % (1 + b), "ht%d" % b, T.ht[:, b:512:4], bank(1 + b))
-            else:
-                act("#%d htz" % (1 + b), "ht%d" % b, T.ht[:, b:512:4], bank(1 + b), AF.Copy)
-        act("#7", "fra", T.fra[:, :], bank(7), AF.Identity, bias=1.0)
-        quant("ht0 ht1 ht2 ht3 htz htz1", "cand%d cand%ds" % (t, t), mc[:, 256:386], mcs[:, 256:386], T.ht[:, :])
-        LM = OWN + " lma%d" % t
-        red(LM, "mx", T.mx[:, :], lm[:, 0:16:2], op.max)
-        ts(LM + " mx", "eq", T.eq[:, :], lm[:, 0:16:2], T.mx[:, 0:1], None, op.is_equal)
-        scan("eq " + WD, "sc", T.sc[:, :], T.wd[:, :], T.eq[:, :], 0.0, op.mult, op.add)
-        tt("eq " + VD, "pv", T.pv[:, :], T.eq[:, :], T.vd[:, :], op.mult)
-        ts("dg sc", "oc8", T.oc8[:, :], T.dg[:, :], T.sc[:, 7:8], None, op.mult)
-        v, an = T.vv[:, t:t + 1], T.an[:, t:t + 1]
-        red("pv", "v%d" % t, v, T.pv[:, :], op.max)
-        cp("oc8 hcz hcx " + WINC, "hcg", T.hc[:, 0:512:4], T.winc[:, :].indirect(T.oc8[:, 0:8]))
-        cp("v%d" % t, "bi0", T.bi[:, 0:1], v)
-        quant("hcg hcz hcx", both("hcc"), T.hcc[:, 0:130], T.hccs[:, 0:130], T.hc[:, :])
-        for k, i in ((5, 1), (6, 2), (0, 4), (7, 3)):
-            mm(k, 130, *W(i), T.hcc[:, 0:130], T.hccs[:, 0:130], "wc wcs wc4 wcs4 " + both("hcc"))
-        ts("tri v%d" % t, "triv", T.triv[:, :], T.tri[:, :], v, None, op.mult)
-        ts("bi0", "bi1", T.bi[:, 1:2], T.bi[:, 0:1], 255, None, op.bitwise_and)
-        scan("#5 zz", "clo", T.clo[:, :], bank(5), T.zz[:, 0:128], 0.0, op.add, op.add)
-        scan("#6 zz", "chi", T.chi[:, :], bank(6), T.zz[:, 0:128], 0.0, op.add, op.add)
-        for c, src, nm in ((0, T.clo, "clo"), (1, T.clo, "clo"), (2, T.chi, "chi")):
-            act("%s kb%d" % (nm, c), "jk acc%d" % c, T.jk[:, 0:128], src[:, :], AF.Sign, bias=T.kb[:, c:c + 1], scale=-1.0,
-                accum=T.acc[:, c:c + 1])
-        tt("#0 triv", "eqt", T.eqt[:, :], bank(0), T.triv[:, :], op.is_equal)
-        ts("chi kb3", "le", T.le[:, :], T.chi[:, :], T.kb[:, 3:4], None, op.is_le)
-        tt("#7 fra", "tg", T.tg[:, :], bank(7), T.fra[:, :], op.mult)
-        red("le", "acv", T.acv[:, :], T.le[:, :], op.add)
-        cp("bi1", "kk1", T.kk[:, 1:2], T.bi[:, 1:2])
-        cp("acv", "os3", T.oslot[:, 3:4], T.acv[:, :])
-        ts("acc0 acc1 acc2", "os0", T.oslot[:, 0:3], T.acc[:, 0:3], 0.5, 64.0, op.mult, op.add)
-        pick(ld[:, 64 * h:64 * h + 64], lds[:, 64 * h:64 * h + 64], mc[:, 256:386], mcs[:, 256:386], T.oslot[:, 0:4],
-             "cand%d" % t, "cand%ds" % t, "slot%d" % t, "slot%ds" % t, "os0 os3")
-        spread("c%d" % t, "slot%d" % t, ld[:, 64 * h:64 * h + 64].bitcast(dt.uint8), ld[:, 64 * h:64 * h + 64].bitcast(dt.uint8))
-        spread("c%d" % t, "slot%ds" % t, lds[:, 64 * h:64 * h + 64], lds[:, 64 * h:64 * h + 64])
-        arrive("c%d" % t, 2 * from_mates, "land%d land%ds" % (t, t))
-        if t == 1:
-            spread("nn", "nlo nlz", T.nl[:, 4 * h:4 * h + 4], T.nl[:, 4 * h:4 * h + 4])
-            arrive("nn", from_mates, "nla")
-        halves = (0, 1) if t == 0 else (own,)
-        for e, (src, nm) in enumerate(((T.clo, "clo"), (T.chi, "chi"))):
-            if e in halves:
-                act("%s kb4" % nm, "jk ta%d" % e, T.jk[:, 0:128], src[:, :], AF.Sign, bias=T.kb[:, 4:5], scale=-1.0,
-                    accum=T.ta[:, e:e + 1])
-        for e in halves:
-            ts("tg cp%d" % e, "ep%d" % e, T.ep[:, 128 * e:128 * e + 128], T.tg[:, :], T.cc[:, e:e + 1], None, op.is_equal)
-        red("eqt", "kk0", T.kk[:, 0:1], T.eqt[:, :], op.add)
-        for e in halves:
-            scan("ep%d zz" % e, "co%d" % e, T.co[:, 128 * e:128 * e + 128], T.ep[:, 128 * e:128 * e + 128], T.zz[:, 0:128],
-                 0.0, op.max, op.add)
-            act("co%d" % e, "jk un%d" % e, T.jk[:, 0:128], T.co[:, 128 * e:128 * e + 128], AF.Identity, bias=1.0, scale=-2.0,
-                accum=T.un[:, e:e + 1])
-        ts("kk0", "an%d" % t, an, T.kk[:, 0:1], float(E), None, op.is_lt)
-        ts("kk0 kk1 nold", "kk2", T.kk[:, 2:3], T.kk[:, 0:1], T.kk[:, 1:2], T.kb[:, 6:7], op.add, op.add)
-        ts("kk2 an%d old" % t, "kk3", T.kk[:, 3:4], T.kk[:, 2:3], an, T.kb[:, 5:6], op.mult, op.add)
-        ts("dg kk3", "o2", T.o2[:, :], T.dg[:, :], T.kk[:, 3:4], None, op.mult)
-        for e in halves:
-            tt("un%d ta%d" % (e, e), "jg%d" % e, T.jg[:, e:e + 1], T.un[:, e:e + 1], T.ta[:, e:e + 1], op.is_lt)
-            ts("un%d cd%d" % (e, e), "jd%d" % e, T.jd[:, e:e + 1], T.un[:, e:e + 1], 0.5, T.cc[:, 4 + e:5 + e], op.mult, op.add)
-        for e in halves:
-            ts("jd%d jg%d cl%d" % (e, e, e), "l3%d" % e, T.l3[:, e:e + 1], T.jd[:, e:e + 1], T.jg[:, e:e + 1], T.cc[:, 2 + e:3 + e],
-               op.mult, op.add)
-        cp("o2 wina hlz", "hl0", T.hl[:, 0:128], T.wina[:, :].indirect(T.o2[:, 0:8]))
-        for i, e in enumerate(halves):
-            ts("dg l3%d" % e, "o3%d" % i, T.o3[:, 8 * i:8 * i + 8], T.dg[:, :], T.l3[:, e:e + 1], None, op.mult)
-        cp("o30 wina hlz", "hl1", T.hl[:, 128:256], T.wina[:, :].indirect(T.o3[:, 0:8]))
-        if t == 0:
-            act("o31 wina hlz", "hl2", T.hl[:, 256:384], T.wina[:, :].indirect(T.o3[:, 8:16]), AF.Copy)
-        quant("hl0 hl1 hl2 hlz hlx", both("hlc"), T.hlc[:, :], T.hlcs[:, :], T.hl[:, :])
-        mm(1, 128, *W(0), T.hlc[:, :], T.hlcs[:, :], "wc wcs " + both("hlc"))
-        n = 96 if t == 0 else 64
-        scan("#1 m1", "w1", T.w1[:, 0:n], bank(1, n), T.m1[:, 0:n], 0.0, op.add, op.mult)
-        scan("w1 hold", "w2", T.w2[:, 0:n], T.hold[:, 0:n], T.w1[:, 0:n], 0.0, op.mult, op.add)
-        cp("w2", "ol", T.ol[:, 0:n // 4], T.w2[:, 3:n:4])
-        if t == 0:
-            pick(T.mc1[:, 0:256], T.mc1s[:, 0:256], mc[:, 0:386], mcs[:, 0:386], T.ol[:, 8:24],
-                 MEM + " cand0", MEMS + " cand0s", "mcown1", "mcown1s", "ol")
-            note(("V", cnt["V"], "V", dict(known["V"])), [], ["mcfar1"])
-            note(("S", cnt["S"], "S", dict(known["S"])), [], ["mcfar1s"])
-            pick(T.ld1[:, QO:QO + 128], T.ld1s[:, QO:QO + 128], ld[:, 0:384], lds[:, 0:384], T.ol[:, 0:8],
-                 "slot0 land0 qown0 qfar0", "slot0s land0s qown0s qfar0s", "qown1", "qown1s", "ol")
-            note(("V", cnt["V"], "V", dict(known["V"])), [], ["qfar1"])
-            note(("S", cnt["S"], "S", dict(known["S"])), [], ["qfar1s"])
-        else:
-            pick(T.fm[:, :], T.fms[:, :], mc[:, 0:386], mcs[:, 0:386], T.ol[:, 8:16],
-                 MEM + " cand1", MEMS + " cand1s", "fm", "fms", "ol")
-            dma("Y", "u0", "fm", "out0", T.oc[:, :], T.fm[:, :].bitcast(dt.uint8))
-            for k in range(4):
-                dma("Y", "u%d" % (1 + k), "fms", "out%d" % (1 + k), T.osc[4 * k:4 * k + 4, :], T.fms[32 * k:32 * k + 4, :])
-
-    wi_steps((0,))
-    pick(T.qf[:, :], T.qfs[:, :], T.ld1[:, 0:384], T.ld1s[:, 0:384], T.ol[:, 0:8],
-         "slot1 land1 qown1 qfar1", "slot1s land1s qown1s qfar1s", "qf", "qfs", "ol")
-    mm(3, 128, T.wq[:, :], T.wqs[:, :], T.qf[:, :], T.qfs[:, :], "wq wqs qf qfs")
-    wi_steps((1,))
-    act("#3", "ysb", T.ysb[:, :], bank(3), AF.Copy)
-    dma("S", "u7", "ysb", "outy", T.y[:, :], T.ysb[:, :])
+        made = o["call"]()
+        if o["sem"]:
+            made.then_inc(T.sem[o["sem"]], o["inc"])
+            cnt[o["sem"]] = cnt.get(o["sem"], 0) + o["inc"]
+            note((o["sem"], cnt[o["sem"]], q if o["sem"] == q else "dma", dict(known[q])), o["r"], o["w"], wr, rd)
     for s, n in cnt.items():
         if known["G"].get(s, 0) < n:
             g.wait_ge(T.sem[s], n)

from concourse.bass import DstId, RemoteDMATransfer
from concourse.mybir import dt, AluOpType, AxisListType, ActivationFunctionType

F8 = "float8_e4m3fn_x4"
SCRATCH = {"ps": ("psum", [128, 4096], "float32")}
for _n, _w in (("xq", 128), ("wq", 128), ("rx", 32), ("rm", 128), ("ld0", 384), ("ld1", 384), ("qf", 128), ("mc0", 416),
               ("mc1", 416), ("fm", 128), ("mp0", 128), ("mp1", 128), ("wc", 896), ("ec", 512), ("hac", 128), ("hfc", 128),
               ("hcc", 136), ("hlc", 128), ("hmc", 128)):
    SCRATCH[_n] = ("sbuf", [128, _w], F8)
    SCRATCH[_n + "s"] = ("sbuf", [128, _w], "uint8")
for _n, _w in (("xt", 512), ("mt", 512), ("wt", 512), ("ha", 512), ("hf", 512), ("hc", 520), ("hl", 512), ("hm", 512), ("ht", 520),
               ("wtile", 3584), ("et", 2048), ("zz", 512), ("wina", 512), ("d1", 512), ("d2", 512), ("winc", 256), ("tc1", 256),
               ("tc2", 256), ("tc3", 256), ("tri", 128), ("m1", 96), ("hold", 96), ("jm", 128), ("jt", 512), ("jw", 96),
               ("idn", 128), ("jk", 5120), ("fra", 128), ("clo", 128), ("chi", 128), ("le", 128), ("eqt", 128), ("tg", 128),
               ("ep", 256), ("co", 256)):
    SCRATCH[_n] = ("sbuf", [128, _w], "bfloat16")
for _n, _w in (("jf", 128), ("b8", 8), ("pf", 4), ("rmk", 8), ("dg", 8), ("kb", 8), ("cc", 8), ("vd", 8), ("wd", 8), ("lm0", 16),
               ("lm1", 16), ("nl", 16), ("cm", 256), ("aa", 4), ("lw", 2), ("vv", 2), ("an", 2), ("w1", 128), ("w2", 128),
               ("mx", 1), ("eq", 8), ("sc", 8), ("acc", 4), ("acv", 1), ("pv", 8), ("triv", 128), ("kk", 4),
               ("ta", 2), ("jg", 2), ("jd", 2), ("l3", 2), ("un", 2), ("nm", 2), ("wv", 8), ("oh", 16), ("og", 16), ("wo", 2),
               ("ysb", 128)):
    SCRATCH[_n] = ("sbuf", [128, _w], "float32")
for _n, _w in (("ox", 2), ("oaw", 8), ("oc8", 8), ("oslot", 4), ("o2", 8), ("o3", 16), ("ol", 24), ("om", 8)):
    SCRATCH[_n] = ("sbuf", [128, _w], "uint16")
for _n, _w in (("pint", 4), ("bi", 2)):
    SCRATCH[_n] = ("sbuf", [128, _w], "int32")
SEMAPHORES = ["V", "S", "P", "G", "ls", "xa", "ma", "mr", "ms", "m0", "m1", "nn", "c0", "c1",
              "dx", "dm", "dw", "t0", "t1", "t2", "t3", "t4", "u0", "u1", "u2", "u3", "u4", "u5", "u6", "u7"]
A = 16
E = 32
QO = 256
WAKE = 0.2
DMA, CALL = 1.8, 0.5
HOP = {"xa": 6.0, "ma": 7.0, "m0": 1.6, "m1": 1.6, "nn": 1.6, "c0": 2.4, "c1": 2.4}


def plan(T, topo):
    cores = T.cores
    n = len(cores)
    near = [[q for q in range(n) if q == r or topo.may_write(cores[r], cores[q])] for r in range(n)]
    far = [[q for q in range(n) if q not in near[r]] for r in range(n)]
    chip = [[q for q in range(n) if cores[q] in topo.cores_of(cores[r])] for r in range(n)]
    partner = [[q for q in far[r] if topo.host(cores[q]) == topo.host(cores[r]) and topo.die(cores[q]) == topo.die(cores[r])][0]
               for r in range(n)]
    port = [[c for c in topo.cores_of(cores[r]) if c not in cores and topo.die(c) == topo.die(cores[r])
             and topo.may_write(c, cores[far[r][0]])] for r in range(n)]
    xrel = [(port[chip[r][0]][0], port[chip[r][1]][0]) for r in range(n)]
    mrel = [(port[r][1], port[r][0]) for r in range(n)]
    return near, far, chip, partner, xrel, mrel


def bits(engines):
    return sum(1 << e for e in engines)


def make_send(g, core, T, topo, count):
    def send(sem, parts):
        tr = []
        for src, dst, eng in parts:
            ids = []
            for c, _ in dst:
                rid, pid = topo.addr(c, core)
                ids.append(DstId(rid=rid, pnc=pid))
            tr.append(RemoteDMATransfer(dst_ids=ids, dma_engine_mask=bits(eng), remote_sem=T.sem[sem],
                                        srcs=[src], dsts=[d for _, d in dst], alu_op=0))
            count[0] += len(eng)
        g.remote_dma_fused(tr, local_sem=T.sem.ls)
    return send


def relay(g, core, T, topo, pl):
    near, far, chip, partner, xrel, mrel = pl
    cores = T.cores
    n = [0]
    send = make_send(g, core, T, topo, n)
    here = [r for r in range(len(cores)) if core in topo.cores_of(cores[r])]
    for r in here[:1]:
        off = topo.engines(core, cores[far[r][0]])
        on = [e for e in topo.engines(core, cores[r]) if e not in off]
        if core in xrel[r]:
            g.wait_ge(T.sem.xa, len(on) * len(here))
            a, b = QO + A * r, QO + A * r + A * len(here)
            if core == xrel[r][0]:
                send("xa", [(T.rx[:].bitcast(dt.uint8), [(cores[q], T.ld0[:, a:b].bitcast(dt.uint8)) for q in far[r]], off)])
            else:
                send("xa", [(T.rxs[:], [(cores[q], T.ld0s[:, a:b]) for q in far[r]], off)])
    for r in here:
        p = partner[r]
        h = 128 if r > p else 0
        off = topo.engines(core, cores[p])
        on = [e for e in topo.engines(core, cores[r]) if e not in off]
        if core == mrel[r][0]:
            g.wait_ge(T.sem.mr, len(on))
            send("ma", [(T.rm[:].bitcast(dt.uint8), [(cores[p], T.mc0[:, h:h + 128].bitcast(dt.uint8))], off)])
        if core == mrel[r][1]:
            g.wait_ge(T.sem.ms, len(on))
            send("ma", [(T.rms[:], [(cores[p], T.mc0s[:, h:h + 128])], off)])
    if n[0]:
        g.wait_ge(T.sem.ls, n[0])


def conflicts(q, r, w, wr, rd, acc, strict):
    d = []
    for k in r:
        d += wr.get(k, [])
        if k[0] == "#":
            d += [e for e in rd.get(k, []) if e[2] != q]
    for k in w:
        d += [e for e in wr.get(k, []) if strict or not (acc and e[2] == q)]
        d += [e for e in rd.get(k, []) if strict or e[2] != q]
    return d


def note(e, r, w, wr, rd):
    for k in w:
        wr[k], rd[k] = [e], []
    for k in r:
        rd.setdefault(k, []).append(e)


def in_order(ops):
    n = len(ops)
    wr, rd, pred = {}, {}, []
    last = {}
    for i, o in enumerate(ops):
        p = {e[0] for e in conflicts(o["q"], o["r"], o["w"], wr, rd, False, True)}
        p.update(last[s] for s in o["after"])
        if o["tag"]:
            last[o["tag"]] = i
        pred.append(p)
        note((i, 0, o["q"]), o["r"], o["w"], wr, rd)
    prio = [o["dur"] for o in ops]
    for i in range(n - 1, -1, -1):
        for p in pred[i]:
            prio[p] = max(prio[p], ops[p]["dur"] + WAKE + prio[i])
    free, done, out = {}, {}, []
    succ = [[] for _ in range(n)]
    wait = [len(p) for p in pred]
    for i in range(n):
        for p in pred[i]:
            succ[p].append(i)
    ready = {i for i in range(n) if wait[i] == 0}
    while ready:
        best = None
        byq = {}
        for i in sorted(ready):
            byq.setdefault(ops[i]["q"], []).append(i)
        for q, c in byq.items():
            st = {i: max([free.get(q, 0.0)] + [done[p] + WAKE for p in pred[i]]) for i in c}
            b = min(c, key=lambda i: (st[i], -prio[i], i))
            better = [i for i in c if prio[i] > prio[b] and st[i] < st[b] + ops[b]["hold"] - 0.03]
            if better:
                b = max(better, key=lambda i: (prio[i], -i))
            if best is None or (st[b], b) < best:
                best = (st[b], b)
        s, i = best
        ready.discard(i)
        free[ops[i]["q"]] = s + ops[i]["hold"]
        done[i] = s + ops[i]["dur"]
        out.append(ops[i])
        for j in succ[i]:
            wait[j] -= 1
            if wait[j] == 0:
                ready.add(j)
    assert len(out) == n
    return out


def rank_program(g, core, T, topo):
    pl = plan(T, topo)
    near, far, chip, partner, xrel, mrel = pl
    cores = T.cores
    N = len(cores)
    rank = T.rank_of(core)
    if rank is None:
        relay(g, core, T, topo, pl)
        return
    op, X, AF = AluOpType, AxisListType.X, ActivationFunctionType
    V, S, P = g.vector, g.scalar, g.tensor
    queue = {"V": g.vector, "S": g.scalar, "P": g.tensor, "G": g, "Y": g.sync}
    ops = []
    ls = [0]
    fused = make_send(g, core, T, topo, ls)

    def add(q, r, w, call, sem, inc, dur, hold=None, acc=False, after=(), tag=None):
        ops.append({"q": q, "r": r.split(), "w": w.split(), "call": call, "sem": sem, "inc": inc, "dur": dur,
                    "hold": dur if hold is None else hold, "acc": acc, "after": after, "tag": tag})

    def do(q, r, w, call, dur, acc=False):
        add(q, r, w, call, q, 1, dur, acc=acc)

    def ew(n):
        return max(64, n) * 0.00083

    def dma(q, sem, r, w, o, i):
        add(q, r, w, lambda: queue[q].dma_start(o, i), sem, 16, DMA, 0.06)

    def send(sem, r, parts, after=(), tag=None):
        add("G", r, "", lambda: fused(sem, parts), None, 0, CALL, after=after, tag=tag or sem)

    def arrive(sem, n, w, after=None):
        add("far " + sem, "", w, None, sem, n, HOP[sem], after=(after or sem,))

    def ts(r, w, out, in0, s1, s2, o0, o1=None, n=8):
        if o1 is None:
            do("V", r, w, lambda: V.tensor_scalar(out, in0, s1, s2, o0), ew(n))
        else:
            do("V", r, w, lambda: V.tensor_scalar(out, in0, s1, s2, o0, o1), ew(n))

    def tt(r, w, out, in0, in1, o, n=8):
        do("V", r, w, lambda: V.tensor_tensor(out, in0, in1, o), ew(n))

    def scan(r, w, out, d0, d1, init, o0, o1, n=8):
        do("V", r, w, lambda: V.tensor_tensor_scan(out, d0, d1, init, o0, o1), ew(n))

    def red(r, w, out, in_, o, n=8):
        do("V", r, w, lambda: V.tensor_reduce(out, in_, X, o), ew(n))

    def cp(r, w, out, in_, n=8):
        do("V", r, w, lambda: V.tensor_copy(out, in_), ew(n))

    def gather(r, w, out, win, off, n):
        do("V", r, w, lambda: V.tensor_copy(out, win.indirect(off)), 0.05 + n * 0.00125)

    def act(r, w, out, in_, f, bias=0.0, scale=1.0, accum=None, n=128):
        do("S", r, w, lambda: S.activation(out, in_, f, bias=bias, scale=scale, accum_out=accum), ew(n) + 0.02)

    junk = [0]

    def count(r, w, in_, f, bias, scale, accum, n=128):
        j = junk[0] % 20
        junk[0] += 1
        act(r, "%s jk%d" % (w, j), T.jk[:, 256 * j:256 * j + n], in_, f, bias, scale, accum, n)

    def quant(r, w, c, s, in_, n=128):
        do("V", r, w, lambda: V.quantize_mx(c, s, in_), 0.012 + 0.00088 * n)

    def fill(w, ap, c, n=8):
        do("V", "", w, lambda: V.memset(ap, c), ew(n))

    def pick(out, outs, win, wins, off, r, rs, w, ws, ro, n):
        do("V", r + " " + ro, w, lambda: V.tensor_copy(out.bitcast(dt.uint32), win.bitcast(dt.uint32).indirect(off)), 0.05 + n * 0.00125)
        do("S", rs + " " + ro, ws, lambda: S.activation(outs, wins.indirect(off), AF.Copy), 0.07 + n * 0.00125)

    def bank(k, n=128):
        return T.ps[:, 512 * k:512 * k + n]

    def mm(k, n, lc, lsc, rc, rsc, r, start=True, stop=True):
        do("P", r, "#%d" % k, lambda: P.matmul_mx(bank(k, n), lc, lsc, rc, rsc, start, stop), (n + 16) * 0.0008, acc=not start)

    grp = near[rank]
    mates = [q for q in grp if q != rank]
    on_mates = [q for q in mates if q in chip[rank]]
    off_mates = [q for q in mates if q not in chip[rank]]
    eoff = topo.engines(core, cores[off_mates[0]])
    eon = [e for e in topo.engines(core, cores[on_mates[0]]) if e not in eoff]
    hosted = {q: sorted((q, partner[q])) for q in grp}
    h = grp.index(rank)
    lo, hi = hosted[rank]
    own = 0 if rank == lo else 1
    order = [s for q in grp for s in hosted[q]]
    weight = [2.0 ** (N - 1 - s) for s in order]
    foff = len(eoff)
    from_mates = len(off_mates) * foff + len(on_mates) * len(eon)

    def spread(sem, r, src, dst):
        send(sem, r, [(src, [(cores[q], dst) for q in off_mates], eoff), (src, [(cores[q], dst) for q in on_mates], eon)])

    def iota(w, ap, pat, n, base=0, mul=0, flag=True):
        if flag:
            do("G", "", w, lambda: g.iota(ap, pat, base, mul, allow_small_or_imprecise_dtypes=True), 0.13 + 0.00166 * n)
        else:
            do("G", "", w, lambda: g.iota(ap, pat, base, mul), 0.13 + 0.00166 * n)
        if n > 128:
            ops[-1]["after"] = ("last",)

    dma("Y", "dx", "", "xt", T.xt[:, 0:64], T.x[:, :])
    dma("S", "dm", "", "mt", T.mt[:, :], T.me[:, :])
    dma("Y", "dw", "", "wt", T.wt[:, :], T.w[:, :])
    fill("xz", T.xt[:, 64:512], 0.0, 448)
    quant("xt xz", "xq xqs", T.xq[:, 0:128], T.xqs[:, 0:128], T.xt[:, :])
    mo = 128 * own
    quant("mt", "mcown0 mcown0s", T.mc0[:, mo:mo + 128], T.mc0s[:, mo:mo + 128], T.mt[:, :])
    qa = QO + A * rank
    ra = A * chip[rank].index(rank)
    xs, xd = T.xq[:, 0:A].bitcast(dt.uint8), T.ld0[:, qa:qa + A].bitcast(dt.uint8)
    ys, yd = T.xqs[:, 0:A], T.ld0s[:, qa:qa + A]
    send("xa", "xq", [(xs, [(xrel[rank][0], T.rx[:, ra:ra + A].bitcast(dt.uint8))] + [(cores[q], xd) for q in on_mates], eon)],
         tag="s0")
    send("xa", "xqs", [(ys, [(xrel[rank][1], T.rxs[:, ra:ra + A])] + [(cores[q], yd) for q in on_mates], eon)],
         after=("s0",), tag="s1")
    send("mr", "mcown0", [(T.mc0[:, mo:mo + 128].bitcast(dt.uint8), [(mrel[rank][0], T.rm[:].bitcast(dt.uint8))], eon)],
         after=("s1",), tag="s2")
    send("ms", "mcown0s", [(T.mc0s[:, mo:mo + 128], [(mrel[rank][1], T.rms[:])], eon)], after=("s2",), tag="s3")
    send("xa", "xq", [(xs, [(cores[q], xd) for q in off_mates], eoff)], after=("s3",), tag="s4")
    send("xa", "xqs", [(ys, [(cores[q], yd) for q in off_mates], eoff)], after=("s4",), tag="last")
    arrive("xa", 2 * (from_mates + foff * (len(far[rank]) // len(chip[rank]))), "qfar0 qfar0s", "s1")
    arrive("ma", 2 * foff, "mcfar0 mcfar0s", "s3")
    iota("pint0", T.pint[:, 0:1], [[0, 1]], 1, 0, 1, False)
    iota("b8", T.b8[:, :], [[1, 8]], 8)
    iota("jf", T.jf[:, :], [[1, 128]], 128)
    iota("jm", T.jm[:, :], [[0, 8], [1, 16]], 128)
    iota("jw", T.jw[:, :], [[0, 24], [1, 4]], 96)
    iota("jt", T.jt[:, :], [[0, 32], [-1, 4], [1, 4]], 512)
    iota("wina", T.wina[:, :], [[0, 32], [1, 16]], 512)
    iota("d1", T.d1[:, :], [[0, 2], [16, 16], [0, 16]], 512)
    iota("d2", T.d2[:, :], [[256, 2], [0, 256]], 512)
    fill("zz", T.zz[:, :], 0.0, 256)
    ts("pint0", "p16i", T.pint[:, 1:2], T.pint[:, 0:1], 15, None, op.bitwise_and)
    ts("pint0", "g16i", T.pint[:, 2:3], T.pint[:, 0:1], 4, None, op.logical_shift_right)
    cp("pint0", "pf0", T.pf[:, 0:1], T.pint[:, 0:1])
    ts("p16i", "p4i", T.pint[:, 3:4], T.pint[:, 1:2], 2, None, op.logical_shift_right)
    cp("p16i", "p16", T.pf[:, 1:2], T.pint[:, 1:2])
    cp("g16i", "g16", T.pf[:, 2:3], T.pint[:, 2:3])
    cp("p4i", "p4", T.pf[:, 3:4], T.pint[:, 3:4])
    cp("p16i", "ox", T.ox[:, 0:1], T.pint[:, 1:2])
    pick(T.ld0[:, qa:qa + A], T.ld0s[:, qa:qa + A], T.xq[:, 0:128], T.xqs[:, 0:128], T.ox[:, 0:1],
         "xq", "xqs", "qown0", "qown0s", "ox", 16)
    pf, p16, g16, p4 = T.pf[:, 0:1], T.pf[:, 1:2], T.pf[:, 2:3], T.pf[:, 3:4]
    for k in range(4):
        ts("p16", "rm%d" % k, T.rmk[:, k:k + 1], p16, float(k), None, op.is_equal)
    ts("p16", "rm4", T.rmk[:, 4:5], p16, 2.0, None, op.is_lt)
    ts("p16", "rm5", T.rmk[:, 5:6], p16, 3.0, None, op.is_lt)
    tt("rm2 rm3", "rm6", T.rmk[:, 6:7], T.rmk[:, 2:3], T.rmk[:, 3:4], op.add)
    for t in range(2):
        fill("lmz%d" % t, T["lm%d" % t][:, 4 * h:4 * h + 4], 0.0)
    fill("nlz", T.nl[:, 4 * h:4 * h + 4], 0.0)
    for i, k in ((1, 0), (2, 1), (3, 4), (4, 6)):
        act("zz rm%d" % k, "wt%d" % i, T.wtile[:, 512 * i:512 * i + 512], T.zz[:, :], AF.Identity, bias=T.rmk[:, k:k + 1], n=512)
    for nm, a, b in (("wt5", 2560, 3072), ("wt6", 3072, 3584)):
        act("zz", nm, T.wtile[:, a:b], T.zz[:, 0:b - a], AF.Copy, n=512)
    for nm in ("ha", "hf", "hc", "hl", "ht", "hm"):
        act("zz", nm + "z", T[nm][:, 0:512], T.zz[:, 0:512], AF.Copy, n=512)
    act("zz", "htz1", T.ht[:, 512:520], T.zz[:, 0:8], AF.Copy, n=8)
    ts("b8 g16", "dg", T.dg[:, :], T.b8[:, :], g16, None, op.is_equal)
    ts("jw p4", "m1", T.m1[:, :], T.jw[:, :], p4, None, op.is_equal)
    ts("jw", "hold", T.hold[:, :], T.jw[:, :], 0.0, None, op.is_gt)
    ts("jf pf0", "idn", T.idn[:, :], T.jf[:, :], pf, None, op.is_equal, n=128)
    fill("et", T.et[:, :], 0.0, 1024)
    for b in range(4):
        ts("idn et", "et%d" % b, T.et[:, 512 * b + b:512 * b + 512:4], T.idn[:, :], 0.5, None, op.mult)
    quant("et et0 et1 et2 et3", "ec ecs", T.ec[:, :], T.ecs[:, :], T.et[:, :], 512)
    ts("jf pf0", "tri", T.tri[:, :], T.jf[:, :], pf, None, op.is_lt, n=128)
    for k in range(4):
        ts("p16", "kb%d" % k, T.kb[:, k:k + 1], p16, 16.0 * (k % 2) + 0.5, None, op.add)
    fill("kb4", T.kb[:, 4:5], E + 0.5)
    ts("pf0", "old", T.kb[:, 5:6], pf, float(QO), None, op.add)
    ts("pf0", "nold", T.kb[:, 6:7], pf, -1.0, -float(QO), op.mult, op.add)
    for e in range(2):
        ts("pf0", "cp%d" % e, T.cc[:, e:e + 1], pf, 128.0 * e + 1, None, op.add)
        ts("pf0", "cl%d" % e, T.cc[:, 2 + e:3 + e], pf, 128.0 * e, None, op.add)
        ts("pf0", "cd%d" % e, T.cc[:, 4 + e:5 + e], pf, -1.0, 320.0 - 128.0 * e, op.mult, op.add)
    for i, (nm, val) in enumerate((("winc", lambda s: float(s == lo)), ("tc1", lambda s: float(s == hi)),
                                   ("tc2", lambda s: 256.0 * (N - s)), ("tc3", lambda s: 32.0 * order.index(s)))):
        fill(nm + "z", T[nm][:, 0:256], 0.0, 128)
        for s in range(N):
            if val(s):
                do("V", nm + "z", nm + "_%d" % s,
                   lambda nm=nm, s=s, val=val: V.memset(T[nm][:, 2 ** (N - 1 - s):2 ** (N - s)], val(s)), ew(8))
    keys = lambda nm: " ".join([nm + "z"] + [nm + "_%d" % s for s in range(N)])
    for i in range(N):
        fill("vd%d" % i, T.vd[:, i:i + 1], 256.0 * (N - order[i]) + 32.0 * i)
        fill("wd%d" % i, T.wd[:, i:i + 1], weight[i - 1] / weight[i] if i else 1.0)
    VD, WD = " ".join("vd%d" % i for i in range(N)), " ".join("wd%d" % i for i in range(N))
    ts("jt rm5", "wt0", T.wtile[:, 0:512], T.jt[:, :], 0.0, T.rmk[:, 5:6], op.is_equal, op.mult, n=256)
    ts("jm p16 wt5", "wt5a", T.wtile[:, 2560:3072:4], T.jm[:, :], p16, 16.0, op.is_equal, op.mult)
    ts("jm p16 wt5", "wt5b", T.wtile[:, 2561:3072:4], T.jm[:, :], p16, None, op.is_equal)
    ts("zz wt6", "wt6a", T.wtile[:, 3072:3584:4], T.zz[:, 0:128], 16.0, None, op.add)
    ts("zz wt6", "wt6b", T.wtile[:, 3073:3584:4], T.zz[:, 0:128], 1.0, None, op.add)
    quant("wt0 wt1 wt2 wt3", "wc wcs", T.wc[:, 0:512], T.wcs[:, 0:512], T.wtile[:, 0:2048], 512)
    quant("wt4 wt5 wt6 wt5a wt5b wt6a wt6b", "wc4 wcs4", T.wc[:, 512:896], T.wcs[:, 512:896], T.wtile[:, 2048:3584], 384)
    cp("xt", "hcx", T.hc[:, 512:520], T.xt[:, 0:8])
    cp("xt hlz", "hlx", T.hl[:, 504:512], T.xt[:, 0:8])
    cp("xt hmz", "hmx", T.hm[:, 504:512], T.xt[:, 0:8])
    quant("wt", "wq wqs", T.wq[:, :], T.wqs[:, :], T.wt[:, :])
    dma("Y", "t0", "d1", "wina", T.wina[1:128:16, :], T.d1[1:128:16, :])
    dma("Y", "t1", "d2", "wina", T.wina[2:128:16, :], T.d2[2:128:16, :])
    for k in (1, 2, 3):
        dma("Y", "t%d" % (k + 1), keys("tc%d" % k) + " " + keys("winc"), "wincr%d" % k,
            T.winc[k:128:16, :], T["tc%d" % k][k:128:16, :])
    WINC = keys("winc") + " wincr1 wincr2 wincr3"

    def W(i):
        return T.wc[:, 128 * i:128 * i + 128], T.wcs[:, 128 * i:128 * i + 128]

    def both(nm):
        return "%s %ss" % (nm, nm)

    def wrapped(k, z, n, out, w, hk, hcod, hsc, h_, r):
        quant("%s %sz %sx" % (r, hk, hk), both(hk + "c"), hcod[:, :], hsc[:, :], h_[:, :])
        mm(k, 128, *W(0), hcod[:, :], hsc[:, :], "wc wcs " + both(hk + "c"))
        scan("#%d m1" % k, "w1" + hk, T.w1[:, z:z + n], bank(k, n), T.m1[:, 0:n], 0.0, op.add, op.mult, n=n)
        scan("w1%s hold" % hk, "w2" + hk, T.w2[:, z:z + n], T.hold[:, 0:n], T.w1[:, z:z + n], 0.0, op.mult, op.add, n=n)
        cp("w2" + hk, w, out, T.w2[:, z + 3:z + n:4])

    def one_round(t):
        ld, lds = T["ld%d" % t], T["ld%ds" % t]
        mc, mcs = T["mc%d" % t], T["mc%ds" % t]
        mp, mps = T["mp%d" % t], T["mp%ds" % t]
        lm = T["lm%d" % t]
        q, qs = ld[:, QO:QO + 128], lds[:, QO:QO + 128]
        Q = "qown%d qown%ds qfar%d qfar%ds" % (t, t, t, t)
        MEM = "mcown%d mcfar%d" % (t, t)
        MEMS = "mcown%ds mcfar%ds" % (t, t)
        mm(0, 256, q, qs, mc[:, 0:256], mcs[:, 0:256], Q + " " + MEM + " " + MEMS)
        for e in range(2):
            red("#0 lmz%d" % t, "lmo%d%d" % (t, e), lm[:, 4 * h + 2 * e:4 * h + 2 * e + 1], T.ps[:, 128 * e:128 * e + 128], op.max, n=128)
        OWN = "lmz%d lmo%d0 lmo%d1" % (t, t, t) + (" lmn1" if t else "")
        spread("m%d" % t, OWN, lm[:, 4 * h:4 * h + 4], lm[:, 4 * h:4 * h + 4])
        arrive("m%d" % t, from_mates, "lma%d" % t)
        for b in range(4):
            mm(1 + b, 128, T.ec[:, 128 * b:128 * b + 128], T.ecs[:, 128 * b:128 * b + 128], q, qs, "ec ecs " + Q, True, False)
        scan("#0 zz", "cm", T.cm[:, :], T.ps[:, 0:256], T.zz[:, 0:256], -1e29, op.max, op.add, n=256)
        a, hi16, low = T.aa[:, t:t + 1], T.aa[:, 2 + t:3 + t], T.lw[:, t:t + 1]
        count("cm", "ah%d" % t, T.cm[:, 15:256:16], AF.Sign, T.cm[:, 255:256], -1.0, hi16, n=16)
        count("cm", "a%d" % t, T.cm[:, :], AF.Sign, T.cm[:, 255:256], -1.0, a, n=256)
        ts("dg haz ah%d" % t, "hah", T.ha[:, 0:32:4], T.dg[:, :], hi16, None, op.mult)
        ts("ah%d a%d" % (t, t), "low%d" % t, low, hi16, -16.0, a, op.mult, op.add)
        ts("dg haz low%d" % t, "hal", T.ha[:, 1:32:4], T.dg[:, :], low, None, op.mult)
        quant("haz hah hal", both("hac"), T.hac[:, :], T.hacs[:, :], T.ha[:, :])
        mm(7, 128, *W(5), T.hac[:, :], T.hacs[:, :], "wc4 wcs4 " + both("hac"))
        cp("#7", "oaw", T.oaw[:, :], bank(7, 8))
        pick(mp[:, :], mps[:, :], mc[:, 0:256], mcs[:, 0:256], T.oaw[:, 0:8], MEM, MEMS, "mp%d" % t, "mp%ds" % t, "oaw", 128)
        for b in range(4):
            mm(1 + b, 128, T.ec[:, 128 * b:128 * b + 128], T.ecs[:, 128 * b:128 * b + 128], mp[:, :], mps[:, :],
               "ec ecs mp%d mp%ds" % (t, t), False, True)
        for b in range(4):
            if b % 2 == 0:
                cp("#%d htz" % (1 + b), "ht%d" % b, T.ht[:, b:512:4], bank(1 + b), n=128)
            else:
                act("#%d htz" % (1 + b), "ht%d" % b, T.ht[:, b:512:4], bank(1 + b), AF.Copy)
        quant("ht0 ht1 ht2 ht3 htz htz1", "cand%d cand%ds" % (t, t), mc[:, 256:386], mcs[:, 256:386], T.ht[:, :], 130)
        ts("idn hfz ah%d" % t, "hfh", T.hf[:, 0:512:4], T.idn[:, :], hi16, None, op.mult)
        ts("idn hfz low%d" % t, "hfl", T.hf[:, 1:512:4], T.idn[:, :], low, None, op.mult)
        quant("hfz hfh hfl", both("hfc"), T.hfc[:, :], T.hfcs[:, :], T.hf[:, :])
        mm(7, 128, *W(6), T.hfc[:, :], T.hfcs[:, :], "wc4 wcs4 " + both("hfc"))
        act("#7", "fra", T.fra[:, :], bank(7), AF.Identity, bias=1.0)
        ts("a%d" % t, "nm0", T.nm[:, 0:1], a, 128.0, 128.0 * (hi - 1 - lo), op.is_ge, op.mult)
        ts("nm0 a%d" % t, "nm1", T.nm[:, 1:2], a, T.nm[:, 0:1], 128.0 * lo, op.add, op.add)
        nt, nk = ((T.lm1, "lmn1"), (T.nl, "nlo"))[t]
        ts("nm1 lmz1 nlz", nk, nt[:, 4 * h + 1:4 * h + 4:2], T.zz[:, 0:2], T.nm[:, 1:2], None, op.add)
        if t == 1:
            spread("nn", "nlo nlz", T.nl[:, 4 * h:4 * h + 4], T.nl[:, 4 * h:4 * h + 4])
            arrive("nn", from_mates, "nla")
        LM = OWN + " lma%d" % t
        red(LM, "mx", T.mx[:, :], lm[:, 0:16:2], op.max)
        ts(LM + " mx", "eq", T.eq[:, :], lm[:, 0:16:2], T.mx[:, 0:1], None, op.is_equal)
        scan("eq " + WD, "sc", T.sc[:, :], T.wd[:, :], T.eq[:, :], 0.0, op.mult, op.add)
        ts("dg sc", "oc8", T.oc8[:, :], T.dg[:, :], T.sc[:, 7:8], None, op.mult)
        gather("oc8 hcz hcx " + WINC, "hcg", T.hc[:, 0:512:4], T.winc[:, :], T.oc8[:, 0:8], 128)
        quant("hcg hcz hcx", both("hcc"), T.hcc[:, 0:130], T.hccs[:, 0:130], T.hc[:, :], 130)
        for k, i in ((5, 1), (6, 2), (7, 3), (0, 4)):
            mm(k, 130, *W(i), T.hcc[:, 0:130], T.hccs[:, 0:130], "wc wcs wc4 wcs4 " + both("hcc"))
        scan("#5 zz", "clo", T.clo[:, :], bank(5), T.zz[:, 0:128], 0.0, op.add, op.add, n=128)
        scan("#6 zz", "chi", T.chi[:, :], bank(6), T.zz[:, 0:128], 0.0, op.add, op.add, n=128)
        for c, src, nm in ((0, T.clo, "clo"), (1, T.clo, "clo"), (2, T.chi, "chi")):
            count("%s kb%d" % (nm, c), "acc%d" % c, src[:, :], AF.Sign, T.kb[:, c:c + 1], -1.0, T.acc[:, c:c + 1])
        ts("chi kb3", "le", T.le[:, :], T.chi[:, :], T.kb[:, 3:4], None, op.is_le)
        red("le", "acv", T.acv[:, :], T.le[:, :], op.add, n=128)
        cp("acv", "os3", T.oslot[:, 3:4], T.acv[:, :])
        ts("acc0 acc1 acc2", "os0", T.oslot[:, 0:3], T.acc[:, 0:3], 0.5, 64.0, op.mult, op.add)
        pick(ld[:, 64 * h:64 * h + 64], lds[:, 64 * h:64 * h + 64], mc[:, 256:386], mcs[:, 256:386], T.oslot[:, 0:4],
             "cand%d" % t, "cand%ds" % t, "slot%d" % t, "slot%ds" % t, "os0 os3", 64)
        spread("c%d" % t, "slot%d" % t, ld[:, 64 * h:64 * h + 64].bitcast(dt.uint8), ld[:, 64 * h:64 * h + 64].bitcast(dt.uint8))
        spread("c%d" % t, "slot%ds" % t, lds[:, 64 * h:64 * h + 64], lds[:, 64 * h:64 * h + 64])
        arrive("c%d" % t, 2 * from_mates, "land%d land%ds" % (t, t))
        halves = (0, 1) if t == 0 else (own,)
        tt("#7 fra", "tg", T.tg[:, :], bank(7), T.fra[:, :], op.mult, n=128)
        for e in halves:
            src, nm = ((T.clo, "clo"), (T.chi, "chi"))[e]
            count("%s kb4" % nm, "ta%d" % e, src[:, :], AF.Sign, T.kb[:, 4:5], -1.0, T.ta[:, e:e + 1])
            ts("tg cp%d" % e, "ep%d" % e, T.ep[:, 128 * e:128 * e + 128], T.tg[:, :], T.cc[:, e:e + 1], None, op.is_equal)
            scan("ep%d zz" % e, "co%d" % e, T.co[:, 128 * e:128 * e + 128], T.ep[:, 128 * e:128 * e + 128], T.zz[:, 0:128],
                 0.0, op.max, op.add)
            count("co%d" % e, "un%d" % e, T.co[:, 128 * e:128 * e + 128], AF.Identity, 1.0, -2.0, T.un[:, e:e + 1])
            tt("un%d ta%d" % (e, e), "jg%d" % e, T.jg[:, e:e + 1], T.un[:, e:e + 1], T.ta[:, e:e + 1], op.is_lt)
            ts("un%d cd%d" % (e, e), "jd%d" % e, T.jd[:, e:e + 1], T.un[:, e:e + 1], 0.5, T.cc[:, 4 + e:5 + e], op.mult, op.add)
            ts("jd%d jg%d cl%d" % (e, e, e), "l3%d" % e, T.l3[:, e:e + 1], T.jd[:, e:e + 1], T.jg[:, e:e + 1],
               T.cc[:, 2 + e:3 + e], op.mult, op.add)
        for i, e in enumerate(halves):
            ts("dg l3%d" % e, "o3%d" % i, T.o3[:, 8 * i:8 * i + 8], T.dg[:, :], T.l3[:, e:e + 1], None, op.mult)
        v, an = T.vv[:, t:t + 1], T.an[:, t:t + 1]
        tt("eq " + VD, "pv", T.pv[:, :], T.eq[:, :], T.vd[:, :], op.mult)
        red("pv", "v%d" % t, v, T.pv[:, :], op.max)
        cp("v%d" % t, "bi0", T.bi[:, 0:1], v)
        ts("bi0", "bi1", T.bi[:, 1:2], T.bi[:, 0:1], 255, None, op.bitwise_and)
        cp("bi1", "kk1", T.kk[:, 1:2], T.bi[:, 1:2])
        ts("tri v%d" % t, "triv", T.triv[:, :], T.tri[:, :], v, None, op.mult, n=128)
        tt("#0 triv", "eqt", T.eqt[:, :], bank(0), T.triv[:, :], op.is_equal, n=128)
        red("eqt", "kk0", T.kk[:, 0:1], T.eqt[:, :], op.add, n=128)
        ts("kk0", "an%d" % t, an, T.kk[:, 0:1], float(E), None, op.is_lt)
        ts("kk0 kk1 nold", "kk2", T.kk[:, 2:3], T.kk[:, 0:1], T.kk[:, 1:2], T.kb[:, 6:7], op.add, op.add)
        ts("kk2 an%d old" % t, "kk3", T.kk[:, 3:4], T.kk[:, 2:3], an, T.kb[:, 5:6], op.mult, op.add)
        ts("dg kk3", "o2", T.o2[:, :], T.dg[:, :], T.kk[:, 3:4], None, op.mult)
        gather("o2 wina hlz", "hl0", T.hl[:, 0:128], T.wina[:, :], T.o2[:, 0:8], 128)
        ts(VD + " v%d" % t, "oh%d" % t, T.oh[:, 8 * t:8 * t + 8], T.vd[:, :], v, None, op.is_equal)
        ts("an%d" % t, "ws%d" % t, T.wv[:, t:t + 1], an, 2.0, -1.0, op.mult, op.add)
        ts("an%d" % t, "wb%d" % t, T.wv[:, 2 + t:3 + t], an, -1.0, None, op.add)
        ts("oh%d ws%d" % (t, t), "og%d" % t, T.og[:, 8 * t:8 * t + 8], T.oh[:, 8 * t:8 * t + 8], T.wv[:, t:t + 1], None, op.mult)
        if t == 0:
            gather("o30 wina hlz", "hl1", T.hl[:, 128:256], T.wina[:, :], T.o3[:, 0:8], 128)
            do("S", "o31 wina hlz", "hl2",
               lambda: S.activation(T.hl[:, 256:384], T.wina[:, :].indirect(T.o3[:, 8:16]), AF.Copy), 0.23)
            wrapped(1, 0, 96, T.ol[:, 0:24], "ol", "hl", T.hlc, T.hlcs, T.hl, "hl0 hl1 hl2")
            pick(T.mc1[:, 0:256], T.mc1s[:, 0:256], mc[:, 0:386], mcs[:, 0:386], T.ol[:, 8:24],
                 MEM + " cand0", MEMS + " cand0s", "mcown1 mcfar1", "mcown1s mcfar1s", "ol", 256)
            pick(T.ld1[:, QO:QO + 128], T.ld1s[:, QO:QO + 128], ld[:, 0:384], lds[:, 0:384], T.ol[:, 0:8],
                 "slot0 land0 qown0 qfar0", "slot0s land0s qown0s qfar0s", "qown1 qfar1", "qown1s qfar1s", "ol", 128)
        else:
            wrapped(1, 0, 32, T.ol[:, 0:8], "ol", "hl", T.hlc, T.hlcs, T.hl, "hl0 hl1 hl2")
            gather("o30 wina hmz", "hm0", T.hm[:, 0:128], T.wina[:, :], T.o3[:, 0:8], 128)
            wrapped(2, 96, 32, T.om[:, 0:8], "om", "hm", T.hmc, T.hmcs, T.hm, "hm0")
            pick(T.fm[:, :], T.fms[:, :], mc[:, 0:386], mcs[:, 0:386], T.om[:, 0:8],
                 MEM + " cand1", MEMS + " cand1s", "fm", "fms", "om", 128)
            dma("Y", "u0", "fm", "out0", T.oc[:, :], T.fm[:, :].bitcast(dt.uint8))
            for k in range(4):
                dma("Y", "u%d" % (1 + k), "fms", "out%d" % (1 + k), T.osc[4 * k:4 * k + 4, :], T.fms[32 * k:32 * k + 4, :])

    one_round(0)
    one_round(1)
    pick(T.qf[:, :], T.qfs[:, :], T.ld1[:, 0:384], T.ld1s[:, 0:384], T.ol[:, 0:8],
         "slot1 land1 qown1 qfar1", "slot1s land1s qown1s qfar1s", "qf", "qfs", "ol", 128)
    mm(3, 128, T.wq[:, :], T.wqs[:, :], T.qf[:, :], T.qfs[:, :], "wq wqs qf qfs")
    act("#3", "ysb", T.ysb[:, :], bank(3), AF.Copy)
    dma("S", "u7", "ysb", "outy", T.y[:, :], T.ysb[:, :])
    for t, nt, nk in ((0, T.lm1, "lmn1 lmz1 lma1"), (1, T.nl, "nlo nlz nla")):
        tt("og%d %s" % (t, nk), "oh%d" % t, T.oh[:, 8 * t:8 * t + 8], T.og[:, 8 * t:8 * t + 8], nt[:, 1:16:2], op.mult)
        red("oh%d" % t, "wg%d" % t, T.wv[:, 4 + t:5 + t], T.oh[:, 8 * t:8 * t + 8], op.add)
        tt("wg%d wb%d" % (t, t), "wo%d" % t, T.wo[:, t:t + 1], T.wv[:, 4 + t:5 + t], T.wv[:, 2 + t:3 + t], op.add)
        dma("Y", "u%d" % (5 + t), "wo%d" % t, "out%d" % (5 + t), T.wi[t:t + 1, :], T.wo[:, t:t + 1])

    cnt, known = {}, {q: {} for q in queue}
    wr, rd = {}, {}
    for o in in_order(ops):
        q = o["q"]
        if o["call"] is None:
            cnt[o["sem"]] = o["inc"]
            note((o["sem"], o["inc"], "far", {}), [], o["w"], wr, rd)
            continue
        deps = conflicts(q, o["r"], o["w"], wr, rd, o["acc"], False)
        want = {}
        for e in deps:
            if known[q].get(e[0], 0) < e[1]:
                want[e[0]] = max(want.get(e[0], 0), e[1])
        for e in deps:
            for s, v in e[3].items():
                if s in want and e[0] != s and want[s] <= v:
                    del want[s]
        for s, v in want.items():
            queue[q].wait_ge(T.sem[s], v)
            known[q][s] = v
        for e in deps:
            for s, v in e[3].items():
                if known[q].get(s, 0) < v:
                    known[q][s] = v
        made = o["call"]()
        if o["sem"]:
            made.then_inc(T.sem[o["sem"]], o["inc"])
            cnt[o["sem"]] = cnt.get(o["sem"], 0) + o["inc"]
            note((o["sem"], cnt[o["sem"]], q if o["sem"] == q else "dma", dict(known[q])), o["r"], o["w"], wr, rd)
    for s, n in cnt.items():
        if known["G"].get(s, 0) < n:
            g.wait_ge(T.sem[s], n)
    g.wait_ge(T.sem.ls, ls[0])
